import numpy as np
import ml_dtypes


def mxq(x, axis, fmt="e4m3"):
    dtype, down = {"e4m3": (ml_dtypes.float8_e4m3fn, 7), "e5m2": (ml_dtypes.float8_e5m2, 14)}[fmt]
    v = np.moveaxis(np.asarray(x, np.float32).astype(ml_dtypes.bfloat16).astype(np.float64), axis, -1)
    blocks = v.reshape(v.shape[:-1] + (-1, 32))
    amax = np.abs(blocks).max(-1, keepdims=True)
    byte = np.maximum(np.where(amax > 0, np.frexp(amax)[1] - 1 + 127, 0) - down, 1)
    scale = np.exp2(byte - 127.0)
    codes = (blocks / scale).astype(np.float32).astype(dtype).astype(np.float64)
    return np.moveaxis((codes * scale).reshape(v.shape), -1, axis)


WIDE = False


def mx_kscale(k):
    if not WIDE:
        return np.ones(k)
    levels = np.array([10, -10, 5, -5, 0])
    if k % 512:
        return np.exp2(np.random.permutation(np.resize(levels, k // 32))).repeat(32)
    a = np.empty((k // 512, 16))
    for p in range(k // 512):
        a[p, :8] = np.random.permutation(np.resize(levels, 8))
        for g in range(8):
            far = levels[np.abs(levels - a[p, g]) >= 10]
            a[p, g + 8] = far[np.random.randint(len(far))]
    return np.exp2(a.ravel()).repeat(32)


def f64(x):
    return np.asarray(x).astype(np.float64)


def striped(idx):
    return np.tile(idx.reshape(-1, 16).T, (8, 1)).astype(np.uint16)


def unstriped(offs):
    return offs[:16].T.reshape(-1).astype(np.int64)


def pack_weight(w):
    k, n = w.shape
    w = f64(np.asarray(w, np.float32).astype(ml_dtypes.bfloat16)).reshape(k // 32, 32, n)
    amax = np.abs(w).max(1)
    byte = np.clip(np.where(amax > 0, np.frexp(amax)[1] - 1 + 127 - 7, 1), 1, 254)
    scaled = (w * np.exp2(127.0 - byte)[:, None, :]).reshape(k, n).astype(np.float32)
    words = np.ascontiguousarray(scaled.reshape(k // 512, 128, 4, n).transpose(0, 1, 3, 2)).astype(ml_dtypes.float8_e4m3fn).view(np.uint8)
    return words, np.ascontiguousarray(byte.astype(np.uint8).reshape(k // 512, 16, n))


def unpack_weight(words, scales):
    g, p, n, _ = words.shape
    vals = np.ascontiguousarray(words).view(ml_dtypes.float8_e4m3fn).astype(np.float64) * np.repeat(np.exp2(scales.astype(np.float64) - 127.0), 8, axis=1)[..., None]
    return vals.transpose(0, 1, 3, 2).reshape(g * 512, n)


def relu(v):
    return np.maximum(v, 0.0)


K, T, E, C, N = 1536, 768, 2, 256, 384


def by_expert(wq, xq):
    return np.concatenate([wq[e].T @ xq[:, e * C:(e + 1) * C] for e in range(E)], axis=1)


def setup_inputs():
    n = np.random.standard_normal
    s = mx_kscale(K)[:, None]
    packed = [pack_weight(m) for m in n((E, K, N)) / np.sqrt(K) / s[None]]
    return {
        "xT": (n((K, T)) * s).astype(np.float32),
        "w_words": np.stack([m[0] for m in packed]),
        "w_scales": np.stack([m[1] for m in packed]),
        "b": (0.3 * n((N, E))).astype(np.float32),
        "gate": np.tile(np.random.uniform(0.2, 1.0, E * C), (K, 1)).astype(np.float32),
        "offs": striped(np.random.permutation(T)[:E * C]),
    }


def reference(xT, w_words, w_scales, b, gate, offs):
    idx = unstriped(offs)
    w = np.stack([unpack_weight(w_words[e], w_scales[e]) for e in range(E)])
    xq = mxq(f64(gate) * f64(xT)[:, idx], 0, "e4m3")
    y = by_expert(w, xq)
    y = relu(y + np.repeat(f64(b), C, axis=1))
    out = np.zeros((N, T))
    out[:, idx] = y
    return out

@@ -1,0 +1,132 @@
+from contextlib import ExitStack
+
+import concourse.mybir as mybir
+
+K, T, E, C, N = 1536, 768, 2, 256, 384
+S = E * C
+P = 128
+PACK = 4
+K_PASS = P * PACK
+PASSES = K // K_PASS
+N_TILES = N // P
+PER_COL = 16
+
+F32 = mybir.dt.float32
+BF16 = mybir.dt.bfloat16
+I32 = mybir.dt.int32
+U32 = mybir.dt.uint32
+U16 = mybir.dt.uint16
+U8 = mybir.dt.uint8
+FP8X4 = mybir.dt.float8_e4m3fn_x4
+MULT = mybir.AluOpType.mult
+RELU = mybir.ActivationFunctionType.Relu
+
+FLOPS = 2 * K * N * S
+BYTES = 4 * K * T + E * K * N + E * (K // 32) * N + 4 * N * E + 4 * S + 2 * S + 4 * N * T
+
+
+def tile_moe_pre_lin_relu_kernel(tc, xT, w_words, w_scales, b, gate, offs, out):
+    nc = tc.nc
+    with ExitStack() as ctx:
+        sb = ctx.enter_context(tc.tile_pool(name="sb", bufs=1))
+        psum = ctx.enter_context(tc.psum_pool(name="psum", bufs=1))
+
+        offsets = sb.tile([P, S // PER_COL], U16, name="offsets")
+        gate_sb = sb.tile([P, S], F32, name="gate_sb")
+        x_rows = [[sb.tile([P, T], F32, name="x_rows%d_%d" % (a, t)) for t in range(PACK)] for a in range(PASSES)]
+        w_codes = [sb.tile([P, PASSES, N], U32, name="w_codes%d" % e, align_bytes=64) for e in range(E)]
+        w_plane = sb.tile([P, E * PASSES, N], U8, name="w_plane", align_bytes=64)
+        bias = sb.tile([P, N_TILES, E], F32, name="bias")
+        result = [sb.tile([P, T], F32, name="result%d" % n) for n in range(N_TILES)]
+        acc = [[psum.tile([P, C], F32, name="acc%d_%d" % (e, n)) for n in range(N_TILES)] for e in range(E)]
+
+        nc.vector.memset(w_plane[:].rearrange("p g n -> p (g n)").bitcast(I32), 0)
+        nc.vector.memset(result[0][:], 0.0)
+        nc.gpsimd.memset(result[1][:], 0.0)
+        nc.gpsimd.memset(result[2][:], 0.0)
+
+        x_view = xT.rearrange("(a p t) j -> a t p j", p=P, t=PACK)
+        nc.sync.dma_start(out=x_rows[0][0][:], in_=x_view[0, 0])
+        nc.sync.dma_start(out=gate_sb[:], in_=gate[0:P, :])
+        nc.sync.dma_start(offsets[:], offs)
+        for a in range(PASSES):
+            for t in range(PACK):
+                if (a, t) != (0, 0):
+                    nc.sync.dma_start(out=x_rows[a][t][:], in_=x_view[a, t])
+        scale_view = w_scales.rearrange("e a (q r) n -> q r (e a) n", r=4)
+        for q in range(4):
+            nc.sync.dma_start(out=w_plane[32 * q : 32 * q + 4, :, :].bitcast(I32), in_=scale_view[q].bitcast(I32))
+        nc.sync.dma_start(out=bias[:], in_=b.rearrange("(n p) e -> p n e", p=P))
+        for e in range(E):
+            nc.sync.dma_start(out=w_codes[e][:].bitcast(I32), in_=w_words[e].rearrange("a p n t -> p a (n t)").bitcast(I32))
+
+        quantised = {}
+
+        def gather(a, lo, hi):
+            gated = sb.tile([P, PACK, hi - lo], F32, name="gated%d_%d" % (a, lo))
+            for t in range(PACK):
+                nc.vector.tensor_tensor(
+                    gated[:, t, :],
+                    x_rows[a][t][:].indirect(offsets[:, lo // PER_COL : hi // PER_COL]),
+                    gate_sb[:, lo:hi],
+                    MULT,
+                )
+            return gated
+
+        def interleave(gated, a, lo, hi):
+            grouped = sb.tile([P, hi - lo, PACK], BF16, name="grouped%d_%d" % (a, lo), align_bytes=64)
+            nc.scalar.copy(
+                grouped[:].rearrange("p (c i) t -> p c t i", i=4),
+                gated[:].rearrange("p t (c i) -> p c t i", i=4),
+            )
+            return grouped
+
+        def quantise(grouped, a, lo, hi):
+            codes = sb.tile([P, hi - lo], U32, name="codes%d_%d" % (a, lo), align_bytes=64)
+            plane = sb.tile([P, hi - lo], U8, name="plane%d_%d" % (a, lo), align_bytes=64)
+            nc.vector.quantize_mx(out=codes[:].bitcast(FP8X4), scales=plane[:], in_=grouped[:].rearrange("p j t -> p (j t)"))
+            for e in range(lo // C, hi // C):
+                cols = slice(e * C - lo, (e + 1) * C - lo)
+                quantised[(a, e)] = (codes[:, cols], plane[:, cols])
+
+        def multiply(a, e):
+            codes, plane = quantised[(a, e)]
+            for n in range(N_TILES):
+                cols = slice(n * P, (n + 1) * P)
+                nc.tensor.matmul_mx(
+                    out=acc[e][n][:],
+                    lhsT=w_codes[e][:, a, cols].bitcast(FP8X4),
+                    lhsT_scale=w_plane[:, e * PASSES + a, cols],
+                    rhs=codes.bitcast(FP8X4),
+                    rhs_scale=plane,
+                    start=(a == 0),
+                    stop=(a == PASSES - 1),
+                )
+
+        def activate(e):
+            ys = []
+            for n in range(N_TILES):
+                y = sb.tile([P, C], F32, name="y%d_%d" % (e, n))
+                nc.scalar.activation(y[:], acc[e][n][:], RELU, bias=bias[:, n, e : e + 1])
+                ys.append(y)
+            return ys
+
+        def scatter(y, e, n):
+            nc.vector.tensor_copy(result[n][:].indirect(offsets[:, e * C // PER_COL : (e + 1) * C // PER_COL]), y[:])
+
+        last = PASSES - 1
+        for a in range(last):
+            quantise(interleave(gather(a, 0, S), a, 0, S), a, 0, S)
+        quantise(interleave(gather(last, 0, C), last, 0, C), last, 0, C)
+        for a in range(PASSES):
+            multiply(a, 0)
+        y0 = activate(0)
+        quantise(interleave(gather(last, C, S), last, C, S), last, C, S)
+        for a in range(PASSES):
+            multiply(a, 1)
+        y1 = activate(1)
+        for n in range(N_TILES):
+            scatter(y0[n], 0, n)
+        for n in range(N_TILES):
+            scatter(y1[n], 1, n)
+            nc.sync.dma_start(out=out[n * P : (n + 1) * P, :], in_=result[n][:])

@@ -41,14 +41,14 @@ def tile_moe_pre_lin_relu_kernel(tc, xT, w_words, w_scales, b, gate, offs, out):
         acc = [[psum.tile([P, C], F32, name="acc%d_%d" % (e, n)) for n in range(N_TILES)] for e in range(E)]
 
         nc.vector.memset(w_plane[:].rearrange("p g n -> p (g n)").bitcast(I32), 0)
-        nc.vector.memset(result[0][:], 0.0)
-        nc.gpsimd.memset(result[1][:], 0.0)
-        nc.gpsimd.memset(result[2][:], 0.0)
+        for n in range(N_TILES):
+            nc.vector.memset(result[n][:], 0.0)
 
         x_view = xT.rearrange("(a p t) j -> a t p j", p=P, t=PACK)
         nc.sync.dma_start(out=x_rows[0][0][:], in_=x_view[0, 0])
-        nc.sync.dma_start(out=gate_sb[:], in_=gate[0:P, :])
+        nc.sync.dma_start(out=gate_sb[:, 0:C], in_=gate[0:P, 0:C])
         nc.sync.dma_start(offsets[:], offs)
+        nc.sync.dma_start(out=gate_sb[:, C:S], in_=gate[0:P, C:S])
         for a in range(PASSES):
             for t in range(PACK):
                 if (a, t) != (0, 0):
@@ -60,36 +60,33 @@ def tile_moe_pre_lin_relu_kernel(tc, xT, w_words, w_scales, b, gate, offs, out):
         for e in range(E):
             nc.sync.dma_start(out=w_codes[e][:].bitcast(I32), in_=w_words[e].rearrange("a p n t -> p a (n t)").bitcast(I32))
 
+        gated = [sb.tile([P, PACK, S], F32, name="gated%d" % a) for a in range(PASSES)]
+        grouped = {}
         quantised = {}
 
-        def gather(a, lo, hi):
-            gated = sb.tile([P, PACK, hi - lo], F32, name="gated%d_%d" % (a, lo))
-            for t in range(PACK):
-                nc.vector.tensor_tensor(
-                    gated[:, t, :],
-                    x_rows[a][t][:].indirect(offsets[:, lo // PER_COL : hi // PER_COL]),
-                    gate_sb[:, lo:hi],
-                    MULT,
-                )
-            return gated
-
-        def interleave(gated, a, lo, hi):
-            grouped = sb.tile([P, hi - lo, PACK], BF16, name="grouped%d_%d" % (a, lo), align_bytes=64)
-            nc.scalar.copy(
-                grouped[:].rearrange("p (c i) t -> p c t i", i=4),
-                gated[:].rearrange("p t (c i) -> p c t i", i=4),
+        def gather(a, t, lo, hi):
+            nc.vector.tensor_tensor(
+                gated[a][:, t, lo:hi],
+                x_rows[a][t][:].indirect(offsets[:, lo // PER_COL : hi // PER_COL]),
+                gate_sb[:, lo:hi],
+                MULT,
             )
-            return grouped
 
-        def quantise(grouped, a, lo, hi):
-            codes = sb.tile([P, hi - lo], U32, name="codes%d_%d" % (a, lo), align_bytes=64)
-            plane = sb.tile([P, hi - lo], U8, name="plane%d_%d" % (a, lo), align_bytes=64)
-            nc.vector.quantize_mx(out=codes[:].bitcast(FP8X4), scales=plane[:], in_=grouped[:].rearrange("p j t -> p (j t)"))
-            for e in range(lo // C, hi // C):
-                cols = slice(e * C - lo, (e + 1) * C - lo)
-                quantised[(a, e)] = (codes[:, cols], plane[:, cols])
+        def interleave(a, e):
+            tile = sb.tile([P, C, PACK], BF16, name="grouped%d_%d" % (a, e), align_bytes=64)
+            nc.scalar.copy(
+                tile[:].rearrange("p (c i) t -> p c t i", i=4),
+                gated[a][:, :, e * C : (e + 1) * C].rearrange("p t (c i) -> p c t i", i=4),
+            )
+            grouped[(a, e)] = tile
 
-        def multiply(a, e):
+        def quantise(a, e):
+            codes = sb.tile([P, C], U32, name="codes%d_%d" % (a, e), align_bytes=64)
+            plane = sb.tile([P, C], U8, name="plane%d_%d" % (a, e), align_bytes=64)
+            nc.vector.quantize_mx(out=codes[:].bitcast(FP8X4), scales=plane[:], in_=grouped[(a, e)][:].rearrange("p j t -> p (j t)"))
+            quantised[(a, e)] = (codes[:], plane[:])
+
+        def multiply(a, e, start, stop):
             codes, plane = quantised[(a, e)]
             for n in range(N_TILES):
                 cols = slice(n * P, (n + 1) * P)
@@ -99,34 +96,58 @@ def tile_moe_pre_lin_relu_kernel(tc, xT, w_words, w_scales, b, gate, offs, out):
                     lhsT_scale=w_plane[:, e * PASSES + a, cols],
                     rhs=codes.bitcast(FP8X4),
                     rhs_scale=plane,
-                    start=(a == 0),
-                    stop=(a == PASSES - 1),
+                    start=start,
+                    stop=stop,
                 )
 
-        def activate(e):
-            ys = []
-            for n in range(N_TILES):
-                y = sb.tile([P, C], F32, name="y%d_%d" % (e, n))
-                nc.scalar.activation(y[:], acc[e][n][:], RELU, bias=bias[:, n, e : e + 1])
-                ys.append(y)
-            return ys
+        ys = {}
 
-        def scatter(y, e, n):
-            nc.vector.tensor_copy(result[n][:].indirect(offsets[:, e * C // PER_COL : (e + 1) * C // PER_COL]), y[:])
+        def activate(e, n):
+            y = sb.tile([P, C], F32, name="y%d_%d" % (e, n))
+            nc.scalar.activation(y[:], acc[e][n][:], RELU, bias=bias[:, n, e : e + 1])
+            ys[(e, n)] = y
 
-        last = PASSES - 1
-        for a in range(last):
-            quantise(interleave(gather(a, 0, S), a, 0, S), a, 0, S)
-        quantise(interleave(gather(last, 0, C), last, 0, C), last, 0, C)
-        for a in range(PASSES):
-            multiply(a, 0)
-        y0 = activate(0)
-        quantise(interleave(gather(last, C, S), last, C, S), last, C, S)
-        for a in range(PASSES):
-            multiply(a, 1)
-        y1 = activate(1)
+        def scatter(e, n):
+            nc.vector.tensor_copy(result[n][:].indirect(offsets[:, e * C // PER_COL : (e + 1) * C // PER_COL]), ys[(e, n)][:])
+
+        gather(0, 0, 0, C)
+        gather(0, 0, C, S)
+        for t in range(1, PACK):
+            gather(0, t, 0, S)
+        interleave(0, 0)
+        interleave(0, 1)
+        for t in range(PACK):
+            gather(1, t, 0, S)
+        interleave(1, 0)
+        interleave(1, 1)
+        quantise(0, 0)
+        multiply(0, 0, True, False)
+        for t in range(PACK):
+            gather(2, t, 0, C)
+        interleave(2, 0)
+        quantise(1, 0)
+        multiply(1, 0, False, False)
+        gather(2, 0, C, S)
+        gather(2, 1, C, S)
+        quantise(0, 1)
+        quantise(2, 0)
+        multiply(2, 0, False, True)
+        activate(0, 0)
+        gather(2, 2, C, S)
+        gather(2, 3, C, S)
+        interleave(2, 1)
+        activate(0, 1)
+        activate(0, 2)
+        quantise(1, 1)
+        multiply(1, 1, True, False)
+        multiply(0, 1, False, False)
+        scatter(0, 0)
+        quantise(2, 1)
+        multiply(2, 1, False, True)
         for n in range(N_TILES):
-            scatter(y0[n], 0, n)
+            activate(1, n)
+        scatter(0, 1)
+        scatter(0, 2)
         for n in range(N_TILES):
-            scatter(y1[n], 1, n)
+            scatter(1, n)
             nc.sync.dma_start(out=out[n * P : (n + 1) * P, :], in_=result[n][:])

@@ -46,9 +46,8 @@ def tile_moe_pre_lin_relu_kernel(tc, xT, w_words, w_scales, b, gate, offs, out):
 
         x_view = xT.rearrange("(a p t) j -> a t p j", p=P, t=PACK)
         nc.sync.dma_start(out=x_rows[0][0][:], in_=x_view[0, 0])
-        nc.sync.dma_start(out=gate_sb[:, 0:C], in_=gate[0:P, 0:C])
+        nc.sync.dma_start(out=gate_sb[:], in_=gate[0:P, :])
         nc.sync.dma_start(offsets[:], offs)
-        nc.sync.dma_start(out=gate_sb[:, C:S], in_=gate[0:P, C:S])
         for a in range(PASSES):
             for t in range(PACK):
                 if (a, t) != (0, 0):
@@ -56,9 +55,10 @@ def tile_moe_pre_lin_relu_kernel(tc, xT, w_words, w_scales, b, gate, offs, out):
         scale_view = w_scales.rearrange("e a (q r) n -> q r (e a) n", r=4)
         for q in range(4):
             nc.sync.dma_start(out=w_plane[32 * q : 32 * q + 4, :, :].bitcast(I32), in_=scale_view[q].bitcast(I32))
+        w_view = w_words.rearrange("e a p n t -> e p a (n t)")
+        nc.sync.dma_start(out=w_codes[0][:].bitcast(I32), in_=w_view[0].bitcast(I32))
         nc.sync.dma_start(out=bias[:], in_=b.rearrange("(n p) e -> p n e", p=P))
-        for e in range(E):
-            nc.sync.dma_start(out=w_codes[e][:].bitcast(I32), in_=w_words[e].rearrange("a p n t -> p a (n t)").bitcast(I32))
+        nc.sync.dma_start(out=w_codes[1][:].bitcast(I32), in_=w_view[1].bitcast(I32))
 
         gated = [sb.tile([P, PACK, S], F32, name="gated%d" % a) for a in range(PASSES)]
         grouped = {}
@@ -74,10 +74,7 @@ def tile_moe_pre_lin_relu_kernel(tc, xT, w_words, w_scales, b, gate, offs, out):
 
         def interleave(a, e):
             tile = sb.tile([P, C, PACK], BF16, name="grouped%d_%d" % (a, e), align_bytes=64)
-            nc.scalar.copy(
-                tile[:].rearrange("p (c i) t -> p c t i", i=4),
-                gated[a][:, :, e * C : (e + 1) * C].rearrange("p t (c i) -> p c t i", i=4),
-            )
+            nc.scalar.copy(tile[:], gated[a][:, :, e * C : (e + 1) * C].rearrange("p t j -> p j t"))
             grouped[(a, e)] = tile
 
         def quantise(a, e):
@@ -110,9 +107,7 @@ def tile_moe_pre_lin_relu_kernel(tc, xT, w_words, w_scales, b, gate, offs, out):
         def scatter(e, n):
             nc.vector.tensor_copy(result[n][:].indirect(offsets[:, e * C // PER_COL : (e + 1) * C // PER_COL]), ys[(e, n)][:])
 
-        gather(0, 0, 0, C)
-        gather(0, 0, C, S)
-        for t in range(1, PACK):
+        for t in range(PACK):
             gather(0, t, 0, S)
         interleave(0, 0)
         interleave(0, 1)

@@ -33,10 +33,13 @@ def tile_moe_pre_lin_relu_kernel(tc, xT, w_words, w_scales, b, gate, offs, out):
 
         offsets = sb.tile([P, S // PER_COL], U16, name="offsets")
         gate_sb = sb.tile([P, S], F32, name="gate_sb")
-        x_rows = [[sb.tile([P, T], F32, name="x_rows%d_%d" % (a, t)) for t in range(PACK)] for a in range(PASSES)]
+        x_rows = [[sb.tile([P, T], F32, name="x_rows%d_%d" % (a, t), align_bytes=64) for t in range(PACK)] for a in range(PASSES)]
         w_codes = [sb.tile([P, PASSES, N], U32, name="w_codes%d" % e, align_bytes=64) for e in range(E)]
         w_plane = sb.tile([P, E * PASSES, N], U8, name="w_plane", align_bytes=64)
         bias = sb.tile([P, N_TILES, E], F32, name="bias")
+        gate_mid = sb.tile([P, C], F32, name="gate_mid")
+        gate_late = sb.tile([P, C], F32, name="gate_late")
+        bias_first = sb.tile([P, 1], F32, name="bias_first", tag="share_a", align_bytes=64)
         result = [sb.tile([P, T], F32, name="result%d" % n) for n in range(N_TILES)]
         acc = [[psum.tile([P, C], F32, name="acc%d_%d" % (e, n)) for n in range(N_TILES)] for e in range(E)]
 
@@ -46,101 +49,129 @@ def tile_moe_pre_lin_relu_kernel(tc, xT, w_words, w_scales, b, gate, offs, out):
 
         x_view = xT.rearrange("(a p t) j -> a t p j", p=P, t=PACK)
         nc.sync.dma_start(out=x_rows[0][0][:], in_=x_view[0, 0])
-        nc.sync.dma_start(out=gate_sb[:], in_=gate[0:P, :])
+        nc.sync.dma_start(out=gate_sb[:, 0:C], in_=gate[0:P, 0:C])
         nc.sync.dma_start(offsets[:], offs)
+        nc.sync.dma_start(out=gate_sb[:, C:S], in_=gate[0:P, C:S])
         for a in range(PASSES):
             for t in range(PACK):
                 if (a, t) != (0, 0):
                     nc.sync.dma_start(out=x_rows[a][t][:], in_=x_view[a, t])
+        nc.sync.dma_start(out=gate_mid[:], in_=gate[P : 2 * P, C:S])
         scale_view = w_scales.rearrange("e a (q r) n -> q r (e a) n", r=4)
         for q in range(4):
             nc.sync.dma_start(out=w_plane[32 * q : 32 * q + 4, :, :].bitcast(I32), in_=scale_view[q].bitcast(I32))
         w_view = w_words.rearrange("e a p n t -> e p a (n t)")
         nc.sync.dma_start(out=w_codes[0][:].bitcast(I32), in_=w_view[0].bitcast(I32))
+        nc.sync.dma_start(out=gate_late[:], in_=gate[2 * P : 3 * P, C:S])
+        nc.sync.dma_start(out=bias_first[:], in_=b[0:P, 0:1])
         nc.sync.dma_start(out=bias[:], in_=b.rearrange("(n p) e -> p n e", p=P))
         nc.sync.dma_start(out=w_codes[1][:].bitcast(I32), in_=w_view[1].bitcast(I32))
 
-        gated = [sb.tile([P, PACK, S], F32, name="gated%d" % a) for a in range(PASSES)]
-        grouped = {}
+        gated = {}
+        for a in range(PASSES - 1):
+            both = sb.tile([P, PACK, S], F32, name="gated%d" % a)
+            gated[(a, 0)] = both[:, :, 0:C]
+            gated[(a, 1)] = both[:, :, C:S]
+            gated[(a, None)] = both[:]
+        last_a = sb.tile([P, PACK, C], F32, name="gated_last0")
+        last_b = sb.tile([P, PACK, C], F32, name="gated_last1", tag="share_b")
+        gated[(PASSES - 1, 0)] = last_a[:]
+        gated[(PASSES - 1, 1)] = last_b[:]
         quantised = {}
 
-        def gather(a, t, lo, hi):
+        def gather(a, t, e, weights=None):
+            lo, hi = (0, S) if e is None else (e * C, (e + 1) * C)
             nc.vector.tensor_tensor(
-                gated[a][:, t, lo:hi],
+                gated[(a, e)][:, t, :],
                 x_rows[a][t][:].indirect(offsets[:, lo // PER_COL : hi // PER_COL]),
-                gate_sb[:, lo:hi],
+                gate_sb[:, lo:hi] if weights is None else weights[:],
                 MULT,
             )
 
+        calls = {
+            "first0": ([(0, 0)], "grouped_first0", "x_rows1_3"),
+            "first12": ([(1, 0), (2, 0)], "grouped_first12", "codes_first12"),
+            "second01": ([(0, 1), (1, 1)], "grouped_second01", "x_rows2_2"),
+            "second2": ([(2, 1)], "share_a", "codes_second2"),
+        }
+        call_input = {}
+
         def interleave(a, e):
-            tile = sb.tile([P, C, PACK], BF16, name="grouped%d_%d" % (a, e), align_bytes=64)
-            nc.scalar.copy(tile[:], gated[a][:, :, e * C : (e + 1) * C].rearrange("p t j -> p j t"))
-            grouped[(a, e)] = tile
+            for name, (members, tag, codes_tag) in calls.items():
+                if (a, e) in members:
+                    if name not in call_input:
+                        call_input[name] = sb.tile([P, len(members), C, PACK], BF16, name="grouped_" + name, tag=tag, align_bytes=64)
+                    nc.scalar.copy(call_input[name][:, members.index((a, e))], gated[(a, e)].rearrange("p t j -> p j t"))
 
-        def quantise(a, e):
-            codes = sb.tile([P, C], U32, name="codes%d_%d" % (a, e), align_bytes=64)
-            plane = sb.tile([P, C], U8, name="plane%d_%d" % (a, e), align_bytes=64)
-            nc.vector.quantize_mx(out=codes[:].bitcast(FP8X4), scales=plane[:], in_=grouped[(a, e)][:].rearrange("p j t -> p (j t)"))
-            quantised[(a, e)] = (codes[:], plane[:])
+        def quantise(name):
+            members, tag, codes_tag = calls[name]
+            codes = sb.tile([P, len(members) * C], U32, name="codes_" + name, tag=codes_tag, align_bytes=64)
+            plane = sb.tile([P, len(members) * C], U8, name="plane_" + name, align_bytes=64)
+            nc.vector.quantize_mx(out=codes[:].bitcast(FP8X4), scales=plane[:], in_=call_input[name][:].rearrange("p m j t -> p (m j t)"))
+            for i, member in enumerate(members):
+                quantised[member] = (codes[:, i * C : (i + 1) * C], plane[:, i * C : (i + 1) * C])
 
-        def multiply(a, e, start, stop):
-            codes, plane = quantised[(a, e)]
+        def multiply(passes, e):
             for n in range(N_TILES):
                 cols = slice(n * P, (n + 1) * P)
-                nc.tensor.matmul_mx(
-                    out=acc[e][n][:],
-                    lhsT=w_codes[e][:, a, cols].bitcast(FP8X4),
-                    lhsT_scale=w_plane[:, e * PASSES + a, cols],
-                    rhs=codes.bitcast(FP8X4),
-                    rhs_scale=plane,
-                    start=start,
-                    stop=stop,
-                )
+                for a in passes:
+                    codes, plane = quantised[(a, e)]
+                    nc.tensor.matmul_mx(
+                        out=acc[e][n][:],
+                        lhsT=w_codes[e][:, a, cols].bitcast(FP8X4),
+                        lhsT_scale=w_plane[:, e * PASSES + a, cols],
+                        rhs=codes.bitcast(FP8X4),
+                        rhs_scale=plane,
+                        start=(a == 0),
+                        stop=(a == PASSES - 1),
+                    )
 
         ys = {}
 
-        def activate(e, n):
-            y = sb.tile([P, C], F32, name="y%d_%d" % (e, n))
-            nc.scalar.activation(y[:], acc[e][n][:], RELU, bias=bias[:, n, e : e + 1])
+        def activate(e, n, y, column):
+            nc.scalar.activation(y, acc[e][n][:], RELU, bias=column)
             ys[(e, n)] = y
 
         def scatter(e, n):
-            nc.vector.tensor_copy(result[n][:].indirect(offsets[:, e * C // PER_COL : (e + 1) * C // PER_COL]), ys[(e, n)][:])
+            nc.vector.tensor_copy(result[n][:].indirect(offsets[:, e * C // PER_COL : (e + 1) * C // PER_COL]), ys[(e, n)])
 
-        for t in range(PACK):
-            gather(0, t, 0, S)
+        gather(0, 0, 0)
+        gather(0, 0, 1)
+        for t in range(1, PACK):
+            gather(0, t, None)
         interleave(0, 0)
         interleave(0, 1)
-        for t in range(PACK):
-            gather(1, t, 0, S)
+        for t in range(PACK - 1):
+            gather(1, t, None)
+        gather(1, PACK - 1, 0)
         interleave(1, 0)
-        interleave(1, 1)
-        quantise(0, 0)
-        multiply(0, 0, True, False)
         for t in range(PACK):
-            gather(2, t, 0, C)
+            gather(2, t, 0)
         interleave(2, 0)
-        quantise(1, 0)
-        multiply(1, 0, False, False)
-        gather(2, 0, C, S)
-        gather(2, 1, C, S)
-        quantise(0, 1)
-        quantise(2, 0)
-        multiply(2, 0, False, True)
-        activate(0, 0)
-        gather(2, 2, C, S)
-        gather(2, 3, C, S)
+        gather(1, PACK - 1, 1, gate_mid)
+        interleave(1, 1)
+        gather(2, 0, 1, gate_mid)
+        quantise("first0")
+        multiply([0], 0)
+        gather(2, 1, 1, gate_mid)
+        quantise("first12")
+        multiply([1, 2], 0)
+        y_first = sb.tile([P, C], F32, name="y_first")
+        activate(0, 0, y_first[:], bias_first[:])
+        gather(2, 2, 1, gate_late)
+        gather(2, 3, 1, gate_late)
+        quantise("second01")
+        multiply([0, 1], 1)
         interleave(2, 1)
-        activate(0, 1)
-        activate(0, 2)
-        quantise(1, 1)
-        multiply(1, 1, True, False)
-        multiply(0, 1, False, False)
+        y_rest = sb.tile([P, N_TILES - 1, C], F32, name="y_rest", tag="share_b")
+        for n in range(1, N_TILES):
+            activate(0, n, y_rest[:, n - 1, :], bias[:, n, 0:1])
         scatter(0, 0)
-        quantise(2, 1)
-        multiply(2, 1, False, True)
+        quantise("second2")
+        multiply([2], 1)
+        y_second = sb.tile([P, N_TILES, C], F32, name="y_second")
         for n in range(N_TILES):
-            activate(1, n)
+            activate(1, n, y_second[:, n, :], bias[:, n, 1:2])
         scatter(0, 1)
         scatter(0, 2)
         for n in range(N_TILES):

@@ -35,7 +35,7 @@ def tile_moe_pre_lin_relu_kernel(tc, xT, w_words, w_scales, b, gate, offs, out):
         gate_sb = sb.tile([P, S], F32, name="gate_sb")
         x_rows = [[sb.tile([P, T], F32, name="x_rows%d_%d" % (a, t), align_bytes=64) for t in range(PACK)] for a in range(PASSES)]
         w_codes = [sb.tile([P, PASSES, N], U32, name="w_codes%d" % e, align_bytes=64) for e in range(E)]
-        w_plane = sb.tile([P, E * PASSES, N], U8, name="w_plane", align_bytes=64)
+        w_plane = sb.tile([P, 2, N], U8, name="w_plane", align_bytes=64)
         bias = sb.tile([P, N_TILES, E], F32, name="bias")
         gate_mid = sb.tile([P, C], F32, name="gate_mid")
         gate_late = sb.tile([P, C], F32, name="gate_late")
@@ -57,14 +57,16 @@ def tile_moe_pre_lin_relu_kernel(tc, xT, w_words, w_scales, b, gate, offs, out):
                 if (a, t) != (0, 0):
                     nc.sync.dma_start(out=x_rows[a][t][:], in_=x_view[a, t])
         nc.sync.dma_start(out=gate_mid[:], in_=gate[P : 2 * P, C:S])
-        scale_view = w_scales.rearrange("e a (q r) n -> q r (e a) n", r=4)
+        scale_view = w_scales.rearrange("e a (q r) n -> q (e a) r n", r=4)
         for q in range(4):
-            nc.sync.dma_start(out=w_plane[32 * q : 32 * q + 4, :, :].bitcast(I32), in_=scale_view[q].bitcast(I32))
+            nc.sync.dma_start(out=w_plane[32 * q : 32 * q + 16, 0, :].bitcast(I32), in_=scale_view[q, 0:4].bitcast(I32))
         w_view = w_words.rearrange("e a p n t -> e p a (n t)")
         nc.sync.dma_start(out=w_codes[0][:].bitcast(I32), in_=w_view[0].bitcast(I32))
         nc.sync.dma_start(out=gate_late[:], in_=gate[2 * P : 3 * P, C:S])
         nc.sync.dma_start(out=bias_first[:], in_=b[0:P, 0:1])
         nc.sync.dma_start(out=bias[:], in_=b.rearrange("(n p) e -> p n e", p=P))
+        for q in range(4):
+            nc.sync.dma_start(out=w_plane[32 * q : 32 * q + 8, 1, :].bitcast(I32), in_=scale_view[q, 4:6].bitcast(I32))
         nc.sync.dma_start(out=w_codes[1][:].bitcast(I32), in_=w_view[1].bitcast(I32))
 
         gated = {}
@@ -119,7 +121,7 @@ def tile_moe_pre_lin_relu_kernel(tc, xT, w_words, w_scales, b, gate, offs, out):
                     nc.tensor.matmul_mx(
                         out=acc[e][n][:],
                         lhsT=w_codes[e][:, a, cols].bitcast(FP8X4),
-                        lhsT_scale=w_plane[:, e * PASSES + a, cols],
+                        lhsT_scale=w_plane[4 * ((e * PASSES + a) % 4) :, (e * PASSES + a) // 4, cols],
                         rhs=codes.bitcast(FP8X4),
                         rhs_scale=plane,
                         start=(a == 0),

@@ -33,148 +33,167 @@ def tile_moe_pre_lin_relu_kernel(tc, xT, w_words, w_scales, b, gate, offs, out):
 
         offsets = sb.tile([P, S // PER_COL], U16, name="offsets")
         gate_sb = sb.tile([P, S], F32, name="gate_sb")
-        x_rows = [[sb.tile([P, T], F32, name="x_rows%d_%d" % (a, t), align_bytes=64) for t in range(PACK)] for a in range(PASSES)]
-        w_codes = [sb.tile([P, PASSES, N], U32, name="w_codes%d" % e, align_bytes=64) for e in range(E)]
-        w_plane = sb.tile([P, 2, N], U8, name="w_plane", align_bytes=64)
-        bias = sb.tile([P, N_TILES, E], F32, name="bias")
-        gate_mid = sb.tile([P, C], F32, name="gate_mid")
         gate_late = sb.tile([P, C], F32, name="gate_late")
-        bias_first = sb.tile([P, 1], F32, name="bias_first", tag="share_a", align_bytes=64)
+        x_rows = [[sb.tile([P, T], F32, name="x_rows%d_%d" % (a, t), align_bytes=64) for t in range(PACK)] for a in range(PASSES)]
+        w_first = sb.tile([P, PASSES, P], U32, name="w_first", align_bytes=64)
+        w_rest = sb.tile([P, PASSES, N - P], U32, name="w_rest", align_bytes=64)
+        w_second = sb.tile([P, PASSES, N], U32, name="w_second", align_bytes=64)
+        planes = sb.tile([P, 3, N], U8, name="planes", align_bytes=64)
+        bias = sb.tile([P, N_TILES, E], F32, name="bias")
+        bias_first = sb.tile([P, 2, E], F32, name="bias_first", tag="share_a", align_bytes=64)
         result = [sb.tile([P, T], F32, name="result%d" % n) for n in range(N_TILES)]
         acc = [[psum.tile([P, C], F32, name="acc%d_%d" % (e, n)) for n in range(N_TILES)] for e in range(E)]
 
-        nc.vector.memset(w_plane[:].rearrange("p g n -> p (g n)").bitcast(I32), 0)
+        nc.vector.memset(planes[:].rearrange("p g n -> p (g n)").bitcast(I32), 0)
         for n in range(N_TILES):
             nc.vector.memset(result[n][:], 0.0)
 
         x_view = xT.rearrange("(a p t) j -> a t p j", p=P, t=PACK)
-        nc.sync.dma_start(out=x_rows[0][0][:], in_=x_view[0, 0])
+        scale_view = w_scales.rearrange("e a (q r) n -> q (e a) r n", r=4)
+        w_view = w_words.rearrange("e a p n t -> e p a (n t)")
+
+        def load_x(a, t):
+            nc.sync.dma_start(out=x_rows[a][t][:], in_=x_view[a, t])
+
+        def load_scales(g):
+            for q in range(4):
+                nc.sync.dma_start(out=planes[32 * q + 4 : 32 * q + 12, g, 0:N].bitcast(I32), in_=scale_view[q, 2 * g : 2 * g + 2].bitcast(I32))
+
+        load_x(0, 0)
         nc.sync.dma_start(out=gate_sb[:, 0:C], in_=gate[0:P, 0:C])
         nc.sync.dma_start(offsets[:], offs)
         nc.sync.dma_start(out=gate_sb[:, C:S], in_=gate[0:P, C:S])
-        for a in range(PASSES):
-            for t in range(PACK):
-                if (a, t) != (0, 0):
-                    nc.sync.dma_start(out=x_rows[a][t][:], in_=x_view[a, t])
-        nc.sync.dma_start(out=gate_mid[:], in_=gate[P : 2 * P, C:S])
-        scale_view = w_scales.rearrange("e a (q r) n -> q (e a) r n", r=4)
-        for q in range(4):
-            nc.sync.dma_start(out=w_plane[32 * q : 32 * q + 16, 0, :].bitcast(I32), in_=scale_view[q, 0:4].bitcast(I32))
-        w_view = w_words.rearrange("e a p n t -> e p a (n t)")
-        nc.sync.dma_start(out=w_codes[0][:].bitcast(I32), in_=w_view[0].bitcast(I32))
-        nc.sync.dma_start(out=gate_late[:], in_=gate[2 * P : 3 * P, C:S])
-        nc.sync.dma_start(out=bias_first[:], in_=b[0:P, 0:1])
+        for t in range(1, PACK):
+            load_x(0, t)
+        for t in range(PACK):
+            load_x(1, t)
+        load_scales(0)
+        for t in range(PACK - 1):
+            load_x(2, t)
+        load_scales(1)
+        load_x(2, PACK - 1)
+        nc.sync.dma_start(out=gate_late[:], in_=gate[P : 2 * P, C:S])
+        nc.sync.dma_start(out=w_first[:].bitcast(I32), in_=w_view[0, :, :, 0 : PACK * P].bitcast(I32))
+        nc.sync.dma_start(out=w_rest[:].bitcast(I32), in_=w_view[0, :, :, PACK * P : PACK * N].bitcast(I32))
+        nc.sync.dma_start(out=bias_first[:], in_=b[0 : 2 * P, :].rearrange("(n p) e -> p n e", p=P))
         nc.sync.dma_start(out=bias[:], in_=b.rearrange("(n p) e -> p n e", p=P))
-        for q in range(4):
-            nc.sync.dma_start(out=w_plane[32 * q : 32 * q + 8, 1, :].bitcast(I32), in_=scale_view[q, 4:6].bitcast(I32))
-        nc.sync.dma_start(out=w_codes[1][:].bitcast(I32), in_=w_view[1].bitcast(I32))
+        load_scales(2)
+        nc.sync.dma_start(out=w_second[:].bitcast(I32), in_=w_view[1].bitcast(I32))
 
-        gated = {}
-        for a in range(PASSES - 1):
-            both = sb.tile([P, PACK, S], F32, name="gated%d" % a)
-            gated[(a, 0)] = both[:, :, 0:C]
-            gated[(a, 1)] = both[:, :, C:S]
-            gated[(a, None)] = both[:]
-        last_a = sb.tile([P, PACK, C], F32, name="gated_last0")
-        last_b = sb.tile([P, PACK, C], F32, name="gated_last1", tag="share_b")
-        gated[(PASSES - 1, 0)] = last_a[:]
-        gated[(PASSES - 1, 1)] = last_b[:]
+        def slots(e):
+            return (0, S) if e is None else (e * C, (e + 1) * C)
+
+        def gather(target, a, t, e, weights):
+            lo, hi = slots(e)
+            nc.vector.tensor_tensor(target, x_rows[a][t][:].indirect(offsets[:, lo // PER_COL : hi // PER_COL]), weights, MULT)
+
+        def weave(grouped, source):
+            nc.scalar.copy(grouped, source.rearrange("p t j -> p j t"))
+
         quantised = {}
 
-        def gather(a, t, e, weights=None):
-            lo, hi = (0, S) if e is None else (e * C, (e + 1) * C)
-            nc.vector.tensor_tensor(
-                gated[(a, e)][:, t, :],
-                x_rows[a][t][:].indirect(offsets[:, lo // PER_COL : hi // PER_COL]),
-                gate_sb[:, lo:hi] if weights is None else weights[:],
-                MULT,
-            )
+        def quantise(a, e, grouped, codes, plane):
+            nc.vector.quantize_mx(out=codes.bitcast(FP8X4), scales=plane, in_=grouped.rearrange("p j t -> p (j t)"))
+            for i, expert in enumerate(range(E) if e is None else [e]):
+                quantised[(a, expert)] = (codes[:, i * C : (i + 1) * C], plane[:, i * C : (i + 1) * C])
 
-        calls = {
-            "first0": ([(0, 0)], "grouped_first0", "x_rows1_3"),
-            "first12": ([(1, 0), (2, 0)], "grouped_first12", "codes_first12"),
-            "second01": ([(0, 1), (1, 1)], "grouped_second01", "x_rows2_2"),
-            "second2": ([(2, 1)], "share_a", "codes_second2"),
-        }
-        call_input = {}
+        def weights_of(e, a, n):
+            if e == 1:
+                return w_second[:, a, n * P : (n + 1) * P]
+            if n == 0:
+                return w_first[:, a, :]
+            return w_rest[:, a, (n - 1) * P : n * P]
 
-        def interleave(a, e):
-            for name, (members, tag, codes_tag) in calls.items():
-                if (a, e) in members:
-                    if name not in call_input:
-                        call_input[name] = sb.tile([P, len(members), C, PACK], BF16, name="grouped_" + name, tag=tag, align_bytes=64)
-                    nc.scalar.copy(call_input[name][:, members.index((a, e))], gated[(a, e)].rearrange("p t j -> p j t"))
-
-        def quantise(name):
-            members, tag, codes_tag = calls[name]
-            codes = sb.tile([P, len(members) * C], U32, name="codes_" + name, tag=codes_tag, align_bytes=64)
-            plane = sb.tile([P, len(members) * C], U8, name="plane_" + name, align_bytes=64)
-            nc.vector.quantize_mx(out=codes[:].bitcast(FP8X4), scales=plane[:], in_=call_input[name][:].rearrange("p m j t -> p (m j t)"))
-            for i, member in enumerate(members):
-                quantised[member] = (codes[:, i * C : (i + 1) * C], plane[:, i * C : (i + 1) * C])
-
-        def multiply(passes, e):
-            for n in range(N_TILES):
-                cols = slice(n * P, (n + 1) * P)
-                for a in passes:
-                    codes, plane = quantised[(a, e)]
-                    nc.tensor.matmul_mx(
-                        out=acc[e][n][:],
-                        lhsT=w_codes[e][:, a, cols].bitcast(FP8X4),
-                        lhsT_scale=w_plane[4 * ((e * PASSES + a) % 4) :, (e * PASSES + a) // 4, cols],
-                        rhs=codes.bitcast(FP8X4),
-                        rhs_scale=plane,
-                        start=(a == 0),
-                        stop=(a == PASSES - 1),
-                    )
+        def multiply(e, n, passes, first, last):
+            for a in passes:
+                codes, plane = quantised[(a, e)]
+                g, k = divmod(e * PASSES + a, 2)
+                nc.tensor.matmul_mx(
+                    out=acc[e][n][:],
+                    lhsT=weights_of(e, a, n).bitcast(FP8X4),
+                    lhsT_scale=planes[4 + 4 * k :, g, n * P : (n + 1) * P],
+                    rhs=codes.bitcast(FP8X4),
+                    rhs_scale=plane,
+                    start=(a == first),
+                    stop=(a == last),
+                )
 
         ys = {}
 
-        def activate(e, n, y, column):
-            nc.scalar.activation(y, acc[e][n][:], RELU, bias=column)
+        def activate(e, n, column, tag=None):
+            y = sb.tile([P, C], F32, name="y%d_%d" % (e, n), tag=tag or "y%d_%d" % (e, n))
+            nc.scalar.activation(y[:], acc[e][n][:], RELU, bias=column)
             ys[(e, n)] = y
 
         def scatter(e, n):
-            nc.vector.tensor_copy(result[n][:].indirect(offsets[:, e * C // PER_COL : (e + 1) * C // PER_COL]), ys[(e, n)])
+            lo, hi = slots(e)
+            nc.vector.tensor_copy(result[n][:].indirect(offsets[:, lo // PER_COL : hi // PER_COL]), ys[(e, n)][:])
 
-        gather(0, 0, 0)
-        gather(0, 0, 1)
+        gated0 = sb.tile([P, PACK, S], F32, name="gated0")
+        grouped0 = sb.tile([P, S, PACK], BF16, name="grouped0", align_bytes=64)
+        codes00 = sb.tile([P, C], U32, name="codes00", align_bytes=64)
+        gather(gated0[:, 0, 0:C], 0, 0, 0, gate_sb[:, 0:C])
+        gather(gated0[:, 0, C:S], 0, 0, 1, gate_sb[:, C:S])
         for t in range(1, PACK):
-            gather(0, t, None)
-        interleave(0, 0)
-        interleave(0, 1)
-        for t in range(PACK - 1):
-            gather(1, t, None)
-        gather(1, PACK - 1, 0)
-        interleave(1, 0)
-        for t in range(PACK):
-            gather(2, t, 0)
-        interleave(2, 0)
-        gather(1, PACK - 1, 1, gate_mid)
-        interleave(1, 1)
-        gather(2, 0, 1, gate_mid)
-        quantise("first0")
-        multiply([0], 0)
-        gather(2, 1, 1, gate_mid)
-        quantise("first12")
-        multiply([1, 2], 0)
-        y_first = sb.tile([P, C], F32, name="y_first")
-        activate(0, 0, y_first[:], bias_first[:])
-        gather(2, 2, 1, gate_late)
-        gather(2, 3, 1, gate_late)
-        quantise("second01")
-        multiply([0, 1], 1)
-        interleave(2, 1)
-        y_rest = sb.tile([P, N_TILES - 1, C], F32, name="y_rest", tag="share_b")
+            gather(gated0[:, t, :], 0, t, None, gate_sb[:])
+        weave(grouped0[:], gated0[:])
+
+        grouped1 = sb.tile([P, S, PACK], BF16, name="grouped1", align_bytes=64)
+        for u in range(2):
+            pair = sb.tile([P, 2, S], F32, name="pair1_%d" % u)
+            for i in range(2):
+                gather(pair[:, i, :], 1, 2 * u + i, None, gate_sb[:])
+            weave(grouped1[:, :, 2 * u : 2 * u + 2], pair[:])
+        quantise(0, 0, grouped0[:, 0:C, :], codes00[:], planes[:, 0, 0:C])
+
+        grouped20 = sb.tile([P, C, PACK], BF16, name="grouped20", align_bytes=64)
+        pair = sb.tile([P, 2, C], F32, name="pair20_0")
+        for i in range(2):
+            gather(pair[:, i, :], 2, i, 0, gate_sb[:, 0:C])
+        weave(grouped20[:, :, 0:2], pair[:])
+        pair = sb.tile([P, 2, C], F32, name="pair20_1", tag="share_c")
+        gather(pair[:, 0, :], 2, 2, 0, gate_sb[:, 0:C])
+        codes10 = sb.tile([P, C], U32, name="codes10", align_bytes=64)
+        quantise(1, 0, grouped1[:, 0:C, :], codes10[:], planes[:, 1, 0:C])
+        gather(pair[:, 1, :], 2, 3, 0, gate_sb[:, 0:C])
+        weave(grouped20[:, :, 2:4], pair[:])
+        multiply(0, 0, [0, 1], 0, 2)
+
+        low = sb.tile([P, 2, C], F32, name="pair21_0")
+        for i in range(2):
+            gather(low[:, i, :], 2, i, 1, gate_late[:])
+        codes01 = sb.tile([P, C], U32, name="codes01", tag="x_rows2_0", align_bytes=64)
+        plane01 = sb.tile([P, C], U8, name="plane01", align_bytes=64)
+        quantise(0, 1, grouped0[:, C:S, :], codes01[:], plane01[:])
+        codes20 = sb.tile([P, C], U32, name="codes20", align_bytes=64)
+        plane20 = sb.tile([P, C], U8, name="plane20", align_bytes=64)
+        quantise(2, 0, grouped20[:], codes20[:], plane20[:])
+        multiply(0, 0, [2], 0, 2)
         for n in range(1, N_TILES):
-            activate(0, n, y_rest[:, n - 1, :], bias[:, n, 0:1])
-        scatter(0, 0)
-        quantise("second2")
-        multiply([2], 1)
-        y_second = sb.tile([P, N_TILES, C], F32, name="y_second")
+            multiply(0, n, [2, 0, 1], 2, 1)
+        for n in range(2):
+            activate(0, n, bias_first[:, n, 0:1])
+        high = sb.tile([P, 2, C], F32, name="pair21_1", tag="share_c")
+        for i in range(2):
+            gather(high[:, i, :], 2, 2 + i, 1, gate_late[:])
+        codes11 = sb.tile([P, C], U32, name="codes11", tag="x_rows2_2", align_bytes=64)
+        plane11 = sb.tile([P, C], U8, name="plane11", align_bytes=64)
+        quantise(1, 1, grouped1[:, C:S, :], codes11[:], plane11[:])
         for n in range(N_TILES):
-            activate(1, n, y_second[:, n, :], bias[:, n, 1:2])
+            multiply(1, n, [1, 0], 1, 2)
+        grouped21 = sb.tile([P, C, PACK], BF16, name="grouped21", tag="share_a", align_bytes=64)
+        weave(grouped21[:, :, 0:2], low[:])
+        weave(grouped21[:, :, 2:4], high[:])
+        activate(0, 2, bias[:, 2, 0:1], "share_c")
+        scatter(0, 0)
         scatter(0, 1)
+        codes21 = sb.tile([P, C], U32, name="codes21", align_bytes=64)
+        plane21 = sb.tile([P, C], U8, name="plane21", align_bytes=64)
+        quantise(2, 1, grouped21[:], codes21[:], plane21[:])
+        for n in range(N_TILES):
+            multiply(1, n, [2], 1, 2)
+        for n in range(N_TILES):
+            activate(1, n, bias[:, n, 1:2])
         scatter(0, 2)
         for n in range(N_TILES):
             scatter(1, n)

@@ -1,6 +1,7 @@
 from contextlib import ExitStack
 
 import concourse.mybir as mybir
+from concourse.masks import make_identity
 
 K, T, E, C, N = 1536, 768, 2, 256, 384
 S = E * C
@@ -10,6 +11,7 @@ K_PASS = P * PACK
 PASSES = K // K_PASS
 N_TILES = N // P
 PER_COL = 16
+GROUPS = S // P
 
 F32 = mybir.dt.float32
 BF16 = mybir.dt.bfloat16
@@ -20,6 +22,7 @@ U8 = mybir.dt.uint8
 FP8X4 = mybir.dt.float8_e4m3fn_x4
 MULT = mybir.AluOpType.mult
 RELU = mybir.ActivationFunctionType.Relu
+COPY = mybir.ActivationFunctionType.Copy
 
 FLOPS = 2 * K * N * S
 BYTES = 4 * K * T + E * K * N + E * (K // 32) * N + 4 * N * E + 4 * S + 2 * S + 4 * N * T
@@ -29,6 +32,7 @@ def tile_moe_pre_lin_relu_kernel(tc, xT, w_words, w_scales, b, gate, offs, out):
     nc = tc.nc
     with ExitStack() as ctx:
         sb = ctx.enter_context(tc.tile_pool(name="sb", bufs=1))
+        reused = ctx.enter_context(tc.tile_pool(name="reused", bufs=1))
         psum = ctx.enter_context(tc.psum_pool(name="psum", bufs=1))
 
         offsets = sb.tile([P, S // PER_COL], U16, name="offsets")
@@ -38,11 +42,13 @@ def tile_moe_pre_lin_relu_kernel(tc, xT, w_words, w_scales, b, gate, offs, out):
         w_first = sb.tile([P, PASSES, P], U32, name="w_first", align_bytes=64)
         w_rest = sb.tile([P, PASSES, N - P], U32, name="w_rest", align_bytes=64)
         w_second = sb.tile([P, PASSES, N], U32, name="w_second", align_bytes=64)
-        planes = sb.tile([P, 3, N], U8, name="planes", align_bytes=64)
+        planes = sb.tile([P, 2, N], U8, name="planes", align_bytes=64)
+        gate_cols = sb.tile([P, GROUPS], F32, name="gate_cols")
+        identity = sb.tile([P, P], F32, name="identity")
         bias = sb.tile([P, N_TILES, E], F32, name="bias")
         bias_first = sb.tile([P, 2, E], F32, name="bias_first", tag="share_a", align_bytes=64)
         result = [sb.tile([P, T], F32, name="result%d" % n) for n in range(N_TILES)]
-        acc = [[psum.tile([P, C], F32, name="acc%d_%d" % (e, n)) for n in range(N_TILES)] for e in range(E)]
+        make_identity(nc, identity[:])
 
         nc.vector.memset(planes[:].rearrange("p g n -> p (g n)").bitcast(I32), 0)
         for n in range(N_TILES):
@@ -55,29 +61,24 @@ def tile_moe_pre_lin_relu_kernel(tc, xT, w_words, w_scales, b, gate, offs, out):
         def load_x(a, t):
             nc.sync.dma_start(out=x_rows[a][t][:], in_=x_view[a, t])
 
-        def load_scales(g):
+        def load_scales(g, first, count):
             for q in range(4):
-                nc.sync.dma_start(out=planes[32 * q + 4 : 32 * q + 12, g, 0:N].bitcast(I32), in_=scale_view[q, 2 * g : 2 * g + 2].bitcast(I32))
+                nc.sync.dma_start(out=planes[32 * q : 32 * q + 4 * count, g, :].bitcast(I32), in_=scale_view[q, first : first + count].bitcast(I32))
 
         load_x(0, 0)
-        nc.sync.dma_start(out=gate_sb[:, 0:C], in_=gate[0:P, 0:C])
         nc.sync.dma_start(offsets[:], offs)
-        nc.sync.dma_start(out=gate_sb[:, C:S], in_=gate[0:P, C:S])
-        for t in range(1, PACK):
-            load_x(0, t)
-        for t in range(PACK):
-            load_x(1, t)
-        load_scales(0)
-        for t in range(PACK - 1):
-            load_x(2, t)
-        load_scales(1)
-        load_x(2, PACK - 1)
+        nc.sync.dma_start(out=gate_cols[:], in_=gate[0, :].rearrange("(p g) -> p g", g=GROUPS))
+        for a in range(PASSES):
+            for t in range(PACK):
+                if (a, t) != (0, 0):
+                    load_x(a, t)
         nc.sync.dma_start(out=gate_late[:], in_=gate[P : 2 * P, C:S])
+        load_scales(0, 0, 4)
         nc.sync.dma_start(out=w_first[:].bitcast(I32), in_=w_view[0, :, :, 0 : PACK * P].bitcast(I32))
         nc.sync.dma_start(out=w_rest[:].bitcast(I32), in_=w_view[0, :, :, PACK * P : PACK * N].bitcast(I32))
         nc.sync.dma_start(out=bias_first[:], in_=b[0 : 2 * P, :].rearrange("(n p) e -> p n e", p=P))
         nc.sync.dma_start(out=bias[:], in_=b.rearrange("(n p) e -> p n e", p=P))
-        load_scales(2)
+        load_scales(1, 4, 2)
         nc.sync.dma_start(out=w_second[:].bitcast(I32), in_=w_view[1].bitcast(I32))
 
         def slots(e):
@@ -92,10 +93,13 @@ def tile_moe_pre_lin_relu_kernel(tc, xT, w_words, w_scales, b, gate, offs, out):
 
         quantised = {}
 
-        def quantise(a, e, grouped, codes, plane):
-            nc.vector.quantize_mx(out=codes.bitcast(FP8X4), scales=plane, in_=grouped.rearrange("p j t -> p (j t)"))
-            for i, expert in enumerate(range(E) if e is None else [e]):
-                quantised[(a, expert)] = (codes[:, i * C : (i + 1) * C], plane[:, i * C : (i + 1) * C])
+        def quantise(members, grouped, tag):
+            name = "%d%d" % members[0]
+            codes = sb.tile([P, len(members) * C], U32, name="codes" + name, tag=tag or "codes" + name, align_bytes=64)
+            plane = sb.tile([P, len(members) * C], U8, name="plane" + name, align_bytes=64)
+            nc.vector.quantize_mx(out=codes[:].bitcast(FP8X4), scales=plane[:], in_=grouped)
+            for i, member in enumerate(members):
+                quantised[member] = (codes[:, i * C : (i + 1) * C], plane[:, i * C : (i + 1) * C])
 
         def weights_of(e, a, n):
             if e == 1:
@@ -107,11 +111,11 @@ def tile_moe_pre_lin_relu_kernel(tc, xT, w_words, w_scales, b, gate, offs, out):
         def multiply(e, n, passes, first, last):
             for a in passes:
                 codes, plane = quantised[(a, e)]
-                g, k = divmod(e * PASSES + a, 2)
+                g, k = divmod(e * PASSES + a, 4)
                 nc.tensor.matmul_mx(
                     out=acc[e][n][:],
                     lhsT=weights_of(e, a, n).bitcast(FP8X4),
-                    lhsT_scale=planes[4 + 4 * k :, g, n * P : (n + 1) * P],
+                    lhsT_scale=planes[4 * k :, g, n * P : (n + 1) * P],
                     rhs=codes.bitcast(FP8X4),
                     rhs_scale=plane,
                     start=(a == first),
@@ -120,8 +124,11 @@ def tile_moe_pre_lin_relu_kernel(tc, xT, w_words, w_scales, b, gate, offs, out):
 
         ys = {}
 
-        def activate(e, n, column, tag=None):
-            y = sb.tile([P, C], F32, name="y%d_%d" % (e, n), tag=tag or "y%d_%d" % (e, n))
+        def activate(e, n, column, offset=None):
+            if offset is None:
+                y = sb.tile([P, C], F32, name="y%d_%d" % (e, n))
+            else:
+                y = reused.tile([P, C], F32, name="y%d_%d" % (e, n), offset=offset, align_bytes=64)
             nc.scalar.activation(y[:], acc[e][n][:], RELU, bias=column)
             ys[(e, n)] = y
 
@@ -129,69 +136,78 @@ def tile_moe_pre_lin_relu_kernel(tc, xT, w_words, w_scales, b, gate, offs, out):
             lo, hi = slots(e)
             nc.vector.tensor_copy(result[n][:].indirect(offsets[:, lo // PER_COL : hi // PER_COL]), ys[(e, n)][:])
 
-        gated0 = sb.tile([P, PACK, S], F32, name="gated0")
-        grouped0 = sb.tile([P, S, PACK], BF16, name="grouped0", align_bytes=64)
-        codes00 = sb.tile([P, C], U32, name="codes00", align_bytes=64)
-        gather(gated0[:, 0, 0:C], 0, 0, 0, gate_sb[:, 0:C])
-        gather(gated0[:, 0, C:S], 0, 0, 1, gate_sb[:, C:S])
-        for t in range(1, PACK):
-            gather(gated0[:, t, :], 0, t, None, gate_sb[:])
-        weave(grouped0[:], gated0[:])
+        picked = [sb.tile([P, P, GROUPS], F32, name="picked%d" % t) for t in range(2)]
+        for t in range(2):
+            nc.vector.tensor_copy(picked[t][:].rearrange("k p g -> k (p g)"), x_rows[0][t][:].indirect(offsets[:]))
 
-        grouped1 = sb.tile([P, S, PACK], BF16, name="grouped1", align_bytes=64)
-        for u in range(2):
-            pair = sb.tile([P, 2, S], F32, name="pair1_%d" % u)
-            for i in range(2):
-                gather(pair[:, i, :], 1, 2 * u + i, None, gate_sb[:])
-            weave(grouped1[:, :, 2 * u : 2 * u + 2], pair[:])
-        quantise(0, 0, grouped0[:, 0:C, :], codes00[:], planes[:, 0, 0:C])
+        spread = psum.tile([P, GROUPS, P], F32, name="spread", tag="acc1_0")
+        for g in range(GROUPS):
+            nc.tensor.transpose(spread[:, g, :], gate_cols[:, g : g + 1].to_broadcast([P, P]), identity[:])
+        nc.scalar.copy(gate_sb[:].rearrange("k (p g) -> k p g", g=GROUPS), spread[:].rearrange("k g p -> k p g"))
 
-        grouped20 = sb.tile([P, C, PACK], BF16, name="grouped20", align_bytes=64)
-        pair = sb.tile([P, 2, C], F32, name="pair20_0")
+        grouped = sb.tile([P, 3, C, PACK], BF16, name="grouped", align_bytes=64)
+        pass0 = grouped[:, 1:3]
+        back = [psum.tile([P, 2, 2, P], F32, name="back%d" % h) for h in range(2)]
+        for t in range(2):
+            by_slot = psum.tile([P, GROUPS, P], F32, name="by_slot%d" % t, tag="acc1_%d" % (t + 1))
+            scaled = sb.tile([P, GROUPS, P], F32, name="scaled%d" % t)
+            for g in range(GROUPS):
+                nc.tensor.transpose(by_slot[:, g, :], picked[t][:, :, g], identity[:])
+            for g in range(GROUPS):
+                nc.scalar.activation(scaled[:, g, :], by_slot[:, g, :], COPY, scale=gate_cols[:, g : g + 1])
+            for g in range(GROUPS):
+                nc.tensor.transpose(back[g // 2][:, t, g % 2, :], scaled[:, g, :], identity[:])
+        for h in range(2):
+            target = pass0[:, :, :, 0:2].rearrange("k e (p g) t -> k (e p) g t", g=GROUPS)[:, :, 2 * h : 2 * h + 2, :]
+            nc.scalar.copy(target, back[h][:].rearrange("k t g p -> k p g t"))
+        acc = [[psum.tile([P, C], F32, name="acc%d_%d" % (e, n)) for n in range(N_TILES)] for e in range(E)]
+
+        pair0 = sb.tile([P, 2, S], F32, name="pair0", align_bytes=64)
         for i in range(2):
-            gather(pair[:, i, :], 2, i, 0, gate_sb[:, 0:C])
-        weave(grouped20[:, :, 0:2], pair[:])
-        pair = sb.tile([P, 2, C], F32, name="pair20_1", tag="share_c")
-        gather(pair[:, 0, :], 2, 2, 0, gate_sb[:, 0:C])
-        codes10 = sb.tile([P, C], U32, name="codes10", align_bytes=64)
-        quantise(1, 0, grouped1[:, 0:C, :], codes10[:], planes[:, 1, 0:C])
-        gather(pair[:, 1, :], 2, 3, 0, gate_sb[:, 0:C])
-        weave(grouped20[:, :, 2:4], pair[:])
-        multiply(0, 0, [0, 1], 0, 2)
+            gather(pair0[:, i, :], 0, 2 + i, None, gate_sb[:])
+        weave(pass0[:, :, :, 2:4].rearrange("k e j t -> k (e j) t"), pair0[:])
+
+        gated1 = sb.tile([P, PACK, S], F32, name="gated1")
+        for t in range(PACK):
+            gather(gated1[:, t, :], 1, t, None, gate_sb[:])
+        weave(grouped[:, 0], gated1[:, :, 0:C])
+
+        grouped20 = sb.tile([P, C, PACK], BF16, name="grouped20", tag="pair0", align_bytes=64)
+        pairs = [sb.tile([P, 2, C], F32, name="pair20_0"), reused.tile([P, 2, C], F32, name="pair20_1", offset=1024, align_bytes=64)]
+        for u in range(2):
+            for i in range(2):
+                gather(pairs[u][:, i, :], 2, 2 * u + i, 0, gate_sb[:, 0:C])
+            weave(grouped20[:, :, 2 * u : 2 * u + 2], pairs[u][:])
+        grouped11 = reused.tile([P, C, PACK], BF16, name="grouped11", offset=0, align_bytes=64)
+        weave(grouped11[:], gated1[:, :, C:S])
 
         low = sb.tile([P, 2, C], F32, name="pair21_0")
         for i in range(2):
             gather(low[:, i, :], 2, i, 1, gate_late[:])
-        codes01 = sb.tile([P, C], U32, name="codes01", tag="x_rows2_0", align_bytes=64)
-        plane01 = sb.tile([P, C], U8, name="plane01", align_bytes=64)
-        quantise(0, 1, grouped0[:, C:S, :], codes01[:], plane01[:])
-        codes20 = sb.tile([P, C], U32, name="codes20", align_bytes=64)
-        plane20 = sb.tile([P, C], U8, name="plane20", align_bytes=64)
-        quantise(2, 0, grouped20[:], codes20[:], plane20[:])
+        quantise([(1, 0), (0, 0)], grouped[:, 0:2].rearrange("k a j t -> k (a j t)"), "x_rows2_0")
+        multiply(0, 0, [0, 1], 0, 2)
+        quantise([(2, 0)], grouped20[:].rearrange("k j t -> k (j t)"), None)
         multiply(0, 0, [2], 0, 2)
         for n in range(1, N_TILES):
             multiply(0, n, [2, 0, 1], 2, 1)
         for n in range(2):
             activate(0, n, bias_first[:, n, 0:1])
-        high = sb.tile([P, 2, C], F32, name="pair21_1", tag="share_c")
+        high = reused.tile([P, 2, C], F32, name="pair21_1", offset=2048, align_bytes=64)
         for i in range(2):
             gather(high[:, i, :], 2, 2 + i, 1, gate_late[:])
-        codes11 = sb.tile([P, C], U32, name="codes11", tag="x_rows2_2", align_bytes=64)
-        plane11 = sb.tile([P, C], U8, name="plane11", align_bytes=64)
-        quantise(1, 1, grouped1[:, C:S, :], codes11[:], plane11[:])
+        quantise([(0, 1)], grouped[:, 2].rearrange("k j t -> k (j t)"), "x_rows2_2")
+        quantise([(1, 1)], grouped11[:].rearrange("k j t -> k (j t)"), None)
         for n in range(N_TILES):
-            multiply(1, n, [1, 0], 1, 2)
+            multiply(1, n, [0, 1], 0, 2)
         grouped21 = sb.tile([P, C, PACK], BF16, name="grouped21", tag="share_a", align_bytes=64)
         weave(grouped21[:, :, 0:2], low[:])
         weave(grouped21[:, :, 2:4], high[:])
-        activate(0, 2, bias[:, 2, 0:1], "share_c")
+        activate(0, 2, bias[:, 2, 0:1], 3072)
         scatter(0, 0)
         scatter(0, 1)
-        codes21 = sb.tile([P, C], U32, name="codes21", align_bytes=64)
-        plane21 = sb.tile([P, C], U8, name="plane21", align_bytes=64)
-        quantise(2, 1, grouped21[:], codes21[:], plane21[:])
+        quantise([(2, 1)], grouped21[:].rearrange("k j t -> k (j t)"), None)
         for n in range(N_TILES):
-            multiply(1, n, [2], 1, 2)
+            multiply(1, n, [2], 0, 2)
         for n in range(N_TILES):
             activate(1, n, bias[:, n, 1:2])
         scatter(0, 2)

@@ -51,8 +51,7 @@ def tile_moe_pre_lin_relu_kernel(tc, xT, w_words, w_scales, b, gate, offs, out):
         make_identity(nc, identity[:])
 
         nc.vector.memset(planes[:].rearrange("p g n -> p (g n)").bitcast(I32), 0)
-        for n in range(N_TILES):
-            nc.vector.memset(result[n][:], 0.0)
+        nc.vector.memset(result[0][:], 0.0)
 
         x_view = xT.rearrange("(a p t) j -> a t p j", p=P, t=PACK)
         scale_view = w_scales.rearrange("e a (q r) n -> q (e a) r n", r=4)
@@ -67,7 +66,9 @@ def tile_moe_pre_lin_relu_kernel(tc, xT, w_words, w_scales, b, gate, offs, out):
 
         load_x(0, 0)
         nc.sync.dma_start(offsets[:], offs)
-        nc.sync.dma_start(out=gate_cols[:], in_=gate[0, :].rearrange("(p g) -> p g", g=GROUPS))
+        nc.scalar.dma_start(out=gate_cols[:], in_=gate[0, :].rearrange("(p g) -> p g", g=GROUPS))
+        for n in range(1, N_TILES):
+            nc.scalar.copy(result[n][:], result[0][:])
         for a in range(PASSES):
             for t in range(PACK):
                 if (a, t) != (0, 0):

@@ -7,11 +7,13 @@ K, T, E, C, N = 1536, 768, 2, 256, 384
 S = E * C
 P = 128
 PACK = 4
-K_PASS = P * PACK
-PASSES = K // K_PASS
+PASSES = K // (P * PACK)
+LAST = PASSES - 1
 N_TILES = N // P
 PER_COL = 16
 GROUPS = S // P
+PLANES = 4
+PAIR_BYTES = 2 * C * 4
 
 F32 = mybir.dt.float32
 BF16 = mybir.dt.bfloat16
@@ -32,37 +34,40 @@ def tile_moe_pre_lin_relu_kernel(tc, xT, w_words, w_scales, b, gate, offs, out):
     nc = tc.nc
     with ExitStack() as ctx:
         sb = ctx.enter_context(tc.tile_pool(name="sb", bufs=1))
-        reused = ctx.enter_context(tc.tile_pool(name="reused", bufs=1))
+        placed = ctx.enter_context(tc.tile_pool(name="placed", bufs=1))
         psum = ctx.enter_context(tc.psum_pool(name="psum", bufs=1))
 
         offsets = sb.tile([P, S // PER_COL], U16, name="offsets")
-        gate_sb = sb.tile([P, S], F32, name="gate_sb")
+        gate_rows = sb.tile([P, S], F32, name="gate_rows")
         gate_late = sb.tile([P, C], F32, name="gate_late")
         x_rows = [[sb.tile([P, T], F32, name="x_rows%d_%d" % (a, t), align_bytes=64) for t in range(PACK)] for a in range(PASSES)]
         w_first = sb.tile([P, PASSES, P], U32, name="w_first", align_bytes=64)
         w_rest = sb.tile([P, PASSES, N - P], U32, name="w_rest", align_bytes=64)
         w_second = sb.tile([P, PASSES, N], U32, name="w_second", align_bytes=64)
-        planes = sb.tile([P, 2, N], U8, name="planes", align_bytes=64)
+        w_planes = sb.tile([P, 2, N], U8, name="w_planes", align_bytes=64)
         gate_cols = sb.tile([P, GROUPS], F32, name="gate_cols")
         identity = sb.tile([P, P], F32, name="identity")
-        bias = sb.tile([P, N_TILES, E], F32, name="bias")
-        bias_first = sb.tile([P, 2, E], F32, name="bias_first", tag="share_a", align_bytes=64)
+        bias_first = sb.tile([P, N_TILES - 1, 1], F32, name="bias_first", align_bytes=64)
+        bias_second = sb.tile([P, N_TILES - 1, 1], F32, name="bias_second")
+        bias_last = sb.tile([P, E], F32, name="bias_last")
         result = [sb.tile([P, T], F32, name="result%d" % n) for n in range(N_TILES)]
         make_identity(nc, identity[:])
 
-        nc.vector.memset(planes[:].rearrange("p g n -> p (g n)").bitcast(I32), 0)
+        nc.vector.memset(w_planes[:].rearrange("p g n -> p (g n)").bitcast(I32), 0)
         nc.vector.memset(result[0][:], 0.0)
 
         x_view = xT.rearrange("(a p t) j -> a t p j", p=P, t=PACK)
         scale_view = w_scales.rearrange("e a (q r) n -> q (e a) r n", r=4)
         w_view = w_words.rearrange("e a p n t -> e p a (n t)")
+        bias_view = b.rearrange("(n p) e -> p n e", p=P)
 
         def load_x(a, t):
             nc.sync.dma_start(out=x_rows[a][t][:], in_=x_view[a, t])
 
-        def load_scales(g, first, count):
+        def load_scales(g, count):
             for q in range(4):
-                nc.sync.dma_start(out=planes[32 * q : 32 * q + 4 * count, g, :].bitcast(I32), in_=scale_view[q, first : first + count].bitcast(I32))
+                source = scale_view[q, PLANES * g : PLANES * g + count]
+                nc.sync.dma_start(out=w_planes[32 * q : 32 * q + 4 * count, g, :].bitcast(I32), in_=source.bitcast(I32))
 
         load_x(0, 0)
         nc.sync.dma_start(offsets[:], offs)
@@ -74,31 +79,31 @@ def tile_moe_pre_lin_relu_kernel(tc, xT, w_words, w_scales, b, gate, offs, out):
                 if (a, t) != (0, 0):
                     load_x(a, t)
         nc.sync.dma_start(out=gate_late[:], in_=gate[P : 2 * P, C:S])
-        load_scales(0, 0, 4)
+        load_scales(0, PLANES)
         nc.sync.dma_start(out=w_first[:].bitcast(I32), in_=w_view[0, :, :, 0 : PACK * P].bitcast(I32))
         nc.sync.dma_start(out=w_rest[:].bitcast(I32), in_=w_view[0, :, :, PACK * P : PACK * N].bitcast(I32))
-        nc.sync.dma_start(out=bias_first[:], in_=b[0 : 2 * P, :].rearrange("(n p) e -> p n e", p=P))
-        nc.sync.dma_start(out=bias[:], in_=b.rearrange("(n p) e -> p n e", p=P))
-        load_scales(1, 4, 2)
+        nc.sync.dma_start(out=bias_first[:], in_=bias_view[:, 0 : N_TILES - 1, 0:1])
+        nc.sync.dma_start(out=bias_last[:], in_=bias_view[:, N_TILES - 1, :])
+        nc.sync.dma_start(out=bias_second[:], in_=bias_view[:, 0 : N_TILES - 1, 1:2])
+        load_scales(1, E * PASSES - PLANES)
         nc.sync.dma_start(out=w_second[:].bitcast(I32), in_=w_view[1].bitcast(I32))
 
-        def slots(e):
-            return (0, S) if e is None else (e * C, (e + 1) * C)
+        def entries(e):
+            return offsets[:, e * C // PER_COL : (e + 1) * C // PER_COL]
 
-        def gather(target, a, t, e, weights):
-            lo, hi = slots(e)
-            nc.vector.tensor_tensor(target, x_rows[a][t][:].indirect(offsets[:, lo // PER_COL : hi // PER_COL]), weights, MULT)
+        def gather(target, a, t, listed, weights):
+            nc.vector.tensor_tensor(target, x_rows[a][t][:].indirect(listed), weights, MULT)
 
-        def weave(grouped, source):
-            nc.scalar.copy(grouped, source.rearrange("p t j -> p j t"))
+        def weave(target, source):
+            nc.scalar.copy(target, source.rearrange("k t j -> k j t"))
 
         quantised = {}
 
-        def quantise(members, grouped, tag):
+        def quantise(members, woven, tag):
             name = "%d%d" % members[0]
-            codes = sb.tile([P, len(members) * C], U32, name="codes" + name, tag=tag or "codes" + name, align_bytes=64)
+            codes = sb.tile([P, len(members) * C], U32, name="codes" + name, tag=tag, align_bytes=64)
             plane = sb.tile([P, len(members) * C], U8, name="plane" + name, align_bytes=64)
-            nc.vector.quantize_mx(out=codes[:].bitcast(FP8X4), scales=plane[:], in_=grouped)
+            nc.vector.quantize_mx(out=codes[:].bitcast(FP8X4), scales=plane[:], in_=woven)
             for i, member in enumerate(members):
                 quantised[member] = (codes[:, i * C : (i + 1) * C], plane[:, i * C : (i + 1) * C])
 
@@ -112,11 +117,11 @@ def tile_moe_pre_lin_relu_kernel(tc, xT, w_words, w_scales, b, gate, offs, out):
         def multiply(e, n, passes, first, last):
             for a in passes:
                 codes, plane = quantised[(a, e)]
-                g, k = divmod(e * PASSES + a, 4)
+                g, i = divmod(e * PASSES + a, PLANES)
                 nc.tensor.matmul_mx(
                     out=acc[e][n][:],
                     lhsT=weights_of(e, a, n).bitcast(FP8X4),
-                    lhsT_scale=planes[4 * k :, g, n * P : (n + 1) * P],
+                    lhsT_scale=w_planes[4 * i :, g, n * P : (n + 1) * P],
                     rhs=codes.bitcast(FP8X4),
                     rhs_scale=plane,
                     start=(a == first),
@@ -125,17 +130,12 @@ def tile_moe_pre_lin_relu_kernel(tc, xT, w_words, w_scales, b, gate, offs, out):
 
         ys = {}
 
-        def activate(e, n, column, offset=None):
-            if offset is None:
-                y = sb.tile([P, C], F32, name="y%d_%d" % (e, n))
-            else:
-                y = reused.tile([P, C], F32, name="y%d_%d" % (e, n), offset=offset, align_bytes=64)
+        def activate(y, e, n, column):
             nc.scalar.activation(y[:], acc[e][n][:], RELU, bias=column)
             ys[(e, n)] = y
 
         def scatter(e, n):
-            lo, hi = slots(e)
-            nc.vector.tensor_copy(result[n][:].indirect(offsets[:, lo // PER_COL : hi // PER_COL]), ys[(e, n)][:])
+            nc.vector.tensor_copy(result[n][:].indirect(entries(e)), ys[(e, n)][:])
 
         picked = [sb.tile([P, P, GROUPS], F32, name="picked%d" % t) for t in range(2)]
         for t in range(2):
@@ -144,10 +144,10 @@ def tile_moe_pre_lin_relu_kernel(tc, xT, w_words, w_scales, b, gate, offs, out):
         spread = psum.tile([P, GROUPS, P], F32, name="spread", tag="acc1_0")
         for g in range(GROUPS):
             nc.tensor.transpose(spread[:, g, :], gate_cols[:, g : g + 1].to_broadcast([P, P]), identity[:])
-        nc.scalar.copy(gate_sb[:].rearrange("k (p g) -> k p g", g=GROUPS), spread[:].rearrange("k g p -> k p g"))
+        nc.scalar.copy(gate_rows[:].rearrange("k (p g) -> k p g", g=GROUPS), spread[:].rearrange("k g p -> k p g"))
 
-        grouped = sb.tile([P, 3, C, PACK], BF16, name="grouped", align_bytes=64)
-        pass0 = grouped[:, 1:3]
+        woven = sb.tile([P, 3, C, PACK], BF16, name="woven", align_bytes=64)
+        woven0 = woven[:, 1:3]
         back = [psum.tile([P, 2, 2, P], F32, name="back%d" % h) for h in range(2)]
         for t in range(2):
             by_slot = psum.tile([P, GROUPS, P], F32, name="by_slot%d" % t, tag="acc1_%d" % (t + 1))
@@ -159,59 +159,63 @@ def tile_moe_pre_lin_relu_kernel(tc, xT, w_words, w_scales, b, gate, offs, out):
             for g in range(GROUPS):
                 nc.tensor.transpose(back[g // 2][:, t, g % 2, :], scaled[:, g, :], identity[:])
         for h in range(2):
-            target = pass0[:, :, :, 0:2].rearrange("k e (p g) t -> k (e p) g t", g=GROUPS)[:, :, 2 * h : 2 * h + 2, :]
+            target = woven0[:, :, :, 0:2].rearrange("k e (p g) t -> k (e p) g t", g=GROUPS)[:, :, 2 * h : 2 * h + 2, :]
             nc.scalar.copy(target, back[h][:].rearrange("k t g p -> k p g t"))
         acc = [[psum.tile([P, C], F32, name="acc%d_%d" % (e, n)) for n in range(N_TILES)] for e in range(E)]
 
         pair0 = sb.tile([P, 2, S], F32, name="pair0", align_bytes=64)
         for i in range(2):
-            gather(pair0[:, i, :], 0, 2 + i, None, gate_sb[:])
-        weave(pass0[:, :, :, 2:4].rearrange("k e j t -> k (e j) t"), pair0[:])
-
+            gather(pair0[:, i, :], 0, 2 + i, offsets[:], gate_rows[:])
+        weave(woven0[:, :, :, 2:4].rearrange("k e j t -> k (e j) t"), pair0[:])
         gated1 = sb.tile([P, PACK, S], F32, name="gated1")
         for t in range(PACK):
-            gather(gated1[:, t, :], 1, t, None, gate_sb[:])
-        weave(grouped[:, 0], gated1[:, :, 0:C])
+            gather(gated1[:, t, :], 1, t, offsets[:], gate_rows[:])
+        weave(woven[:, 0], gated1[:, :, 0:C])
 
-        grouped20 = sb.tile([P, C, PACK], BF16, name="grouped20", tag="pair0", align_bytes=64)
-        pairs = [sb.tile([P, 2, C], F32, name="pair20_0"), reused.tile([P, 2, C], F32, name="pair20_1", offset=1024, align_bytes=64)]
-        for u in range(2):
+        woven20 = sb.tile([P, C, PACK], BF16, name="woven20", tag="pair0", align_bytes=64)
+        lower20 = sb.tile([P, 2, C], F32, name="lower20")
+        upper20 = placed.tile([P, 2, C], F32, name="upper20", offset=PAIR_BYTES // 2, align_bytes=64)
+        for u, pair in enumerate((lower20, upper20)):
             for i in range(2):
-                gather(pairs[u][:, i, :], 2, 2 * u + i, 0, gate_sb[:, 0:C])
-            weave(grouped20[:, :, 2 * u : 2 * u + 2], pairs[u][:])
-        grouped11 = reused.tile([P, C, PACK], BF16, name="grouped11", offset=0, align_bytes=64)
-        weave(grouped11[:], gated1[:, :, C:S])
+                gather(pair[:, i, :], LAST, 2 * u + i, entries(0), gate_rows[:, 0:C])
+            weave(woven20[:, :, 2 * u : 2 * u + 2], pair[:])
+        woven11 = placed.tile([P, C, PACK], BF16, name="woven11", offset=0, align_bytes=64)
+        weave(woven11[:], gated1[:, :, C:S])
 
-        low = sb.tile([P, 2, C], F32, name="pair21_0")
+        lower21 = sb.tile([P, 2, C], F32, name="lower21")
         for i in range(2):
-            gather(low[:, i, :], 2, i, 1, gate_late[:])
-        quantise([(1, 0), (0, 0)], grouped[:, 0:2].rearrange("k a j t -> k (a j t)"), "x_rows2_0")
-        multiply(0, 0, [0, 1], 0, 2)
-        quantise([(2, 0)], grouped20[:].rearrange("k j t -> k (j t)"), None)
-        multiply(0, 0, [2], 0, 2)
+            gather(lower21[:, i, :], LAST, i, entries(1), gate_late[:])
+        quantise([(1, 0), (0, 0)], woven[:, 0:2].rearrange("k m j t -> k (m j t)"), "x_rows2_0")
+        multiply(0, 0, [0, 1], 0, LAST)
+        quantise([(LAST, 0)], woven20[:].rearrange("k j t -> k (j t)"), "codes20")
+        multiply(0, 0, [LAST], 0, LAST)
         for n in range(1, N_TILES):
-            multiply(0, n, [2, 0, 1], 2, 1)
-        for n in range(2):
-            activate(0, n, bias_first[:, n, 0:1])
-        high = reused.tile([P, 2, C], F32, name="pair21_1", offset=2048, align_bytes=64)
+            multiply(0, n, [LAST, 0, 1], LAST, 1)
+        for n in range(N_TILES - 1):
+            activate(sb.tile([P, C], F32, name="y0_%d" % n), 0, n, bias_first[:, n, :])
+
+        upper21 = placed.tile([P, 2, C], F32, name="upper21", offset=PAIR_BYTES, align_bytes=64)
         for i in range(2):
-            gather(high[:, i, :], 2, 2 + i, 1, gate_late[:])
-        quantise([(0, 1)], grouped[:, 2].rearrange("k j t -> k (j t)"), "x_rows2_2")
-        quantise([(1, 1)], grouped11[:].rearrange("k j t -> k (j t)"), None)
+            gather(upper21[:, i, :], LAST, 2 + i, entries(1), gate_late[:])
+        quantise([(0, 1)], woven[:, 2].rearrange("k j t -> k (j t)"), "x_rows2_2")
+        quantise([(1, 1)], woven11[:].rearrange("k j t -> k (j t)"), "codes11")
         for n in range(N_TILES):
-            multiply(1, n, [0, 1], 0, 2)
-        grouped21 = sb.tile([P, C, PACK], BF16, name="grouped21", tag="share_a", align_bytes=64)
-        weave(grouped21[:, :, 0:2], low[:])
-        weave(grouped21[:, :, 2:4], high[:])
-        activate(0, 2, bias[:, 2, 0:1], 3072)
-        scatter(0, 0)
-        scatter(0, 1)
-        quantise([(2, 1)], grouped21[:].rearrange("k j t -> k (j t)"), None)
+            multiply(1, n, [0, 1], 0, LAST)
+
+        woven21 = sb.tile([P, C, PACK], BF16, name="woven21", tag="bias_first", align_bytes=64)
+        weave(woven21[:, :, 0:2], lower21[:])
+        weave(woven21[:, :, 2:4], upper21[:])
+        y_third = placed.tile([P, C], F32, name="y_third", offset=PAIR_BYTES + PAIR_BYTES // 2, align_bytes=64)
+        activate(y_third, 0, N_TILES - 1, bias_last[:, 0:1])
+        for n in range(N_TILES - 1):
+            scatter(0, n)
+        quantise([(LAST, 1)], woven21[:].rearrange("k j t -> k (j t)"), "codes21")
         for n in range(N_TILES):
-            multiply(1, n, [2], 0, 2)
+            multiply(1, n, [LAST], 0, LAST)
         for n in range(N_TILES):
-            activate(1, n, bias[:, n, 1:2])
-        scatter(0, 2)
+            column = bias_second[:, n, :] if n < N_TILES - 1 else bias_last[:, 1:2]
+            activate(sb.tile([P, C], F32, name="y1_%d" % n), 1, n, column)
+        scatter(0, N_TILES - 1)
         for n in range(N_TILES):
             scatter(1, n)
             nc.sync.dma_start(out=out[n * P : (n + 1) * P, :], in_=result[n][:])

@@ -54,7 +54,8 @@ def tile_moe_pre_lin_relu_kernel(tc, xT, w_words, w_scales, b, gate, offs, out):
         make_identity(nc, identity[:])
 
         nc.vector.memset(w_planes[:].rearrange("p g n -> p (g n)").bitcast(I32), 0)
-        nc.vector.memset(result[0][:], 0.0)
+        for n in range(N_TILES):
+            nc.vector.memset(result[n][:], 0.0)
 
         x_view = xT.rearrange("(a p t) j -> a t p j", p=P, t=PACK)
         scale_view = w_scales.rearrange("e a (q r) n -> q (e a) r n", r=4)
@@ -71,9 +72,7 @@ def tile_moe_pre_lin_relu_kernel(tc, xT, w_words, w_scales, b, gate, offs, out):
 
         load_x(0, 0)
         nc.sync.dma_start(offsets[:], offs)
-        nc.scalar.dma_start(out=gate_cols[:], in_=gate[0, :].rearrange("(p g) -> p g", g=GROUPS))
-        for n in range(1, N_TILES):
-            nc.scalar.copy(result[n][:], result[0][:])
+        nc.sync.dma_start(out=gate_cols[:], in_=gate[0, :].rearrange("(p g) -> p g", g=GROUPS))
         for a in range(PASSES):
             for t in range(PACK):
                 if (a, t) != (0, 0):
@@ -96,6 +95,9 @@ def tile_moe_pre_lin_relu_kernel(tc, xT, w_words, w_scales, b, gate, offs, out):
 
         def weave(target, source):
             nc.scalar.copy(target, source.rearrange("k t j -> k j t"))
+
+        def weave_whole(target, source):
+            nc.scalar.copy(target.rearrange("k (c i) t -> k c t i", i=4), source.rearrange("k t (c i) -> k c t i", i=4))
 
         quantised = {}
 
@@ -170,7 +172,7 @@ def tile_moe_pre_lin_relu_kernel(tc, xT, w_words, w_scales, b, gate, offs, out):
         gated1 = sb.tile([P, PACK, S], F32, name="gated1")
         for t in range(PACK):
             gather(gated1[:, t, :], 1, t, offsets[:], gate_rows[:])
-        weave(woven[:, 0], gated1[:, :, 0:C])
+        weave_whole(woven[:, 0], gated1[:, :, 0:C])
 
         woven20 = sb.tile([P, C, PACK], BF16, name="woven20", tag="pair0", align_bytes=64)
         lower20 = sb.tile([P, 2, C], F32, name="lower20")
@@ -180,7 +182,7 @@ def tile_moe_pre_lin_relu_kernel(tc, xT, w_words, w_scales, b, gate, offs, out):
                 gather(pair[:, i, :], LAST, 2 * u + i, entries(0), gate_rows[:, 0:C])
             weave(woven20[:, :, 2 * u : 2 * u + 2], pair[:])
         woven11 = placed.tile([P, C, PACK], BF16, name="woven11", offset=0, align_bytes=64)
-        weave(woven11[:], gated1[:, :, C:S])
+        weave_whole(woven11[:], gated1[:, :, C:S])
 
         lower21 = sb.tile([P, 2, C], F32, name="lower21")
         for i in range(2):

@@ -38,7 +38,7 @@ def tile_moe_pre_lin_relu_kernel(tc, xT, w_words, w_scales, b, gate, offs, out):
         psum = ctx.enter_context(tc.psum_pool(name="psum", bufs=1))
 
         offsets = sb.tile([P, S // PER_COL], U16, name="offsets")
-        gate_rows = sb.tile([P, S], F32, name="gate_rows")
+        gate_rows = sb.tile([P, S], F32, name="gate_rows", align_bytes=64)
         gate_late = sb.tile([P, C], F32, name="gate_late")
         x_rows = [[sb.tile([P, T], F32, name="x_rows%d_%d" % (a, t), align_bytes=64) for t in range(PACK)] for a in range(PASSES)]
         w_first = sb.tile([P, PASSES, P], U32, name="w_first", align_bytes=64)
@@ -175,20 +175,21 @@ def tile_moe_pre_lin_relu_kernel(tc, xT, w_words, w_scales, b, gate, offs, out):
         weave_whole(woven[:, 0], gated1[:, :, 0:C])
 
         woven20 = sb.tile([P, C, PACK], BF16, name="woven20", tag="pair0", align_bytes=64)
-        lower20 = sb.tile([P, 2, C], F32, name="lower20")
+        lower2 = sb.tile([P, 2, S], F32, name="lower2")
         upper20 = placed.tile([P, 2, C], F32, name="upper20", offset=PAIR_BYTES // 2, align_bytes=64)
-        for u, pair in enumerate((lower20, upper20)):
-            for i in range(2):
-                gather(pair[:, i, :], LAST, 2 * u + i, entries(0), gate_rows[:, 0:C])
-            weave(woven20[:, :, 2 * u : 2 * u + 2], pair[:])
+        gather(lower2[:, 0, :], LAST, 0, offsets[:], gate_rows[:])
+        gather(lower2[:, 1, 0:C], LAST, 1, entries(0), gate_rows[:, 0:C])
+        weave(woven20[:, :, 0:2], lower2[:, :, 0:C])
+        for i in range(2):
+            gather(upper20[:, i, :], LAST, 2 + i, entries(0), gate_rows[:, 0:C])
+        weave(woven20[:, :, 2:4], upper20[:])
         woven11 = placed.tile([P, C, PACK], BF16, name="woven11", offset=0, align_bytes=64)
         weave_whole(woven11[:], gated1[:, :, C:S])
 
-        lower21 = sb.tile([P, 2, C], F32, name="lower21")
-        for i in range(2):
-            gather(lower21[:, i, :], LAST, i, entries(1), gate_late[:])
-        quantise([(1, 0), (0, 0)], woven[:, 0:2].rearrange("k m j t -> k (m j t)"), "x_rows2_0")
+        gather(lower2[:, 1, C:S], LAST, 1, entries(1), gate_late[:])
+        quantise([(1, 0), (0, 0)], woven[:, 0:2].rearrange("k m j t -> k (m j t)"), "gate_rows")
         multiply(0, 0, [0, 1], 0, LAST)
+        quantise([(0, 1)], woven[:, 2].rearrange("k j t -> k (j t)"), "x_rows2_1")
         quantise([(LAST, 0)], woven20[:].rearrange("k j t -> k (j t)"), "codes20")
         multiply(0, 0, [LAST], 0, LAST)
         for n in range(1, N_TILES):
@@ -199,13 +200,12 @@ def tile_moe_pre_lin_relu_kernel(tc, xT, w_words, w_scales, b, gate, offs, out):
         upper21 = placed.tile([P, 2, C], F32, name="upper21", offset=PAIR_BYTES, align_bytes=64)
         for i in range(2):
             gather(upper21[:, i, :], LAST, 2 + i, entries(1), gate_late[:])
-        quantise([(0, 1)], woven[:, 2].rearrange("k j t -> k (j t)"), "x_rows2_2")
         quantise([(1, 1)], woven11[:].rearrange("k j t -> k (j t)"), "codes11")
         for n in range(N_TILES):
             multiply(1, n, [0, 1], 0, LAST)
 
         woven21 = sb.tile([P, C, PACK], BF16, name="woven21", tag="bias_first", align_bytes=64)
-        weave(woven21[:, :, 0:2], lower21[:])
+        weave(woven21[:, :, 0:2], lower2[:, :, C:S])
         weave(woven21[:, :, 2:4], upper21[:])
         y_third = placed.tile([P, C], F32, name="y_third", offset=PAIR_BYTES + PAIR_BYTES // 2, align_bytes=64)
         activate(y_third, 0, N_TILES - 1, bias_last[:, 0:1])
@@ -214,10 +214,10 @@ def tile_moe_pre_lin_relu_kernel(tc, xT, w_words, w_scales, b, gate, offs, out):
         quantise([(LAST, 1)], woven21[:].rearrange("k j t -> k (j t)"), "codes21")
         for n in range(N_TILES):
             multiply(1, n, [LAST], 0, LAST)
+        scatter(0, N_TILES - 1)
         for n in range(N_TILES):
             column = bias_second[:, n, :] if n < N_TILES - 1 else bias_last[:, 1:2]
-            activate(sb.tile([P, C], F32, name="y1_%d" % n), 1, n, column)
-        scatter(0, N_TILES - 1)
+            activate(ys[(0, n)], 1, n, column)
         for n in range(N_TILES):
             scatter(1, n)
             nc.sync.dma_start(out=out[n * P : (n + 1) * P, :], in_=result[n][:])

@@ -13,7 +13,7 @@ N_TILES = N // P
 PER_COL = 16
 GROUPS = S // P
 PLANES = 4
-PAIR_BYTES = 2 * C * 4
+LINE = 4
 
 F32 = mybir.dt.float32
 BF16 = mybir.dt.bfloat16
@@ -23,6 +23,8 @@ U16 = mybir.dt.uint16
 U8 = mybir.dt.uint8
 FP8X4 = mybir.dt.float8_e4m3fn_x4
 MULT = mybir.AluOpType.mult
+ADD = mybir.AluOpType.add
+MAX = mybir.AluOpType.max
 RELU = mybir.ActivationFunctionType.Relu
 COPY = mybir.ActivationFunctionType.Copy
 
@@ -34,80 +36,74 @@ def tile_moe_pre_lin_relu_kernel(tc, xT, w_words, w_scales, b, gate, offs, out):
     nc = tc.nc
     with ExitStack() as ctx:
         sb = ctx.enter_context(tc.tile_pool(name="sb", bufs=1))
-        placed = ctx.enter_context(tc.tile_pool(name="placed", bufs=1))
         psum = ctx.enter_context(tc.psum_pool(name="psum", bufs=1))
 
         offsets = sb.tile([P, S // PER_COL], U16, name="offsets")
-        gate_rows = sb.tile([P, S], F32, name="gate_rows", align_bytes=64)
-        gate_late = sb.tile([P, C], F32, name="gate_late")
-        x_rows = [[sb.tile([P, T], F32, name="x_rows%d_%d" % (a, t), align_bytes=64) for t in range(PACK)] for a in range(PASSES)]
+        x_rows = [[sb.tile([P, T], F32, name="x_rows%d_%d" % (a, t), align_bytes=64) for t in range(PACK) if (a, t) != (LAST, PACK - 1)] for a in range(PASSES)]
+        x_last = sb.tile([P, PACK * C], F32, name="x_last", align_bytes=64)
         w_first = sb.tile([P, PASSES, P], U32, name="w_first", align_bytes=64)
         w_rest = sb.tile([P, PASSES, N - P], U32, name="w_rest", align_bytes=64)
         w_second = sb.tile([P, PASSES, N], U32, name="w_second", align_bytes=64)
         w_planes = sb.tile([P, 2, N], U8, name="w_planes", align_bytes=64)
         gate_cols = sb.tile([P, GROUPS], F32, name="gate_cols")
         identity = sb.tile([P, P], F32, name="identity")
-        bias_first = sb.tile([P, N_TILES - 1, 1], F32, name="bias_first", align_bytes=64)
-        bias_second = sb.tile([P, N_TILES - 1, 1], F32, name="bias_second")
-        bias_last = sb.tile([P, E], F32, name="bias_last")
+        bias = sb.tile([P, N_TILES, E], F32, name="bias")
         result = [sb.tile([P, T], F32, name="result%d" % n) for n in range(N_TILES)]
         make_identity(nc, identity[:])
 
         nc.vector.memset(w_planes[:].rearrange("p g n -> p (g n)").bitcast(I32), 0)
-        for n in range(N_TILES):
+        for n in range(N_TILES - 1):
             nc.vector.memset(result[n][:], 0.0)
+        nc.scalar.activation(result[N_TILES - 1][:], result[0][:], COPY)
 
         x_view = xT.rearrange("(a p t) j -> a t p j", p=P, t=PACK)
         scale_view = w_scales.rearrange("e a (q r) n -> q (e a) r n", r=4)
         w_view = w_words.rearrange("e a p n t -> e p a (n t)")
-        bias_view = b.rearrange("(n p) e -> p n e", p=P)
-
-        def load_x(a, t):
-            nc.sync.dma_start(out=x_rows[a][t][:], in_=x_view[a, t])
 
         def load_scales(g, count):
             for q in range(4):
                 source = scale_view[q, PLANES * g : PLANES * g + count]
                 nc.sync.dma_start(out=w_planes[32 * q : 32 * q + 4 * count, g, :].bitcast(I32), in_=source.bitcast(I32))
 
-        load_x(0, 0)
+        nc.sync.dma_start(out=x_rows[0][0][:], in_=x_view[0, 0])
         nc.sync.dma_start(offsets[:], offs)
         nc.sync.dma_start(out=gate_cols[:], in_=gate[0, :].rearrange("(p g) -> p g", g=GROUPS))
-        for a in range(PASSES):
+        for a in range(LAST):
             for t in range(PACK):
                 if (a, t) != (0, 0):
-                    load_x(a, t)
-        nc.sync.dma_start(out=gate_late[:], in_=gate[P : 2 * P, C:S])
+                    nc.sync.dma_start(out=x_rows[a][t][:], in_=x_view[a, t])
+        for t in range(PACK - 1):
+            nc.sync.dma_start(out=x_rows[LAST][t][:], in_=x_view[LAST, t])
+        nc.sync.dma_start(out=x_last[:, 0:T], in_=x_view[LAST, PACK - 1])
         load_scales(0, PLANES)
         nc.sync.dma_start(out=w_first[:].bitcast(I32), in_=w_view[0, :, :, 0 : PACK * P].bitcast(I32))
+        nc.sync.dma_start(out=bias[:], in_=b.rearrange("(n p) e -> p n e", p=P))
         nc.sync.dma_start(out=w_rest[:].bitcast(I32), in_=w_view[0, :, :, PACK * P : PACK * N].bitcast(I32))
-        nc.sync.dma_start(out=bias_first[:], in_=bias_view[:, 0 : N_TILES - 1, 0:1])
-        nc.sync.dma_start(out=bias_last[:], in_=bias_view[:, N_TILES - 1, :])
-        nc.sync.dma_start(out=bias_second[:], in_=bias_view[:, 0 : N_TILES - 1, 1:2])
         load_scales(1, E * PASSES - PLANES)
         nc.sync.dma_start(out=w_second[:].bitcast(I32), in_=w_view[1].bitcast(I32))
 
-        def entries(e):
-            return offsets[:, e * C // PER_COL : (e + 1) * C // PER_COL]
+        def entries(lo, hi):
+            return offsets[:, lo // PER_COL : hi // PER_COL]
 
-        def gather(target, a, t, listed, weights):
-            nc.vector.tensor_tensor(target, x_rows[a][t][:].indirect(listed), weights, MULT)
+        def by_lines(rows):
+            return rows.rearrange("k t (c i) -> k c t i", i=LINE)
 
-        def weave(target, source):
-            nc.scalar.copy(target, source.rearrange("k t j -> k j t"))
+        def woven_by_lines(woven):
+            return woven.rearrange("k (c i) t -> k c t i", i=LINE)
 
-        def weave_whole(target, source):
-            nc.scalar.copy(target.rearrange("k (c i) t -> k c t i", i=4), source.rearrange("k t (c i) -> k c t i", i=4))
+        def gate_and_weave(woven, rows, lo, hi):
+            weights = spread[:, :, lo // LINE : hi // LINE].rearrange("k i c -> k c i").unsqueeze(2)
+            nc.vector.tensor_tensor(woven_by_lines(woven), by_lines(rows), weights.to_broadcast([P, (hi - lo) // LINE, PACK, LINE]), MULT)
 
         quantised = {}
 
-        def quantise(members, woven, tag):
-            name = "%d%d" % members[0]
-            codes = sb.tile([P, len(members) * C], U32, name="codes" + name, tag=tag, align_bytes=64)
-            plane = sb.tile([P, len(members) * C], U8, name="plane" + name, align_bytes=64)
-            nc.vector.quantize_mx(out=codes[:].bitcast(FP8X4), scales=plane[:], in_=woven)
-            for i, member in enumerate(members):
-                quantised[member] = (codes[:, i * C : (i + 1) * C], plane[:, i * C : (i + 1) * C])
+        def quantise(a, experts, woven, tag=None):
+            name = "%d%d" % (a, experts[0])
+            codes = sb.tile([P, len(experts) * C], U32, name="codes" + name, tag=tag or "codes" + name, align_bytes=64)
+            plane = sb.tile([P, len(experts) * C], U8, name="plane" + name, align_bytes=64)
+            nc.vector.quantize_mx(out=codes[:].bitcast(FP8X4), scales=plane[:], in_=woven.rearrange("k j t -> k (j t)"))
+            for i, e in enumerate(experts):
+                quantised[(a, e)] = (codes[:, i * C : (i + 1) * C], plane[:, i * C : (i + 1) * C])
 
         def weights_of(e, a, n):
             if e == 1:
@@ -116,108 +112,104 @@ def tile_moe_pre_lin_relu_kernel(tc, xT, w_words, w_scales, b, gate, offs, out):
                 return w_first[:, a, :]
             return w_rest[:, a, (n - 1) * P : n * P]
 
-        def multiply(e, n, passes, first, last):
-            for a in passes:
-                codes, plane = quantised[(a, e)]
-                g, i = divmod(e * PASSES + a, PLANES)
-                nc.tensor.matmul_mx(
-                    out=acc[e][n][:],
-                    lhsT=weights_of(e, a, n).bitcast(FP8X4),
-                    lhsT_scale=w_planes[4 * i :, g, n * P : (n + 1) * P],
-                    rhs=codes.bitcast(FP8X4),
-                    rhs_scale=plane,
-                    start=(a == first),
-                    stop=(a == last),
-                )
-
-        ys = {}
-
-        def activate(y, e, n, column):
-            nc.scalar.activation(y[:], acc[e][n][:], RELU, bias=column)
-            ys[(e, n)] = y
-
-        def scatter(e, n):
-            nc.vector.tensor_copy(result[n][:].indirect(entries(e)), ys[(e, n)][:])
-
-        picked = [sb.tile([P, P, GROUPS], F32, name="picked%d" % t) for t in range(2)]
-        for t in range(2):
-            nc.vector.tensor_copy(picked[t][:].rearrange("k p g -> k (p g)"), x_rows[0][t][:].indirect(offsets[:]))
-
-        spread = psum.tile([P, GROUPS, P], F32, name="spread", tag="acc1_0")
-        for g in range(GROUPS):
-            nc.tensor.transpose(spread[:, g, :], gate_cols[:, g : g + 1].to_broadcast([P, P]), identity[:])
-        nc.scalar.copy(gate_rows[:].rearrange("k (p g) -> k p g", g=GROUPS), spread[:].rearrange("k g p -> k p g"))
-
-        woven = sb.tile([P, 3, C, PACK], BF16, name="woven", align_bytes=64)
-        woven0 = woven[:, 1:3]
-        back = [psum.tile([P, 2, 2, P], F32, name="back%d" % h) for h in range(2)]
-        for t in range(2):
-            by_slot = psum.tile([P, GROUPS, P], F32, name="by_slot%d" % t, tag="acc1_%d" % (t + 1))
-            scaled = sb.tile([P, GROUPS, P], F32, name="scaled%d" % t)
-            for g in range(GROUPS):
-                nc.tensor.transpose(by_slot[:, g, :], picked[t][:, :, g], identity[:])
-            for g in range(GROUPS):
-                nc.scalar.activation(scaled[:, g, :], by_slot[:, g, :], COPY, scale=gate_cols[:, g : g + 1])
-            for g in range(GROUPS):
-                nc.tensor.transpose(back[g // 2][:, t, g % 2, :], scaled[:, g, :], identity[:])
-        for h in range(2):
-            target = woven0[:, :, :, 0:2].rearrange("k e (p g) t -> k (e p) g t", g=GROUPS)[:, :, 2 * h : 2 * h + 2, :]
-            nc.scalar.copy(target, back[h][:].rearrange("k t g p -> k p g t"))
         acc = [[psum.tile([P, C], F32, name="acc%d_%d" % (e, n)) for n in range(N_TILES)] for e in range(E)]
 
-        pair0 = sb.tile([P, 2, S], F32, name="pair0", align_bytes=64)
-        for i in range(2):
-            gather(pair0[:, i, :], 0, 2 + i, offsets[:], gate_rows[:])
-        weave(woven0[:, :, :, 2:4].rearrange("k e j t -> k (e j) t"), pair0[:])
-        gated1 = sb.tile([P, PACK, S], F32, name="gated1")
+        def multiply(e, n, passes):
+            for a in passes:
+                one_pass(e, n, a, a == passes[0], a == passes[-1])
+
+        def one_pass(e, n, a, start, stop):
+            codes, plane = quantised[(a, e)]
+            g, i = divmod(e * PASSES + a, PLANES)
+            nc.tensor.matmul_mx(
+                out=acc[e][n][:],
+                lhsT=weights_of(e, a, n).bitcast(FP8X4),
+                lhsT_scale=w_planes[4 * i :, g, n * P : (n + 1) * P],
+                rhs=codes.bitcast(FP8X4),
+                rhs_scale=plane,
+                start=start,
+                stop=stop,
+            )
+
+        ys = [[sb.tile([P, C], F32, name="y%d_%d" % (e, n)) for n in range(N_TILES)] for e in range(E)]
+
+        def relu_scalar(e, n):
+            nc.scalar.activation(ys[e][n][:], acc[e][n][:], RELU, bias=bias[:, n, e : e + 1])
+
+        def relu_vector(e, n):
+            nc.vector.tensor_scalar(ys[e][n][:], acc[e][n][:], bias[:, n, e : e + 1], 0.0, ADD, MAX)
+
+        def scatter_scalar(e, n, lo, hi):
+            nc.scalar.activation(result[n][:].indirect(entries(e * C + lo, e * C + hi)), ys[e][n][:, lo:hi], COPY)
+
+        def scatter_vector(e, n, lo, hi):
+            nc.vector.tensor_copy(result[n][:].indirect(entries(e * C + lo, e * C + hi)), ys[e][n][:, lo:hi])
+
+        spread = psum.tile([P, GROUPS, P], F32, name="spread")
+        for g in range(GROUPS):
+            nc.tensor.transpose(spread[:, g, :], gate_cols[:, g : g + 1].to_broadcast([P, P]), identity[:])
+
+        woven0 = sb.tile([P, S, PACK], BF16, name="woven0", align_bytes=64)
+        rows00 = sb.tile([P, PACK, C], F32, name="rows00")
+        rows01 = sb.tile([P, PACK, C], F32, name="rows01")
         for t in range(PACK):
-            gather(gated1[:, t, :], 1, t, offsets[:], gate_rows[:])
-        weave_whole(woven[:, 0], gated1[:, :, 0:C])
+            nc.scalar.activation(rows00[:, t, :], x_rows[0][t][:].indirect(entries(0, C)), COPY)
+            nc.vector.tensor_copy(rows01[:, t, :], x_rows[0][t][:].indirect(entries(C, S)))
+        gate_and_weave(woven0[:, C:S], rows01[:], C, S)
+        gate_and_weave(woven0[:, 0:C], rows00[:], 0, C)
+        quantise(0, [0, 1], woven0[:])
 
-        woven20 = sb.tile([P, C, PACK], BF16, name="woven20", tag="pair0", align_bytes=64)
-        lower2 = sb.tile([P, 2, S], F32, name="lower2")
-        upper20 = placed.tile([P, 2, C], F32, name="upper20", offset=PAIR_BYTES // 2, align_bytes=64)
-        gather(lower2[:, 0, :], LAST, 0, offsets[:], gate_rows[:])
-        gather(lower2[:, 1, 0:C], LAST, 1, entries(0), gate_rows[:, 0:C])
-        weave(woven20[:, :, 0:2], lower2[:, :, 0:C])
-        for i in range(2):
-            gather(upper20[:, i, :], LAST, 2 + i, entries(0), gate_rows[:, 0:C])
-        weave(woven20[:, :, 2:4], upper20[:])
-        woven11 = placed.tile([P, C, PACK], BF16, name="woven11", offset=0, align_bytes=64)
-        weave_whole(woven11[:], gated1[:, :, C:S])
+        cut = 320
+        woven10 = sb.tile([P, C, PACK], BF16, name="woven10", align_bytes=64)
+        rows1s = sb.tile([P, PACK, cut], F32, name="rows1s")
+        rows1v = sb.tile([P, PACK, S - cut], F32, name="rows1v")
+        gate_share = sb.tile([P, S - cut], F32, name="gate_share", tag="rows01")
+        nc.vector.tensor_copy(gate_share[:].rearrange("k (c i) -> k c i", i=LINE), spread[:, :, cut // LINE :].rearrange("k i c -> k c i"))
+        for t in range(PACK):
+            nc.scalar.activation(rows1s[:, t, :], x_rows[1][t][:].indirect(entries(0, cut)), COPY)
+            nc.vector.tensor_tensor(rows1v[:, t, :], x_rows[1][t][:].indirect(entries(cut, S)), gate_share[:], MULT)
+        gate_and_weave(woven10[:], rows1s[:, :, 0:C], 0, C)
+        quantise(1, [0], woven10[:])
 
-        gather(lower2[:, 1, C:S], LAST, 1, entries(1), gate_late[:])
-        quantise([(1, 0), (0, 0)], woven[:, 0:2].rearrange("k m j t -> k (m j t)"), "gate_rows")
-        multiply(0, 0, [0, 1], 0, LAST)
-        quantise([(0, 1)], woven[:, 2].rearrange("k j t -> k (j t)"), "x_rows2_1")
-        quantise([(LAST, 0)], woven20[:].rearrange("k j t -> k (j t)"), "codes20")
-        multiply(0, 0, [LAST], 0, LAST)
+        rows20 = sb.tile([P, PACK, C], F32, name="rows20", align_bytes=64)
+        rows21 = x_last[:].rearrange("k (t j) -> k t j", t=PACK)
+        woven2 = [sb.tile([P, C, PACK], BF16, name="woven2%d" % e, align_bytes=64) for e in range(E)]
+        for t in range(PACK - 1):
+            nc.scalar.activation(rows20[:, t, :], x_rows[LAST][t][:].indirect(entries(0, C)), COPY)
+        nc.scalar.activation(rows20[:, PACK - 1, :], x_last[:, 0:T].indirect(entries(0, C)), COPY)
+        nc.scalar.activation(rows21[:, PACK - 1, :], x_last[:, 0:T].indirect(entries(C, S)), COPY)
+        gate_and_weave(woven2[0][:], rows20[:], 0, C)
+        quantise(LAST, [0], woven2[0][:])
+        multiply(0, 0, [0, 1, LAST])
         for n in range(1, N_TILES):
-            multiply(0, n, [LAST, 0, 1], LAST, 1)
-        for n in range(N_TILES - 1):
-            activate(sb.tile([P, C], F32, name="y0_%d" % n), 0, n, bias_first[:, n, :])
+            multiply(0, n, [LAST, 0, 1])
+        woven11 = sb.tile([P, C, PACK], BF16, name="woven11", tag="rows20", align_bytes=64)
+        gate_and_weave(woven11[:, 0 : cut - C], rows1s[:, :, C:cut], C, cut)
+        nc.vector.tensor_copy(woven_by_lines(woven11[:, cut - C :]), by_lines(rows1v[:]))
+        quantise(1, [1], woven11[:])
+        for t in range(PACK - 1):
+            nc.scalar.activation(rows21[:, t, :], x_rows[LAST][t][:].indirect(entries(C, S)), COPY)
+        gate_and_weave(woven2[1][:], rows21, C, S)
+        quantise(LAST, [1], woven2[1][:])
+        for n in (2, 1, 0):
+            multiply(1, n, [1, 0, LAST])
 
-        upper21 = placed.tile([P, 2, C], F32, name="upper21", offset=PAIR_BYTES, align_bytes=64)
-        for i in range(2):
-            gather(upper21[:, i, :], LAST, 2 + i, entries(1), gate_late[:])
-        quantise([(1, 1)], woven11[:].rearrange("k j t -> k (j t)"), "codes11")
-        for n in range(N_TILES):
-            multiply(1, n, [0, 1], 0, LAST)
-
-        woven21 = sb.tile([P, C, PACK], BF16, name="woven21", tag="bias_first", align_bytes=64)
-        weave(woven21[:, :, 0:2], lower2[:, :, C:S])
-        weave(woven21[:, :, 2:4], upper21[:])
-        y_third = placed.tile([P, C], F32, name="y_third", offset=PAIR_BYTES + PAIR_BYTES // 2, align_bytes=64)
-        activate(y_third, 0, N_TILES - 1, bias_last[:, 0:1])
-        for n in range(N_TILES - 1):
-            scatter(0, n)
-        quantise([(LAST, 1)], woven21[:].rearrange("k j t -> k (j t)"), "codes21")
-        for n in range(N_TILES):
-            multiply(1, n, [LAST], 0, LAST)
-        scatter(0, N_TILES - 1)
-        for n in range(N_TILES):
-            column = bias_second[:, n, :] if n < N_TILES - 1 else bias_last[:, 1:2]
-            activate(ys[(0, n)], 1, n, column)
-        for n in range(N_TILES):
-            scatter(1, n)
+        def store(n):
             nc.sync.dma_start(out=out[n * P : (n + 1) * P, :], in_=result[n][:])
+
+        relu_scalar(0, 0)
+        scatter_scalar(0, 0, 0, C)
+        relu_scalar(0, 1)
+        scatter_scalar(0, 1, 0, C)
+        relu_vector(0, 2)
+        scatter_vector(0, 2, 0, C)
+        relu_vector(1, 2)
+        scatter_vector(1, 2, 0, C)
+        store(2)
+        relu_scalar(1, 1)
+        scatter_scalar(1, 1, 0, C // 2)
+        scatter_vector(1, 1, C // 2, C)
+        store(1)
+        relu_scalar(1, 0)
+        scatter_scalar(1, 0, 0, C)
+        store(0)

@@ -41,9 +41,7 @@ def tile_moe_pre_lin_relu_kernel(tc, xT, w_words, w_scales, b, gate, offs, out):
         offsets = sb.tile([P, S // PER_COL], U16, name="offsets")
         x_rows = [[sb.tile([P, T], F32, name="x_rows%d_%d" % (a, t), align_bytes=64) for t in range(PACK) if (a, t) != (LAST, PACK - 1)] for a in range(PASSES)]
         x_last = sb.tile([P, PACK * C], F32, name="x_last", align_bytes=64)
-        w_first = sb.tile([P, PASSES, P], U32, name="w_first", align_bytes=64)
-        w_rest = sb.tile([P, PASSES, N - P], U32, name="w_rest", align_bytes=64)
-        w_second = sb.tile([P, PASSES, N], U32, name="w_second", align_bytes=64)
+        w_codes = [sb.tile([P, PASSES, N], U32, name="w_codes%d" % e, align_bytes=64) for e in range(E)]
         w_planes = sb.tile([P, 2, N], U8, name="w_planes", align_bytes=64)
         gate_cols = sb.tile([P, GROUPS], F32, name="gate_cols")
         identity = sb.tile([P, P], F32, name="identity")
@@ -76,11 +74,10 @@ def tile_moe_pre_lin_relu_kernel(tc, xT, w_words, w_scales, b, gate, offs, out):
             nc.sync.dma_start(out=x_rows[LAST][t][:], in_=x_view[LAST, t])
         nc.sync.dma_start(out=x_last[:, 0:T], in_=x_view[LAST, PACK - 1])
         load_scales(0, PLANES)
-        nc.sync.dma_start(out=w_first[:].bitcast(I32), in_=w_view[0, :, :, 0 : PACK * P].bitcast(I32))
+        nc.sync.dma_start(out=w_codes[0][:].bitcast(I32), in_=w_view[0].bitcast(I32))
         nc.sync.dma_start(out=bias[:], in_=b.rearrange("(n p) e -> p n e", p=P))
-        nc.sync.dma_start(out=w_rest[:].bitcast(I32), in_=w_view[0, :, :, PACK * P : PACK * N].bitcast(I32))
         load_scales(1, E * PASSES - PLANES)
-        nc.sync.dma_start(out=w_second[:].bitcast(I32), in_=w_view[1].bitcast(I32))
+        nc.sync.dma_start(out=w_codes[1][:].bitcast(I32), in_=w_view[1].bitcast(I32))
 
         def entries(lo, hi):
             return offsets[:, lo // PER_COL : hi // PER_COL]
@@ -105,25 +102,21 @@ def tile_moe_pre_lin_relu_kernel(tc, xT, w_words, w_scales, b, gate, offs, out):
             for i, e in enumerate(experts):
                 quantised[(a, e)] = (codes[:, i * C : (i + 1) * C], plane[:, i * C : (i + 1) * C])
 
-        def weights_of(e, a, n):
-            if e == 1:
-                return w_second[:, a, n * P : (n + 1) * P]
-            if n == 0:
-                return w_first[:, a, :]
-            return w_rest[:, a, (n - 1) * P : n * P]
-
         acc = [[psum.tile([P, C], F32, name="acc%d_%d" % (e, n)) for n in range(N_TILES)] for e in range(E)]
 
-        def multiply(e, n, passes):
-            for a in passes:
-                one_pass(e, n, a, a == passes[0], a == passes[-1])
+        def multiply(e, blocks):
+            for n in blocks:
+                one_pass(e, n, 1, True, False)
+                one_pass(e, n, 0, False, False)
+            for n in blocks:
+                one_pass(e, n, LAST, False, True)
 
         def one_pass(e, n, a, start, stop):
             codes, plane = quantised[(a, e)]
             g, i = divmod(e * PASSES + a, PLANES)
             nc.tensor.matmul_mx(
                 out=acc[e][n][:],
-                lhsT=weights_of(e, a, n).bitcast(FP8X4),
+                lhsT=w_codes[e][:, a, n * P : (n + 1) * P].bitcast(FP8X4),
                 lhsT_scale=w_planes[4 * i :, g, n * P : (n + 1) * P],
                 rhs=codes.bitcast(FP8X4),
                 rhs_scale=plane,
@@ -131,19 +124,19 @@ def tile_moe_pre_lin_relu_kernel(tc, xT, w_words, w_scales, b, gate, offs, out):
                 stop=stop,
             )
 
-        ys = [[sb.tile([P, C], F32, name="y%d_%d" % (e, n)) for n in range(N_TILES)] for e in range(E)]
+        ys = {(e, n): sb.tile([P, C], F32, name="y%d_%d" % (e, n)) for e in range(E) for n in range(N_TILES)}
 
         def relu_scalar(e, n):
-            nc.scalar.activation(ys[e][n][:], acc[e][n][:], RELU, bias=bias[:, n, e : e + 1])
+            nc.scalar.activation(ys[(e, n)][:], acc[e][n][:], RELU, bias=bias[:, n, e : e + 1])
 
         def relu_vector(e, n):
-            nc.vector.tensor_scalar(ys[e][n][:], acc[e][n][:], bias[:, n, e : e + 1], 0.0, ADD, MAX)
+            nc.vector.tensor_scalar(ys[(e, n)][:], acc[e][n][:], bias[:, n, e : e + 1], 0.0, ADD, MAX)
 
         def scatter_scalar(e, n, lo, hi):
-            nc.scalar.activation(result[n][:].indirect(entries(e * C + lo, e * C + hi)), ys[e][n][:, lo:hi], COPY)
+            nc.scalar.activation(result[n][:].indirect(entries(e * C + lo, e * C + hi)), ys[(e, n)][:, lo:hi], COPY)
 
         def scatter_vector(e, n, lo, hi):
-            nc.vector.tensor_copy(result[n][:].indirect(entries(e * C + lo, e * C + hi)), ys[e][n][:, lo:hi])
+            nc.vector.tensor_copy(result[n][:].indirect(entries(e * C + lo, e * C + hi)), ys[(e, n)][:, lo:hi])
 
         spread = psum.tile([P, GROUPS, P], F32, name="spread")
         for g in range(GROUPS):
@@ -159,57 +152,51 @@ def tile_moe_pre_lin_relu_kernel(tc, xT, w_words, w_scales, b, gate, offs, out):
         gate_and_weave(woven0[:, 0:C], rows00[:], 0, C)
         quantise(0, [0, 1], woven0[:])
 
-        cut = 320
-        woven10 = sb.tile([P, C, PACK], BF16, name="woven10", align_bytes=64)
-        rows1s = sb.tile([P, PACK, cut], F32, name="rows1s")
-        rows1v = sb.tile([P, PACK, S - cut], F32, name="rows1v")
-        gate_share = sb.tile([P, S - cut], F32, name="gate_share", tag="rows01")
-        nc.vector.tensor_copy(gate_share[:].rearrange("k (c i) -> k c i", i=LINE), spread[:, :, cut // LINE :].rearrange("k i c -> k c i"))
+        cut = 384
+        woven1 = sb.tile([P, S, PACK], BF16, name="woven1", align_bytes=64)
+        rows1 = sb.tile([P, PACK, S], F32, name="rows1")
         for t in range(PACK):
-            nc.scalar.activation(rows1s[:, t, :], x_rows[1][t][:].indirect(entries(0, cut)), COPY)
-            nc.vector.tensor_tensor(rows1v[:, t, :], x_rows[1][t][:].indirect(entries(cut, S)), gate_share[:], MULT)
-        gate_and_weave(woven10[:], rows1s[:, :, 0:C], 0, C)
-        quantise(1, [0], woven10[:])
+            nc.scalar.activation(rows1[:, t, 0:cut], x_rows[1][t][:].indirect(entries(0, cut)), COPY)
+            nc.vector.tensor_copy(rows1[:, t, cut:S], x_rows[1][t][:].indirect(entries(cut, S)))
+        gate_and_weave(woven1[:, 0:C], rows1[:, :, 0:C], 0, C)
+        gate_and_weave(woven1[:, C:S], rows1[:, :, C:S], C, S)
+        quantise(1, [0], woven1[:, 0:C])
 
         rows20 = sb.tile([P, PACK, C], F32, name="rows20", align_bytes=64)
         rows21 = x_last[:].rearrange("k (t j) -> k t j", t=PACK)
-        woven2 = [sb.tile([P, C, PACK], BF16, name="woven2%d" % e, align_bytes=64) for e in range(E)]
+        woven20 = sb.tile([P, C, PACK], BF16, name="woven20", align_bytes=64)
         for t in range(PACK - 1):
             nc.scalar.activation(rows20[:, t, :], x_rows[LAST][t][:].indirect(entries(0, C)), COPY)
         nc.scalar.activation(rows20[:, PACK - 1, :], x_last[:, 0:T].indirect(entries(0, C)), COPY)
         nc.scalar.activation(rows21[:, PACK - 1, :], x_last[:, 0:T].indirect(entries(C, S)), COPY)
-        gate_and_weave(woven2[0][:], rows20[:], 0, C)
-        quantise(LAST, [0], woven2[0][:])
-        multiply(0, 0, [0, 1, LAST])
-        for n in range(1, N_TILES):
-            multiply(0, n, [LAST, 0, 1])
-        woven11 = sb.tile([P, C, PACK], BF16, name="woven11", tag="rows20", align_bytes=64)
-        gate_and_weave(woven11[:, 0 : cut - C], rows1s[:, :, C:cut], C, cut)
-        nc.vector.tensor_copy(woven_by_lines(woven11[:, cut - C :]), by_lines(rows1v[:]))
-        quantise(1, [1], woven11[:])
+        gate_and_weave(woven20[:], rows20[:], 0, C)
+        quantise(LAST, [0], woven20[:])
+        multiply(0, [0, 1])
+        multiply(0, [2])
+        quantise(1, [1], woven1[:, C:S], "woven20")
         for t in range(PACK - 1):
             nc.scalar.activation(rows21[:, t, :], x_rows[LAST][t][:].indirect(entries(C, S)), COPY)
-        gate_and_weave(woven2[1][:], rows21, C, S)
-        quantise(LAST, [1], woven2[1][:])
-        for n in (2, 1, 0):
-            multiply(1, n, [1, 0, LAST])
 
         def store(n):
             nc.sync.dma_start(out=out[n * P : (n + 1) * P, :], in_=result[n][:])
 
-        relu_scalar(0, 0)
-        scatter_scalar(0, 0, 0, C)
-        relu_scalar(0, 1)
-        scatter_scalar(0, 1, 0, C)
+        woven21 = sb.tile([P, C, PACK], BF16, name="woven21", align_bytes=64)
+        gate_and_weave(woven21[:], rows21, C, S)
         relu_vector(0, 2)
+        quantise(LAST, [1], woven21[:])
+        multiply(1, [2, 1, 0])
+        relu_scalar(0, 0)
+        relu_scalar(0, 1)
+        scatter_scalar(0, 0, 0, C)
+        scatter_scalar(0, 1, 0, C)
         scatter_vector(0, 2, 0, C)
         relu_vector(1, 2)
+        relu_vector(1, 1)
         scatter_vector(1, 2, 0, C)
         store(2)
-        relu_scalar(1, 1)
-        scatter_scalar(1, 1, 0, C // 2)
-        scatter_vector(1, 1, C // 2, C)
-        store(1)
         relu_scalar(1, 0)
+        scatter_scalar(1, 1, 0, 160)
+        scatter_vector(1, 1, 160, C)
+        store(1)
         scatter_scalar(1, 0, 0, C)
         store(0)

@@ -41,7 +41,9 @@ def tile_moe_pre_lin_relu_kernel(tc, xT, w_words, w_scales, b, gate, offs, out):
         offsets = sb.tile([P, S // PER_COL], U16, name="offsets")
         x_rows = [[sb.tile([P, T], F32, name="x_rows%d_%d" % (a, t), align_bytes=64) for t in range(PACK) if (a, t) != (LAST, PACK - 1)] for a in range(PASSES)]
         x_last = sb.tile([P, PACK * C], F32, name="x_last", align_bytes=64)
-        w_codes = [sb.tile([P, PASSES, N], U32, name="w_codes%d" % e, align_bytes=64) for e in range(E)]
+        w_first = sb.tile([P, PASSES, 2 * P], U32, name="w_first", align_bytes=64)
+        w_third = sb.tile([P, PASSES, P], U32, name="w_third", align_bytes=64)
+        w_second = sb.tile([P, PASSES, N], U32, name="w_second", align_bytes=64)
         w_planes = sb.tile([P, 2, N], U8, name="w_planes", align_bytes=64)
         gate_cols = sb.tile([P, GROUPS], F32, name="gate_cols")
         identity = sb.tile([P, P], F32, name="identity")
@@ -74,10 +76,11 @@ def tile_moe_pre_lin_relu_kernel(tc, xT, w_words, w_scales, b, gate, offs, out):
             nc.sync.dma_start(out=x_rows[LAST][t][:], in_=x_view[LAST, t])
         nc.sync.dma_start(out=x_last[:, 0:T], in_=x_view[LAST, PACK - 1])
         load_scales(0, PLANES)
-        nc.sync.dma_start(out=w_codes[0][:].bitcast(I32), in_=w_view[0].bitcast(I32))
+        nc.sync.dma_start(out=w_first[:].bitcast(I32), in_=w_view[0, :, :, 0 : 2 * PACK * P].bitcast(I32))
+        nc.sync.dma_start(out=w_third[:].bitcast(I32), in_=w_view[0, :, :, 2 * PACK * P :].bitcast(I32))
         nc.sync.dma_start(out=bias[:], in_=b.rearrange("(n p) e -> p n e", p=P))
         load_scales(1, E * PASSES - PLANES)
-        nc.sync.dma_start(out=w_codes[1][:].bitcast(I32), in_=w_view[1].bitcast(I32))
+        nc.sync.dma_start(out=w_second[:].bitcast(I32), in_=w_view[1].bitcast(I32))
 
         def entries(lo, hi):
             return offsets[:, lo // PER_COL : hi // PER_COL]
@@ -106,17 +109,22 @@ def tile_moe_pre_lin_relu_kernel(tc, xT, w_words, w_scales, b, gate, offs, out):
 
         def multiply(e, blocks):
             for n in blocks:
-                one_pass(e, n, 1, True, False)
-                one_pass(e, n, 0, False, False)
+                one_pass(e, n, e, True, False)
+                one_pass(e, n, 1 - e, False, False)
             for n in blocks:
                 one_pass(e, n, LAST, False, True)
+
+        def weights_of(e, n, a):
+            if e == 1:
+                return w_second[:, a, n * P : (n + 1) * P]
+            return w_first[:, a, n * P : (n + 1) * P] if n < 2 else w_third[:, a, :]
 
         def one_pass(e, n, a, start, stop):
             codes, plane = quantised[(a, e)]
             g, i = divmod(e * PASSES + a, PLANES)
             nc.tensor.matmul_mx(
                 out=acc[e][n][:],
-                lhsT=w_codes[e][:, a, n * P : (n + 1) * P].bitcast(FP8X4),
+                lhsT=weights_of(e, n, a).bitcast(FP8X4),
                 lhsT_scale=w_planes[4 * i :, g, n * P : (n + 1) * P],
                 rhs=codes.bitcast(FP8X4),
                 rhs_scale=plane,
@@ -152,7 +160,7 @@ def tile_moe_pre_lin_relu_kernel(tc, xT, w_words, w_scales, b, gate, offs, out):
         gate_and_weave(woven0[:, 0:C], rows00[:], 0, C)
         quantise(0, [0, 1], woven0[:])
 
-        cut = 384
+        cut = 352
         woven1 = sb.tile([P, S, PACK], BF16, name="woven1", align_bytes=64)
         rows1 = sb.tile([P, PACK, S], F32, name="rows1")
         for t in range(PACK):
@@ -162,26 +170,28 @@ def tile_moe_pre_lin_relu_kernel(tc, xT, w_words, w_scales, b, gate, offs, out):
         gate_and_weave(woven1[:, C:S], rows1[:, :, C:S], C, S)
         quantise(1, [0], woven1[:, 0:C])
 
-        rows20 = sb.tile([P, PACK, C], F32, name="rows20", align_bytes=64)
-        rows21 = x_last[:].rearrange("k (t j) -> k t j", t=PACK)
+        wide = C + 64
+        rows20 = sb.tile([P, PACK, wide], F32, name="rows20", align_bytes=64)
+        rows21 = x_last[:].rearrange("k (t j) -> k t j", t=PACK)[:, :, 0 : S - wide]
         woven20 = sb.tile([P, C, PACK], BF16, name="woven20", align_bytes=64)
+        woven21 = sb.tile([P, C, PACK], BF16, name="woven21", align_bytes=64)
         for t in range(PACK - 1):
-            nc.scalar.activation(rows20[:, t, :], x_rows[LAST][t][:].indirect(entries(0, C)), COPY)
-        nc.scalar.activation(rows20[:, PACK - 1, :], x_last[:, 0:T].indirect(entries(0, C)), COPY)
-        nc.scalar.activation(rows21[:, PACK - 1, :], x_last[:, 0:T].indirect(entries(C, S)), COPY)
-        gate_and_weave(woven20[:], rows20[:], 0, C)
+            nc.scalar.activation(rows20[:, t, :], x_rows[LAST][t][:].indirect(entries(0, wide)), COPY)
+        nc.scalar.activation(rows20[:, PACK - 1, :], x_last[:, 0:T].indirect(entries(0, wide)), COPY)
+        nc.scalar.activation(rows21[:, PACK - 1, :], x_last[:, 0:T].indirect(entries(wide, S)), COPY)
+        gate_and_weave(woven20[:], rows20[:, :, 0:C], 0, C)
         quantise(LAST, [0], woven20[:])
         multiply(0, [0, 1])
         multiply(0, [2])
+        gate_and_weave(woven21[:, 0 : wide - C], rows20[:, :, C:wide], C, wide)
         quantise(1, [1], woven1[:, C:S], "woven20")
         for t in range(PACK - 1):
-            nc.scalar.activation(rows21[:, t, :], x_rows[LAST][t][:].indirect(entries(C, S)), COPY)
+            nc.scalar.activation(rows21[:, t, :], x_rows[LAST][t][:].indirect(entries(wide, S)), COPY)
 
         def store(n):
             nc.sync.dma_start(out=out[n * P : (n + 1) * P, :], in_=result[n][:])
 
-        woven21 = sb.tile([P, C, PACK], BF16, name="woven21", align_bytes=64)
-        gate_and_weave(woven21[:], rows21, C, S)
+        gate_and_weave(woven21[:, wide - C :], rows21, wide, S)
         relu_vector(0, 2)
         quantise(LAST, [1], woven21[:])
         multiply(1, [2, 1, 0])

@@ -92,7 +92,7 @@ def tile_moe_pre_lin_relu_kernel(tc, xT, w_words, w_scales, b, gate, offs, out):
             return woven.rearrange("k (c i) t -> k c t i", i=LINE)
 
         def gate_and_weave(woven, rows, lo, hi):
-            weights = spread[:, :, lo // LINE : hi // LINE].rearrange("k i c -> k c i").unsqueeze(2)
+            weights = spread[:, lo // LINE : hi // LINE, :].unsqueeze(2)
             nc.vector.tensor_tensor(woven_by_lines(woven), by_lines(rows), weights.to_broadcast([P, (hi - lo) // LINE, PACK, LINE]), MULT)
 
         quantised = {}
@@ -105,12 +105,13 @@ def tile_moe_pre_lin_relu_kernel(tc, xT, w_words, w_scales, b, gate, offs, out):
             for i, e in enumerate(experts):
                 quantised[(a, e)] = (codes[:, i * C : (i + 1) * C], plane[:, i * C : (i + 1) * C])
 
-        acc = [[psum.tile([P, C], F32, name="acc%d_%d" % (e, n)) for n in range(N_TILES)] for e in range(E)]
+        acc = {}
 
         def multiply(e, blocks):
             for n in blocks:
-                one_pass(e, n, e, True, False)
-                one_pass(e, n, 1 - e, False, False)
+                acc[(e, n)] = psum.tile([P, C], F32, name="acc%d_%d" % (e, n), tag="acc%d" % n)
+                one_pass(e, n, 0, True, False)
+                one_pass(e, n, 1, False, False)
             for n in blocks:
                 one_pass(e, n, LAST, False, True)
 
@@ -123,7 +124,7 @@ def tile_moe_pre_lin_relu_kernel(tc, xT, w_words, w_scales, b, gate, offs, out):
             codes, plane = quantised[(a, e)]
             g, i = divmod(e * PASSES + a, PLANES)
             nc.tensor.matmul_mx(
-                out=acc[e][n][:],
+                out=acc[(e, n)][:],
                 lhsT=weights_of(e, n, a).bitcast(FP8X4),
                 lhsT_scale=w_planes[4 * i :, g, n * P : (n + 1) * P],
                 rhs=codes.bitcast(FP8X4),
@@ -135,10 +136,10 @@ def tile_moe_pre_lin_relu_kernel(tc, xT, w_words, w_scales, b, gate, offs, out):
         ys = {(e, n): sb.tile([P, C], F32, name="y%d_%d" % (e, n)) for e in range(E) for n in range(N_TILES)}
 
         def relu_scalar(e, n):
-            nc.scalar.activation(ys[(e, n)][:], acc[e][n][:], RELU, bias=bias[:, n, e : e + 1])
+            nc.scalar.activation(ys[(e, n)][:], acc[(e, n)][:], RELU, bias=bias[:, n, e : e + 1])
 
         def relu_vector(e, n):
-            nc.vector.tensor_scalar(ys[(e, n)][:], acc[e][n][:], bias[:, n, e : e + 1], 0.0, ADD, MAX)
+            nc.vector.tensor_scalar(ys[(e, n)][:], acc[(e, n)][:], bias[:, n, e : e + 1], 0.0, ADD, MAX)
 
         def scatter_scalar(e, n, lo, hi):
             nc.scalar.activation(result[n][:].indirect(entries(e * C + lo, e * C + hi)), ys[(e, n)][:, lo:hi], COPY)
@@ -146,9 +147,9 @@ def tile_moe_pre_lin_relu_kernel(tc, xT, w_words, w_scales, b, gate, offs, out):
         def scatter_vector(e, n, lo, hi):
             nc.vector.tensor_copy(result[n][:].indirect(entries(e * C + lo, e * C + hi)), ys[(e, n)][:, lo:hi])
 
-        spread = psum.tile([P, GROUPS, P], F32, name="spread")
+        spread = psum.tile([P, P, GROUPS], F32, name="spread")
         for g in range(GROUPS):
-            nc.tensor.transpose(spread[:, g, :], gate_cols[:, g : g + 1].to_broadcast([P, P]), identity[:])
+            nc.tensor.transpose(spread[:, :, g], gate_cols[:, g : g + 1].to_broadcast([P, P]), identity[:])
 
         woven0 = sb.tile([P, S, PACK], BF16, name="woven0", align_bytes=64)
         rows00 = sb.tile([P, PACK, C], F32, name="rows00")
@@ -160,7 +161,7 @@ def tile_moe_pre_lin_relu_kernel(tc, xT, w_words, w_scales, b, gate, offs, out):
         gate_and_weave(woven0[:, 0:C], rows00[:], 0, C)
         quantise(0, [0, 1], woven0[:])
 
-        cut = 352
+        cut = 384
         woven1 = sb.tile([P, S, PACK], BF16, name="woven1", align_bytes=64)
         rows1 = sb.tile([P, PACK, S], F32, name="rows1")
         for t in range(PACK):
@@ -170,21 +171,22 @@ def tile_moe_pre_lin_relu_kernel(tc, xT, w_words, w_scales, b, gate, offs, out):
         gate_and_weave(woven1[:, C:S], rows1[:, :, C:S], C, S)
         quantise(1, [0], woven1[:, 0:C])
 
-        wide = C + 64
+        wide = C + 32
         rows20 = sb.tile([P, PACK, wide], F32, name="rows20", align_bytes=64)
         rows21 = x_last[:].rearrange("k (t j) -> k t j", t=PACK)[:, :, 0 : S - wide]
-        woven20 = sb.tile([P, C, PACK], BF16, name="woven20", align_bytes=64)
-        woven21 = sb.tile([P, C, PACK], BF16, name="woven21", align_bytes=64)
+        woven2 = sb.tile([P, wide, PACK], BF16, name="woven2", align_bytes=64)
+        woven20 = woven2[:, wide - C :]
+        woven21 = woven2[:, 0:C]
         for t in range(PACK - 1):
             nc.scalar.activation(rows20[:, t, :], x_rows[LAST][t][:].indirect(entries(0, wide)), COPY)
         nc.scalar.activation(rows20[:, PACK - 1, :], x_last[:, 0:T].indirect(entries(0, wide)), COPY)
         nc.scalar.activation(rows21[:, PACK - 1, :], x_last[:, 0:T].indirect(entries(wide, S)), COPY)
-        gate_and_weave(woven20[:], rows20[:, :, 0:C], 0, C)
-        quantise(LAST, [0], woven20[:])
+        gate_and_weave(woven20, rows20[:, :, 0:C], 0, C)
+        quantise(LAST, [0], woven20)
         multiply(0, [0, 1])
         multiply(0, [2])
         gate_and_weave(woven21[:, 0 : wide - C], rows20[:, :, C:wide], C, wide)
-        quantise(1, [1], woven1[:, C:S], "woven20")
+        quantise(1, [1], woven1[:, C:S], "rows20")
         for t in range(PACK - 1):
             nc.scalar.activation(rows21[:, t, :], x_rows[LAST][t][:].indirect(entries(wide, S)), COPY)
 
@@ -192,21 +194,22 @@ def tile_moe_pre_lin_relu_kernel(tc, xT, w_words, w_scales, b, gate, offs, out):
             nc.sync.dma_start(out=out[n * P : (n + 1) * P, :], in_=result[n][:])
 
         gate_and_weave(woven21[:, wide - C :], rows21, wide, S)
-        relu_vector(0, 2)
-        quantise(LAST, [1], woven21[:])
-        multiply(1, [2, 1, 0])
+        first = 96
         relu_scalar(0, 0)
         relu_scalar(0, 1)
+        relu_vector(0, 2)
+        quantise(LAST, [1], woven21)
+        multiply(1, [0, 1])
+        multiply(1, [2])
         scatter_scalar(0, 0, 0, C)
         scatter_scalar(0, 1, 0, C)
-        scatter_vector(0, 2, 0, C)
-        relu_vector(1, 2)
+        scatter_vector(0, 2, 0, first)
+        scatter_scalar(0, 2, first, C)
+        relu_vector(1, 0)
         relu_vector(1, 1)
-        scatter_vector(1, 2, 0, C)
+        for n in range(2):
+            scatter_vector(1, n, 0, C)
+            store(n)
+        relu_scalar(1, 2)
+        scatter_scalar(1, 2, 0, C)
         store(2)
-        relu_scalar(1, 0)
-        scatter_scalar(1, 1, 0, 160)
-        scatter_vector(1, 1, 160, C)
-        store(1)
-        scatter_scalar(1, 0, 0, C)
-        store(0)

@@ -157,21 +157,31 @@ def tile_moe_pre_lin_relu_kernel(tc, xT, w_words, w_scales, b, gate, offs, out):
         for t in range(PACK):
             nc.scalar.activation(rows00[:, t, :], x_rows[0][t][:].indirect(entries(0, C)), COPY)
             nc.vector.tensor_copy(rows01[:, t, :], x_rows[0][t][:].indirect(entries(C, S)))
-        gate_and_weave(woven0[:, C:S], rows01[:], C, S)
+        cut = 352
+        gate_tail = sb.tile([P, S - cut], F32, name="gate_tail")
+        nc.vector.tensor_copy(gate_tail[:], spread[:, cut // LINE :, :].rearrange("k c i -> k (c i)"))
+
+        def gate_and_weave_gpsimd(woven, rows, lo):
+            weights = gate_tail[:, lo - cut :].rearrange("k (c i) -> k c i", i=LINE).unsqueeze(2)
+            nc.gpsimd.tensor_tensor(woven_by_lines(woven), by_lines(rows), weights.to_broadcast([P, (S - lo) // LINE, PACK, LINE]), MULT)
+
+        gate_and_weave_gpsimd(woven0[:, cut:S], rows01[:, :, cut - C :], cut)
         gate_and_weave(woven0[:, 0:C], rows00[:], 0, C)
-        quantise(0, [0, 1], woven0[:])
+        gate_and_weave(woven0[:, C:cut], rows01[:, :, 0 : cut - C], C, cut)
 
-        cut = 384
         woven1 = sb.tile([P, S, PACK], BF16, name="woven1", align_bytes=64)
-        rows1 = sb.tile([P, PACK, S], F32, name="rows1")
+        rows1s = sb.tile([P, PACK, cut], F32, name="rows1s")
+        rows1v = sb.tile([P, PACK, S - cut], F32, name="rows1v", tag="rows00")
         for t in range(PACK):
-            nc.scalar.activation(rows1[:, t, 0:cut], x_rows[1][t][:].indirect(entries(0, cut)), COPY)
-            nc.vector.tensor_copy(rows1[:, t, cut:S], x_rows[1][t][:].indirect(entries(cut, S)))
-        gate_and_weave(woven1[:, 0:C], rows1[:, :, 0:C], 0, C)
-        gate_and_weave(woven1[:, C:S], rows1[:, :, C:S], C, S)
+            nc.scalar.activation(rows1s[:, t, :], x_rows[1][t][:].indirect(entries(0, cut)), COPY)
+            nc.vector.tensor_copy(rows1v[:, t, :], x_rows[1][t][:].indirect(entries(cut, S)))
+        quantise(0, [0, 1], woven0[:], "x_rows1_1")
+        gate_and_weave_gpsimd(woven1[:, cut:S], rows1v[:], cut)
+        gate_and_weave(woven1[:, 0:cut], rows1s[:], 0, cut)
         quantise(1, [0], woven1[:, 0:C])
+        quantise(1, [1], woven1[:, C:S])
 
-        wide = C + 32
+        wide = C + 64
         rows20 = sb.tile([P, PACK, wide], F32, name="rows20", align_bytes=64)
         rows21 = x_last[:].rearrange("k (t j) -> k t j", t=PACK)[:, :, 0 : S - wide]
         woven2 = sb.tile([P, wide, PACK], BF16, name="woven2", align_bytes=64)
@@ -186,7 +196,6 @@ def tile_moe_pre_lin_relu_kernel(tc, xT, w_words, w_scales, b, gate, offs, out):
         multiply(0, [0, 1])
         multiply(0, [2])
         gate_and_weave(woven21[:, 0 : wide - C], rows20[:, :, C:wide], C, wide)
-        quantise(1, [1], woven1[:, C:S], "rows20")
         for t in range(PACK - 1):
             nc.scalar.activation(rows21[:, t, :], x_rows[LAST][t][:].indirect(entries(wide, S)), COPY)
 

@@ -157,17 +157,17 @@ def tile_moe_pre_lin_relu_kernel(tc, xT, w_words, w_scales, b, gate, offs, out):
         for t in range(PACK):
             nc.scalar.activation(rows00[:, t, :], x_rows[0][t][:].indirect(entries(0, C)), COPY)
             nc.vector.tensor_copy(rows01[:, t, :], x_rows[0][t][:].indirect(entries(C, S)))
-        cut = 352
-        gate_tail = sb.tile([P, S - cut], F32, name="gate_tail")
-        nc.vector.tensor_copy(gate_tail[:], spread[:, cut // LINE :, :].rearrange("k c i -> k (c i)"))
+        cut, tail = 320, 352
+        gate_second = sb.tile([P, C], F32, name="gate_second")
+        nc.vector.tensor_copy(gate_second[:], spread[:, C // LINE :, :].rearrange("k c i -> k (c i)"))
 
-        def gate_and_weave_gpsimd(woven, rows, lo):
-            weights = gate_tail[:, lo - cut :].rearrange("k (c i) -> k c i", i=LINE).unsqueeze(2)
-            nc.gpsimd.tensor_tensor(woven_by_lines(woven), by_lines(rows), weights.to_broadcast([P, (S - lo) // LINE, PACK, LINE]), MULT)
+        def gate_and_weave_gpsimd(woven, rows, lo, hi):
+            weights = gate_second[:, lo - C : hi - C].rearrange("k (c i) -> k c i", i=LINE).unsqueeze(2)
+            nc.gpsimd.tensor_tensor(woven_by_lines(woven), by_lines(rows), weights.to_broadcast([P, (hi - lo) // LINE, PACK, LINE]), MULT)
 
-        gate_and_weave_gpsimd(woven0[:, cut:S], rows01[:, :, cut - C :], cut)
+        gate_and_weave_gpsimd(woven0[:, tail:S], rows01[:, :, tail - C :], tail, S)
         gate_and_weave(woven0[:, 0:C], rows00[:], 0, C)
-        gate_and_weave(woven0[:, C:cut], rows01[:, :, 0 : cut - C], C, cut)
+        gate_and_weave(woven0[:, C:tail], rows01[:, :, 0 : tail - C], C, tail)
 
         woven1 = sb.tile([P, S, PACK], BF16, name="woven1", align_bytes=64)
         rows1s = sb.tile([P, PACK, cut], F32, name="rows1s")
@@ -176,26 +176,30 @@ def tile_moe_pre_lin_relu_kernel(tc, xT, w_words, w_scales, b, gate, offs, out):
             nc.scalar.activation(rows1s[:, t, :], x_rows[1][t][:].indirect(entries(0, cut)), COPY)
             nc.vector.tensor_copy(rows1v[:, t, :], x_rows[1][t][:].indirect(entries(cut, S)))
         quantise(0, [0, 1], woven0[:], "x_rows1_1")
-        gate_and_weave_gpsimd(woven1[:, cut:S], rows1v[:], cut)
+        gate_and_weave_gpsimd(woven1[:, tail:S], rows1v[:, :, tail - cut :], tail, S)
+        gate_and_weave(woven1[:, cut:tail], rows1v[:, :, 0 : tail - cut], cut, tail)
         gate_and_weave(woven1[:, 0:cut], rows1s[:], 0, cut)
         quantise(1, [0], woven1[:, 0:C])
-        quantise(1, [1], woven1[:, C:S])
 
-        wide = C + 64
+        wide = C + 96
         rows20 = sb.tile([P, PACK, wide], F32, name="rows20", align_bytes=64)
         rows21 = x_last[:].rearrange("k (t j) -> k t j", t=PACK)[:, :, 0 : S - wide]
         woven2 = sb.tile([P, wide, PACK], BF16, name="woven2", align_bytes=64)
         woven20 = woven2[:, wide - C :]
         woven21 = woven2[:, 0:C]
-        for t in range(PACK - 1):
+        for t in range(2):
             nc.scalar.activation(rows20[:, t, :], x_rows[LAST][t][:].indirect(entries(0, wide)), COPY)
-        nc.scalar.activation(rows20[:, PACK - 1, :], x_last[:, 0:T].indirect(entries(0, wide)), COPY)
+        nc.scalar.activation(rows20[:, 2, 0:C], x_rows[LAST][2][:].indirect(entries(0, C)), COPY)
+        nc.vector.tensor_copy(rows20[:, 2, C:wide], x_rows[LAST][2][:].indirect(entries(C, wide)))
+        nc.scalar.activation(rows20[:, PACK - 1, 0:C], x_last[:, 0:T].indirect(entries(0, C)), COPY)
+        nc.vector.tensor_copy(rows20[:, PACK - 1, C:wide], x_last[:, 0:T].indirect(entries(C, wide)))
         nc.scalar.activation(rows21[:, PACK - 1, :], x_last[:, 0:T].indirect(entries(wide, S)), COPY)
         gate_and_weave(woven20, rows20[:, :, 0:C], 0, C)
         quantise(LAST, [0], woven20)
         multiply(0, [0, 1])
         multiply(0, [2])
-        gate_and_weave(woven21[:, 0 : wide - C], rows20[:, :, C:wide], C, wide)
+        gate_and_weave_gpsimd(woven21[:, 0 : wide - C], rows20[:, :, C:wide], C, wide)
+        quantise(1, [1], woven1[:, C:S], "rows20")
         for t in range(PACK - 1):
             nc.scalar.activation(rows21[:, t, :], x_rows[LAST][t][:].indirect(entries(wide, S)), COPY)
 

@@ -41,17 +41,20 @@ def tile_moe_pre_lin_relu_kernel(tc, xT, w_words, w_scales, b, gate, offs, out):
         offsets = sb.tile([P, S // PER_COL], U16, name="offsets")
         x_rows = [[sb.tile([P, T], F32, name="x_rows%d_%d" % (a, t), align_bytes=64) for t in range(PACK) if (a, t) != (LAST, PACK - 1)] for a in range(PASSES)]
         x_last = sb.tile([P, PACK * C], F32, name="x_last", align_bytes=64)
-        w_first = sb.tile([P, PASSES, 2 * P], U32, name="w_first", align_bytes=64)
-        w_third = sb.tile([P, PASSES, P], U32, name="w_third", align_bytes=64)
-        w_second = sb.tile([P, PASSES, N], U32, name="w_second", align_bytes=64)
+        w_first = sb.tile([P, LAST, 2 * P], U32, name="w_first", align_bytes=64)
+        w_third = sb.tile([P, LAST, P], U32, name="w_third", align_bytes=64)
+        w_second = sb.tile([P, LAST, N], U32, name="w_second", align_bytes=64)
+        w_last = [sb.tile([P, N], U32, name="w_last%d" % e, align_bytes=64) for e in range(E)]
         w_planes = sb.tile([P, 2, N], U8, name="w_planes", align_bytes=64)
         gate_cols = sb.tile([P, GROUPS], F32, name="gate_cols")
         identity = sb.tile([P, P], F32, name="identity")
-        bias = sb.tile([P, N_TILES, E], F32, name="bias")
+        bias_rows = sb.tile([P, P, E], F32, name="bias_rows")
         result = [sb.tile([P, T], F32, name="result%d" % n) for n in range(N_TILES)]
         make_identity(nc, identity[:])
 
         nc.vector.memset(w_planes[:].rearrange("p g n -> p (g n)").bitcast(I32), 0)
+        nc.vector.memset(bias_rows[:], 0.0)
+        nc.gpsimd.dma_start(out=bias_rows[0:N_TILES], in_=b.rearrange("(n p) e -> n p e", p=P))
         for n in range(N_TILES - 1):
             nc.vector.memset(result[n][:], 0.0)
         nc.scalar.activation(result[N_TILES - 1][:], result[0][:], COPY)
@@ -76,11 +79,12 @@ def tile_moe_pre_lin_relu_kernel(tc, xT, w_words, w_scales, b, gate, offs, out):
             nc.sync.dma_start(out=x_rows[LAST][t][:], in_=x_view[LAST, t])
         nc.sync.dma_start(out=x_last[:, 0:T], in_=x_view[LAST, PACK - 1])
         load_scales(0, PLANES)
-        nc.sync.dma_start(out=w_first[:].bitcast(I32), in_=w_view[0, :, :, 0 : 2 * PACK * P].bitcast(I32))
-        nc.sync.dma_start(out=w_third[:].bitcast(I32), in_=w_view[0, :, :, 2 * PACK * P :].bitcast(I32))
-        nc.sync.dma_start(out=bias[:], in_=b.rearrange("(n p) e -> p n e", p=P))
+        nc.sync.dma_start(out=w_first[:].bitcast(I32), in_=w_view[0, :, 0:LAST, 0 : 2 * PACK * P].bitcast(I32))
+        nc.sync.dma_start(out=w_last[0][:].bitcast(I32), in_=w_view[0, :, LAST, :].bitcast(I32))
+        nc.sync.dma_start(out=w_third[:].bitcast(I32), in_=w_view[0, :, 0:LAST, 2 * PACK * P :].bitcast(I32))
         load_scales(1, E * PASSES - PLANES)
-        nc.sync.dma_start(out=w_second[:].bitcast(I32), in_=w_view[1].bitcast(I32))
+        nc.sync.dma_start(out=w_second[:].bitcast(I32), in_=w_view[1, :, 0:LAST, :].bitcast(I32))
+        nc.sync.dma_start(out=w_last[1][:].bitcast(I32), in_=w_view[1, :, LAST, :].bitcast(I32))
 
         def entries(lo, hi):
             return offsets[:, lo // PER_COL : hi // PER_COL]
@@ -116,6 +120,8 @@ def tile_moe_pre_lin_relu_kernel(tc, xT, w_words, w_scales, b, gate, offs, out):
                 one_pass(e, n, LAST, False, True)
 
         def weights_of(e, n, a):
+            if a == LAST:
+                return w_last[e][:, n * P : (n + 1) * P]
             if e == 1:
                 return w_second[:, a, n * P : (n + 1) * P]
             return w_first[:, a, n * P : (n + 1) * P] if n < 2 else w_third[:, a, :]
@@ -136,10 +142,10 @@ def tile_moe_pre_lin_relu_kernel(tc, xT, w_words, w_scales, b, gate, offs, out):
         ys = {(e, n): sb.tile([P, C], F32, name="y%d_%d" % (e, n)) for e in range(E) for n in range(N_TILES)}
 
         def relu_scalar(e, n):
-            nc.scalar.activation(ys[(e, n)][:], acc[(e, n)][:], RELU, bias=bias[:, n, e : e + 1])
+            nc.scalar.activation(ys[(e, n)][:], acc[(e, n)][:], RELU, bias=bias[:, e, n : n + 1])
 
         def relu_vector(e, n):
-            nc.vector.tensor_scalar(ys[(e, n)][:], acc[(e, n)][:], bias[:, n, e : e + 1], 0.0, ADD, MAX)
+            nc.vector.tensor_scalar(ys[(e, n)][:], acc[(e, n)][:], bias[:, e, n : n + 1], 0.0, ADD, MAX)
 
         def scatter_scalar(e, n, lo, hi):
             nc.scalar.activation(result[n][:].indirect(entries(e * C + lo, e * C + hi)), ys[(e, n)][:, lo:hi], COPY)
@@ -150,6 +156,10 @@ def tile_moe_pre_lin_relu_kernel(tc, xT, w_words, w_scales, b, gate, offs, out):
         spread = psum.tile([P, P, GROUPS], F32, name="spread")
         for g in range(GROUPS):
             nc.tensor.transpose(spread[:, :, g], gate_cols[:, g : g + 1].to_broadcast([P, P]), identity[:])
+
+        bias_turned = psum.tile([P, E, P], F32, name="bias_turned")
+        for e in range(E):
+            nc.tensor.transpose(bias_turned[:, e, :], bias_rows[:, :, e], identity[:])
 
         woven0 = sb.tile([P, S, PACK], BF16, name="woven0", align_bytes=64)
         rows00 = sb.tile([P, PACK, C], F32, name="rows00")
@@ -180,6 +190,9 @@ def tile_moe_pre_lin_relu_kernel(tc, xT, w_words, w_scales, b, gate, offs, out):
         gate_and_weave(woven1[:, cut:tail], rows1v[:, :, 0 : tail - cut], cut, tail)
         gate_and_weave(woven1[:, 0:cut], rows1s[:], 0, cut)
         quantise(1, [0], woven1[:, 0:C])
+
+        bias = sb.tile([P, E, N_TILES], F32, name="bias", tag="x_rows1_3", align_bytes=64)
+        nc.scalar.copy(bias[:], bias_turned[:, :, 0:N_TILES])
 
         wide = C + 96
         rows20 = sb.tile([P, PACK, wide], F32, name="rows20", align_bytes=64)

@@ -1,7 +1,6 @@
 from contextlib import ExitStack
 
 import concourse.mybir as mybir
-from concourse.masks import make_identity
 
 K, T, E, C, N = 1536, 768, 2, 256, 384
 S = E * C
@@ -14,6 +13,15 @@ PER_COL = 16
 GROUPS = S // P
 PLANES = 4
 LINE = 4
+PAIR = 2
+QUAD = 32
+
+CUTS = [[256, 256, 256, 256], [384, 384, 256, 256]]
+HEADS = [256, 224]
+WIDE = 384
+SIDE = 80
+LAST_CUTS = [256, 256, 384]
+FIRST = 128
 
 F32 = mybir.dt.float32
 BF16 = mybir.dt.bfloat16
@@ -25,6 +33,7 @@ FP8X4 = mybir.dt.float8_e4m3fn_x4
 MULT = mybir.AluOpType.mult
 ADD = mybir.AluOpType.add
 MAX = mybir.AluOpType.max
+IS_EQUAL = mybir.AluOpType.is_equal
 RELU = mybir.ActivationFunctionType.Relu
 COPY = mybir.ActivationFunctionType.Copy
 
@@ -40,7 +49,7 @@ def tile_moe_pre_lin_relu_kernel(tc, xT, w_words, w_scales, b, gate, offs, out):
 
         offsets = sb.tile([P, S // PER_COL], U16, name="offsets")
         x_rows = [[sb.tile([P, T], F32, name="x_rows%d_%d" % (a, t), align_bytes=64) for t in range(PACK) if (a, t) != (LAST, PACK - 1)] for a in range(PASSES)]
-        x_last = sb.tile([P, PACK * C], F32, name="x_last", align_bytes=64)
+        x_last = sb.tile([P, T + S - WIDE], F32, name="x_last", align_bytes=64)
         w_first = sb.tile([P, LAST, 2 * P], U32, name="w_first", align_bytes=64)
         w_third = sb.tile([P, LAST, P], U32, name="w_third", align_bytes=64)
         w_second = sb.tile([P, LAST, N], U32, name="w_second", align_bytes=64)
@@ -50,13 +59,21 @@ def tile_moe_pre_lin_relu_kernel(tc, xT, w_words, w_scales, b, gate, offs, out):
         identity = sb.tile([P, P], F32, name="identity")
         bias_rows = sb.tile([P, P, E], F32, name="bias_rows")
         result = [sb.tile([P, T], F32, name="result%d" % n) for n in range(N_TILES)]
-        make_identity(nc, identity[:])
+        ones = sb.tile([P, QUAD], F32, name="ones", align_bytes=64)
+        column_no = sb.tile([P, QUAD], F32, name="column_no", align_bytes=64)
+        row_no = sb.tile([P, QUAD], F32, name="row_no", align_bytes=64)
+        nc.vector.memset(ones[:], 1.0)
+        nc.vector.memset(identity[:], 0.0)
+        nc.vector.tensor_tensor_scan(column_no[:], ones[:], ones[:], 0.0, MULT, ADD)
+        nc.vector.transpose(row_no[:], column_no[:])
+        for q in range(P // QUAD):
+            quad = slice(QUAD * q, QUAD * (q + 1))
+            nc.vector.tensor_tensor(identity[quad, quad], column_no[quad, :], row_no[quad, :], IS_EQUAL)
 
         nc.vector.memset(w_planes[:].rearrange("p g n -> p (g n)").bitcast(I32), 0)
         nc.vector.memset(bias_rows[:], 0.0)
-        nc.gpsimd.dma_start(out=bias_rows[0:N_TILES], in_=b.rearrange("(n p) e -> n p e", p=P))
         for n in range(N_TILES - 1):
-            nc.vector.memset(result[n][:], 0.0)
+            nc.gpsimd.memset(result[n][:], 0.0)
         nc.scalar.activation(result[N_TILES - 1][:], result[0][:], COPY)
 
         x_view = xT.rearrange("(a p t) j -> a t p j", p=P, t=PACK)
@@ -68,20 +85,21 @@ def tile_moe_pre_lin_relu_kernel(tc, xT, w_words, w_scales, b, gate, offs, out):
                 source = scale_view[q, PLANES * g : PLANES * g + count]
                 nc.sync.dma_start(out=w_planes[32 * q : 32 * q + 4 * count, g, :].bitcast(I32), in_=source.bitcast(I32))
 
+        nc.sync.dma_start(out=gate_cols[:], in_=gate[0, :].rearrange("(p g) -> p g", g=GROUPS))
         nc.sync.dma_start(out=x_rows[0][0][:], in_=x_view[0, 0])
         nc.sync.dma_start(offsets[:], offs)
-        nc.sync.dma_start(out=gate_cols[:], in_=gate[0, :].rearrange("(p g) -> p g", g=GROUPS))
         for a in range(LAST):
             for t in range(PACK):
                 if (a, t) != (0, 0):
                     nc.sync.dma_start(out=x_rows[a][t][:], in_=x_view[a, t])
+        nc.sync.dma_start(out=bias_rows[0:N_TILES], in_=b.rearrange("(n p) e -> n p e", p=P))
         for t in range(PACK - 1):
             nc.sync.dma_start(out=x_rows[LAST][t][:], in_=x_view[LAST, t])
         nc.sync.dma_start(out=x_last[:, 0:T], in_=x_view[LAST, PACK - 1])
         load_scales(0, PLANES)
         nc.sync.dma_start(out=w_first[:].bitcast(I32), in_=w_view[0, :, 0:LAST, 0 : 2 * PACK * P].bitcast(I32))
-        nc.sync.dma_start(out=w_last[0][:].bitcast(I32), in_=w_view[0, :, LAST, :].bitcast(I32))
         nc.sync.dma_start(out=w_third[:].bitcast(I32), in_=w_view[0, :, 0:LAST, 2 * PACK * P :].bitcast(I32))
+        nc.sync.dma_start(out=w_last[0][:].bitcast(I32), in_=w_view[0, :, LAST, :].bitcast(I32))
         load_scales(1, E * PASSES - PLANES)
         nc.sync.dma_start(out=w_second[:].bitcast(I32), in_=w_view[1, :, 0:LAST, :].bitcast(I32))
         nc.sync.dma_start(out=w_last[1][:].bitcast(I32), in_=w_view[1, :, LAST, :].bitcast(I32))
@@ -89,15 +107,24 @@ def tile_moe_pre_lin_relu_kernel(tc, xT, w_words, w_scales, b, gate, offs, out):
         def entries(lo, hi):
             return offsets[:, lo // PER_COL : hi // PER_COL]
 
-        def by_lines(rows):
-            return rows.rearrange("k t (c i) -> k c t i", i=LINE)
+        def gather_scalar(rows, window, lo, hi):
+            nc.scalar.activation(rows, window.indirect(entries(lo, hi)), COPY)
 
-        def woven_by_lines(woven):
-            return woven.rearrange("k (c i) t -> k c t i", i=LINE)
+        def gather_vector(rows, window, lo, hi):
+            nc.vector.tensor_copy(rows, window.indirect(entries(lo, hi)))
 
-        def gate_and_weave(woven, rows, lo, hi):
-            weights = spread[:, lo // LINE : hi // LINE, :].unsqueeze(2)
-            nc.vector.tensor_tensor(woven_by_lines(woven), by_lines(rows), weights.to_broadcast([P, (hi - lo) // LINE, PACK, LINE]), MULT)
+        def gate_and_weave(engine, woven, rows, weights):
+            slots, planes = woven.shape[1], woven.shape[2]
+            engine.tensor_tensor(
+                woven.rearrange("k (c i) t -> k c t i", i=LINE),
+                rows.rearrange("k t (c i) -> k c t i", i=LINE),
+                weights.rearrange("k (c i) -> k c i", i=LINE).unsqueeze(2).to_broadcast([P, slots // LINE, planes, LINE]),
+                MULT,
+            )
+
+        def gate_and_weave_gpsimd(woven, rows, weights):
+            slots, planes = woven.shape[1], woven.shape[2]
+            nc.gpsimd.tensor_tensor(woven, rows.rearrange("k t j -> k j t"), weights.unsqueeze(2).to_broadcast([P, slots, planes]), MULT)
 
         quantised = {}
 
@@ -141,11 +168,14 @@ def tile_moe_pre_lin_relu_kernel(tc, xT, w_words, w_scales, b, gate, offs, out):
 
         ys = {(e, n): sb.tile([P, C], F32, name="y%d_%d" % (e, n)) for e in range(E) for n in range(N_TILES)}
 
+        def bias_of(e, n):
+            return bias_first[:] if (e, n) == (0, 0) else bias[:, N_TILES * e + n - 1 : N_TILES * e + n]
+
         def relu_scalar(e, n):
-            nc.scalar.activation(ys[(e, n)][:], acc[(e, n)][:], RELU, bias=bias[:, e, n : n + 1])
+            nc.scalar.activation(ys[(e, n)][:], acc[(e, n)][:], RELU, bias=bias_of(e, n))
 
         def relu_vector(e, n):
-            nc.vector.tensor_scalar(ys[(e, n)][:], acc[(e, n)][:], bias[:, e, n : n + 1], 0.0, ADD, MAX)
+            nc.vector.tensor_scalar(ys[(e, n)][:], acc[(e, n)][:], bias_of(e, n), 0.0, ADD, MAX)
 
         def scatter_scalar(e, n, lo, hi):
             nc.scalar.activation(result[n][:].indirect(entries(e * C + lo, e * C + hi)), ys[(e, n)][:, lo:hi], COPY)
@@ -153,84 +183,75 @@ def tile_moe_pre_lin_relu_kernel(tc, xT, w_words, w_scales, b, gate, offs, out):
         def scatter_vector(e, n, lo, hi):
             nc.vector.tensor_copy(result[n][:].indirect(entries(e * C + lo, e * C + hi)), ys[(e, n)][:, lo:hi])
 
-        spread = psum.tile([P, P, GROUPS], F32, name="spread")
-        for g in range(GROUPS):
-            nc.tensor.transpose(spread[:, :, g], gate_cols[:, g : g + 1].to_broadcast([P, P]), identity[:])
-
-        bias_turned = psum.tile([P, E, P], F32, name="bias_turned")
-        for e in range(E):
-            nc.tensor.transpose(bias_turned[:, e, :], bias_rows[:, :, e], identity[:])
-
-        woven0 = sb.tile([P, S, PACK], BF16, name="woven0", align_bytes=64)
-        rows00 = sb.tile([P, PACK, C], F32, name="rows00")
-        rows01 = sb.tile([P, PACK, C], F32, name="rows01")
-        for t in range(PACK):
-            nc.scalar.activation(rows00[:, t, :], x_rows[0][t][:].indirect(entries(0, C)), COPY)
-            nc.vector.tensor_copy(rows01[:, t, :], x_rows[0][t][:].indirect(entries(C, S)))
-        cut, tail = 320, 352
-        gate_second = sb.tile([P, C], F32, name="gate_second")
-        nc.vector.tensor_copy(gate_second[:], spread[:, C // LINE :, :].rearrange("k c i -> k (c i)"))
-
-        def gate_and_weave_gpsimd(woven, rows, lo, hi):
-            weights = gate_second[:, lo - C : hi - C].rearrange("k (c i) -> k c i", i=LINE).unsqueeze(2)
-            nc.gpsimd.tensor_tensor(woven_by_lines(woven), by_lines(rows), weights.to_broadcast([P, (hi - lo) // LINE, PACK, LINE]), MULT)
-
-        gate_and_weave_gpsimd(woven0[:, tail:S], rows01[:, :, tail - C :], tail, S)
-        gate_and_weave(woven0[:, 0:C], rows00[:], 0, C)
-        gate_and_weave(woven0[:, C:tail], rows01[:, :, 0 : tail - C], C, tail)
-
-        woven1 = sb.tile([P, S, PACK], BF16, name="woven1", align_bytes=64)
-        rows1s = sb.tile([P, PACK, cut], F32, name="rows1s")
-        rows1v = sb.tile([P, PACK, S - cut], F32, name="rows1v", tag="rows00")
-        for t in range(PACK):
-            nc.scalar.activation(rows1s[:, t, :], x_rows[1][t][:].indirect(entries(0, cut)), COPY)
-            nc.vector.tensor_copy(rows1v[:, t, :], x_rows[1][t][:].indirect(entries(cut, S)))
-        quantise(0, [0, 1], woven0[:], "x_rows1_1")
-        gate_and_weave_gpsimd(woven1[:, tail:S], rows1v[:, :, tail - cut :], tail, S)
-        gate_and_weave(woven1[:, cut:tail], rows1v[:, :, 0 : tail - cut], cut, tail)
-        gate_and_weave(woven1[:, 0:cut], rows1s[:], 0, cut)
-        quantise(1, [0], woven1[:, 0:C])
-
-        bias = sb.tile([P, E, N_TILES], F32, name="bias", tag="x_rows1_3", align_bytes=64)
-        nc.scalar.copy(bias[:], bias_turned[:, :, 0:N_TILES])
-
-        wide = C + 96
-        rows20 = sb.tile([P, PACK, wide], F32, name="rows20", align_bytes=64)
-        rows21 = x_last[:].rearrange("k (t j) -> k t j", t=PACK)[:, :, 0 : S - wide]
-        woven2 = sb.tile([P, wide, PACK], BF16, name="woven2", align_bytes=64)
-        woven20 = woven2[:, wide - C :]
-        woven21 = woven2[:, 0:C]
-        for t in range(2):
-            nc.scalar.activation(rows20[:, t, :], x_rows[LAST][t][:].indirect(entries(0, wide)), COPY)
-        nc.scalar.activation(rows20[:, 2, 0:C], x_rows[LAST][2][:].indirect(entries(0, C)), COPY)
-        nc.vector.tensor_copy(rows20[:, 2, C:wide], x_rows[LAST][2][:].indirect(entries(C, wide)))
-        nc.scalar.activation(rows20[:, PACK - 1, 0:C], x_last[:, 0:T].indirect(entries(0, C)), COPY)
-        nc.vector.tensor_copy(rows20[:, PACK - 1, C:wide], x_last[:, 0:T].indirect(entries(C, wide)))
-        nc.scalar.activation(rows21[:, PACK - 1, :], x_last[:, 0:T].indirect(entries(wide, S)), COPY)
-        gate_and_weave(woven20, rows20[:, :, 0:C], 0, C)
-        quantise(LAST, [0], woven20)
-        multiply(0, [0, 1])
-        multiply(0, [2])
-        gate_and_weave_gpsimd(woven21[:, 0 : wide - C], rows20[:, :, C:wide], C, wide)
-        quantise(1, [1], woven1[:, C:S], "rows20")
-        for t in range(PACK - 1):
-            nc.scalar.activation(rows21[:, t, :], x_rows[LAST][t][:].indirect(entries(wide, S)), COPY)
-
         def store(n):
             nc.sync.dma_start(out=out[n * P : (n + 1) * P, :], in_=result[n][:])
 
-        gate_and_weave(woven21[:, wide - C :], rows21, wide, S)
-        first = 96
+        spread = psum.tile([P, P, GROUPS], F32, name="spread")
+        for g in range(GROUPS):
+            nc.tensor.transpose(spread[:, :, g], gate_cols[:, g : g + 1].to_broadcast([P, P]), identity[:])
+        gates = spread[:].rearrange("k c i -> k (c i)")
+
+
+        gate_copy = sb.tile([P, C], F32, name="gate_copy")
+        nc.vector.tensor_copy(gate_copy[:], gates[:, 0:C])
+
+        def pair(h):
+            return slice(PAIR * h, PAIR * (h + 1))
+
+        woven = [sb.tile([P, S, PACK], BF16, name="woven%d" % a, align_bytes=64) for a in range(LAST)]
+        for a in range(LAST):
+            rows = sb.tile([P, PACK, S], F32, name="rows%d" % a, align_bytes=64)
+            head = HEADS[a]
+            for h in range(2):
+                for t in range(PAIR * h, PAIR * (h + 1)):
+                    cut = CUTS[a][t]
+                    gather_scalar(rows[:, t, 0:cut], x_rows[a][t][:], 0, cut)
+                    gather_vector(rows[:, t, cut:S], x_rows[a][t][:], cut, S)
+                gate_and_weave_gpsimd(woven[a][:, 0:head, pair(h)], rows[:, pair(h), 0:head], gate_copy[:, 0:head])
+            gate_and_weave(nc.vector, woven[a][:, head:S], rows[:, :, head:S], gates[:, head:S])
+
+        bias_turned = psum.tile([P, E * N_TILES + P], F32, name="bias_turned")
+        for e in range(E):
+            nc.tensor.transpose(bias_turned[:, N_TILES * e : N_TILES * e + P], bias_rows[:, :, e], identity[:])
+        bias_first = sb.tile([P, 1], F32, name="bias_first", align_bytes=64)
+        bias = sb.tile([P, E * N_TILES - 1], F32, name="bias")
+        nc.scalar.copy(bias_first[:], bias_turned[:, 0:1])
+        nc.scalar.copy(bias[:], bias_turned[:, 1 : E * N_TILES])
+
+        rows2 = sb.tile([P, PACK, WIDE], F32, name="rows2", align_bytes=64)
+        late_rows = x_last[:, T - (PACK - 1) * (S - WIDE) :].rearrange("k (t j) -> k t j", t=PACK)
+        woven2 = sb.tile([P, WIDE, PACK], BF16, name="woven2", tag="woven0", align_bytes=64)
+        woven20 = woven2[:, WIDE - C :]
+        woven21 = woven2[:, 0:C]
+        for t in range(PAIR):
+            gather_scalar(rows2[:, t, 0 : LAST_CUTS[t]], x_rows[LAST][t][:], 0, LAST_CUTS[t])
+            gather_vector(rows2[:, t, LAST_CUTS[t] : WIDE], x_rows[LAST][t][:], LAST_CUTS[t], WIDE)
+        quantise(0, [0, 1], woven[0][:], "rows1")
+        quantise(1, [0], woven[1][:, 0:C])
+        gather_scalar(rows2[:, 2, 0 : LAST_CUTS[2]], x_rows[LAST][2][:], 0, LAST_CUTS[2])
+        gather_scalar(rows2[:, 3, 0:C], x_last[:, 0:T], 0, C)
+        gather_scalar(rows2[:, 3, C:WIDE], x_last[:, 0:T], C, WIDE)
+        gate_and_weave_gpsimd(woven20[:, 0:SIDE], rows2[:, :, 0:SIDE], gate_copy[:, 0:SIDE])
+        gate_and_weave(nc.vector, woven20[:, SIDE:], rows2[:, :, SIDE:C], gates[:, SIDE:C])
+        gate_and_weave(nc.vector, woven21[:, 0 : WIDE - C], rows2[:, :, C:WIDE], gates[:, C:WIDE])
+        quantise(LAST, [0], woven20)
+        multiply(0, [0, 1, 2])
+        quantise(1, [1], woven[1][:, C:S], "rows2")
+        gather_scalar(late_rows[:, PACK - 1, :], x_last[:, 0:T], WIDE, S)
+        for t in range(PACK - 1):
+            gather_scalar(late_rows[:, t, :], x_rows[LAST][t][:], WIDE, S)
+        gate_and_weave(nc.vector, woven21[:, WIDE - C :], late_rows, gates[:, WIDE:S])
+
         relu_scalar(0, 0)
         relu_scalar(0, 1)
         relu_vector(0, 2)
-        quantise(LAST, [1], woven21)
+        quantise(LAST, [1], woven21, "bias_first")
         multiply(1, [0, 1])
         multiply(1, [2])
         scatter_scalar(0, 0, 0, C)
         scatter_scalar(0, 1, 0, C)
-        scatter_vector(0, 2, 0, first)
-        scatter_scalar(0, 2, first, C)
+        scatter_vector(0, 2, 0, FIRST)
+        scatter_scalar(0, 2, FIRST, C)
         relu_vector(1, 0)
         relu_vector(1, 1)
         for n in range(2):

@@ -17,7 +17,7 @@ PAIR = 2
 QUAD = 32
 
 CUTS = [[256, 256, 256, 256], [384, 384, 256, 256]]
-HEADS = [256, 224]
+HEADS = [272, 160]
 WIDE = 384
 SIDE = 80
 LAST_CUTS = [256, 256, 384]
@@ -192,22 +192,18 @@ def tile_moe_pre_lin_relu_kernel(tc, xT, w_words, w_scales, b, gate, offs, out):
         gates = spread[:].rearrange("k c i -> k (c i)")
 
 
-        gate_copy = sb.tile([P, C], F32, name="gate_copy")
-        nc.vector.tensor_copy(gate_copy[:], gates[:, 0:C])
-
-        def pair(h):
-            return slice(PAIR * h, PAIR * (h + 1))
+        gate_copy = sb.tile([P, HEADS[0]], F32, name="gate_copy")
+        nc.vector.tensor_copy(gate_copy[:], gates[:, 0 : HEADS[0]])
 
         woven = [sb.tile([P, S, PACK], BF16, name="woven%d" % a, align_bytes=64) for a in range(LAST)]
         for a in range(LAST):
             rows = sb.tile([P, PACK, S], F32, name="rows%d" % a, align_bytes=64)
             head = HEADS[a]
-            for h in range(2):
-                for t in range(PAIR * h, PAIR * (h + 1)):
-                    cut = CUTS[a][t]
-                    gather_scalar(rows[:, t, 0:cut], x_rows[a][t][:], 0, cut)
-                    gather_vector(rows[:, t, cut:S], x_rows[a][t][:], cut, S)
-                gate_and_weave_gpsimd(woven[a][:, 0:head, pair(h)], rows[:, pair(h), 0:head], gate_copy[:, 0:head])
+            for t in range(PACK):
+                cut = CUTS[a][t]
+                gather_scalar(rows[:, t, 0:cut], x_rows[a][t][:], 0, cut)
+                gather_vector(rows[:, t, cut:S], x_rows[a][t][:], cut, S)
+            gate_and_weave_gpsimd(woven[a][:, 0:head], rows[:, :, 0:head], gate_copy[:, 0:head])
             gate_and_weave(nc.vector, woven[a][:, head:S], rows[:, :, head:S], gates[:, head:S])
 
         bias_turned = psum.tile([P, E * N_TILES + P], F32, name="bias_turned")

@@ -73,7 +73,7 @@ def tile_moe_pre_lin_relu_kernel(tc, xT, w_words, w_scales, b, gate, offs, out):
         nc.vector.memset(w_planes[:].rearrange("p g n -> p (g n)").bitcast(I32), 0)
         nc.vector.memset(bias_rows[:], 0.0)
         for n in range(N_TILES - 1):
-            nc.gpsimd.memset(result[n][:], 0.0)
+            nc.vector.memset(result[n][:], 0.0)
         nc.scalar.activation(result[N_TILES - 1][:], result[0][:], COPY)
 
         x_view = xT.rearrange("(a p t) j -> a t p j", p=P, t=PACK)
@@ -85,9 +85,9 @@ def tile_moe_pre_lin_relu_kernel(tc, xT, w_words, w_scales, b, gate, offs, out):
                 source = scale_view[q, PLANES * g : PLANES * g + count]
                 nc.sync.dma_start(out=w_planes[32 * q : 32 * q + 4 * count, g, :].bitcast(I32), in_=source.bitcast(I32))
 
-        nc.sync.dma_start(out=gate_cols[:], in_=gate[0, :].rearrange("(p g) -> p g", g=GROUPS))
         nc.sync.dma_start(out=x_rows[0][0][:], in_=x_view[0, 0])
         nc.sync.dma_start(offsets[:], offs)
+        nc.sync.dma_start(out=gate_cols[:], in_=gate[0, :].rearrange("(p g) -> p g", g=GROUPS))
         for a in range(LAST):
             for t in range(PACK):
                 if (a, t) != (0, 0):

@@ -12,7 +12,7 @@ N_TILES = N // P
 PER_COL = 16
 GROUPS = S // P
 PLANES = 4
-LINE = 4
+LINE = 2
 PAIR = 2
 QUAD = 32
 

@@ -21,7 +21,7 @@ HEADS = [272, 160]
 WIDE = 384
 SIDE = 80
 LAST_CUTS = [256, 256, 384]
-FIRST = 128
+FIRST = 192
 
 F32 = mybir.dt.float32
 BF16 = mybir.dt.bfloat16
@@ -166,22 +166,22 @@ def tile_moe_pre_lin_relu_kernel(tc, xT, w_words, w_scales, b, gate, offs, out):
                 stop=stop,
             )
 
-        ys = {(e, n): sb.tile([P, C], F32, name="y%d_%d" % (e, n)) for e in range(E) for n in range(N_TILES)}
+        ys = [sb.tile([P, S], F32, name="y%d" % n) for n in range(N_TILES)]
 
         def bias_of(e, n):
             return bias_first[:] if (e, n) == (0, 0) else bias[:, N_TILES * e + n - 1 : N_TILES * e + n]
 
         def relu_scalar(e, n):
-            nc.scalar.activation(ys[(e, n)][:], acc[(e, n)][:], RELU, bias=bias_of(e, n))
+            nc.scalar.activation(ys[n][:, e * C : (e + 1) * C], acc[(e, n)][:], RELU, bias=bias_of(e, n))
 
         def relu_vector(e, n):
-            nc.vector.tensor_scalar(ys[(e, n)][:], acc[(e, n)][:], bias_of(e, n), 0.0, ADD, MAX)
+            nc.vector.tensor_scalar(ys[n][:, e * C : (e + 1) * C], acc[(e, n)][:], bias_of(e, n), 0.0, ADD, MAX)
 
-        def scatter_scalar(e, n, lo, hi):
-            nc.scalar.activation(result[n][:].indirect(entries(e * C + lo, e * C + hi)), ys[(e, n)][:, lo:hi], COPY)
+        def scatter_scalar(n, lo, hi):
+            nc.scalar.activation(result[n][:].indirect(entries(lo, hi)), ys[n][:, lo:hi], COPY)
 
-        def scatter_vector(e, n, lo, hi):
-            nc.vector.tensor_copy(result[n][:].indirect(entries(e * C + lo, e * C + hi)), ys[(e, n)][:, lo:hi])
+        def scatter_vector(n, lo, hi):
+            nc.vector.tensor_copy(result[n][:].indirect(entries(lo, hi)), ys[n][:, lo:hi])
 
         def store(n):
             nc.sync.dma_start(out=out[n * P : (n + 1) * P, :], in_=result[n][:])
@@ -242,17 +242,15 @@ def tile_moe_pre_lin_relu_kernel(tc, xT, w_words, w_scales, b, gate, offs, out):
         relu_scalar(0, 1)
         relu_vector(0, 2)
         quantise(LAST, [1], woven21, "bias_first")
-        multiply(1, [0, 1])
-        multiply(1, [2])
-        scatter_scalar(0, 0, 0, C)
-        scatter_scalar(0, 1, 0, C)
-        scatter_vector(0, 2, 0, FIRST)
-        scatter_scalar(0, 2, FIRST, C)
-        relu_vector(1, 0)
-        relu_vector(1, 1)
-        for n in range(2):
-            scatter_vector(1, n, 0, C)
-            store(n)
-        relu_scalar(1, 2)
-        scatter_scalar(1, 2, 0, C)
+        multiply(1, [0, 1, 2])
+        scatter_scalar(0, 0, C)
+        scatter_scalar(1, 0, C)
+        scatter_vector(2, 0, FIRST)
+        for n in range(N_TILES):
+            relu_vector(1, n)
+        scatter_vector(0, C, S)
+        store(0)
+        scatter_scalar(2, FIRST, S)
         store(2)
+        scatter_vector(1, C, S)
+        store(1)

@@ -21,7 +21,7 @@ HEADS = [272, 160]
 WIDE = 384
 SIDE = 80
 LAST_CUTS = [256, 256, 384]
-FIRST = 192
+FIRST = 160
 
 F32 = mybir.dt.float32
 BF16 = mybir.dt.bfloat16
@@ -50,10 +50,7 @@ def tile_moe_pre_lin_relu_kernel(tc, xT, w_words, w_scales, b, gate, offs, out):
         offsets = sb.tile([P, S // PER_COL], U16, name="offsets")
         x_rows = [[sb.tile([P, T], F32, name="x_rows%d_%d" % (a, t), align_bytes=64) for t in range(PACK) if (a, t) != (LAST, PACK - 1)] for a in range(PASSES)]
         x_last = sb.tile([P, T + S - WIDE], F32, name="x_last", align_bytes=64)
-        w_first = sb.tile([P, LAST, 2 * P], U32, name="w_first", align_bytes=64)
-        w_third = sb.tile([P, LAST, P], U32, name="w_third", align_bytes=64)
-        w_second = sb.tile([P, LAST, N], U32, name="w_second", align_bytes=64)
-        w_last = [sb.tile([P, N], U32, name="w_last%d" % e, align_bytes=64) for e in range(E)]
+        weights = [[sb.tile([P, N], U32, name="weights%d_%d" % (e, a), align_bytes=64) for a in range(PASSES)] for e in range(E)]
         w_planes = sb.tile([P, 2, N], U8, name="w_planes", align_bytes=64)
         gate_cols = sb.tile([P, GROUPS], F32, name="gate_cols")
         identity = sb.tile([P, P], F32, name="identity")
@@ -96,13 +93,10 @@ def tile_moe_pre_lin_relu_kernel(tc, xT, w_words, w_scales, b, gate, offs, out):
         for t in range(PACK - 1):
             nc.sync.dma_start(out=x_rows[LAST][t][:], in_=x_view[LAST, t])
         nc.sync.dma_start(out=x_last[:, 0:T], in_=x_view[LAST, PACK - 1])
-        load_scales(0, PLANES)
-        nc.sync.dma_start(out=w_first[:].bitcast(I32), in_=w_view[0, :, 0:LAST, 0 : 2 * PACK * P].bitcast(I32))
-        nc.sync.dma_start(out=w_third[:].bitcast(I32), in_=w_view[0, :, 0:LAST, 2 * PACK * P :].bitcast(I32))
-        nc.sync.dma_start(out=w_last[0][:].bitcast(I32), in_=w_view[0, :, LAST, :].bitcast(I32))
-        load_scales(1, E * PASSES - PLANES)
-        nc.sync.dma_start(out=w_second[:].bitcast(I32), in_=w_view[1, :, 0:LAST, :].bitcast(I32))
-        nc.sync.dma_start(out=w_last[1][:].bitcast(I32), in_=w_view[1, :, LAST, :].bitcast(I32))
+        for e in range(E):
+            load_scales(e, min(PLANES, E * PASSES - PLANES * e))
+            for a in range(PASSES):
+                nc.sync.dma_start(out=weights[e][a][:].bitcast(I32), in_=w_view[e, :, a, :].bitcast(I32))
 
         def entries(lo, hi):
             return offsets[:, lo // PER_COL : hi // PER_COL]
@@ -138,27 +132,19 @@ def tile_moe_pre_lin_relu_kernel(tc, xT, w_words, w_scales, b, gate, offs, out):
 
         acc = {}
 
-        def multiply(e, blocks):
-            for n in blocks:
-                acc[(e, n)] = psum.tile([P, C], F32, name="acc%d_%d" % (e, n), tag="acc%d" % n)
-                one_pass(e, n, 0, True, False)
-                one_pass(e, n, 1, False, False)
-            for n in blocks:
-                one_pass(e, n, LAST, False, True)
-
-        def weights_of(e, n, a):
-            if a == LAST:
-                return w_last[e][:, n * P : (n + 1) * P]
-            if e == 1:
-                return w_second[:, a, n * P : (n + 1) * P]
-            return w_first[:, a, n * P : (n + 1) * P] if n < 2 else w_third[:, a, :]
+        def multiply(e):
+            for n in range(N_TILES):
+                acc[(e, n)] = psum.tile([P, C], F32, name="acc%d_%d" % (e, n))
+            for a in range(PASSES):
+                for n in range(N_TILES):
+                    one_pass(e, n, a, a == 0, a == LAST)
 
         def one_pass(e, n, a, start, stop):
             codes, plane = quantised[(a, e)]
             g, i = divmod(e * PASSES + a, PLANES)
             nc.tensor.matmul_mx(
                 out=acc[(e, n)][:],
-                lhsT=weights_of(e, n, a).bitcast(FP8X4),
+                lhsT=weights[e][a][:, n * P : (n + 1) * P].bitcast(FP8X4),
                 lhsT_scale=w_planes[4 * i :, g, n * P : (n + 1) * P],
                 rhs=codes.bitcast(FP8X4),
                 rhs_scale=plane,
@@ -231,7 +217,7 @@ def tile_moe_pre_lin_relu_kernel(tc, xT, w_words, w_scales, b, gate, offs, out):
         gate_and_weave(nc.vector, woven20[:, SIDE:], rows2[:, :, SIDE:C], gates[:, SIDE:C])
         gate_and_weave(nc.vector, woven21[:, 0 : WIDE - C], rows2[:, :, C:WIDE], gates[:, C:WIDE])
         quantise(LAST, [0], woven20)
-        multiply(0, [0, 1, 2])
+        multiply(0)
         quantise(1, [1], woven[1][:, C:S], "rows2")
         gather_scalar(late_rows[:, PACK - 1, :], x_last[:, 0:T], WIDE, S)
         for t in range(PACK - 1):
@@ -242,7 +228,7 @@ def tile_moe_pre_lin_relu_kernel(tc, xT, w_words, w_scales, b, gate, offs, out):
         relu_scalar(0, 1)
         relu_vector(0, 2)
         quantise(LAST, [1], woven21, "bias_first")
-        multiply(1, [0, 1, 2])
+        multiply(1)
         scatter_scalar(0, 0, C)
         scatter_scalar(1, 0, C)
         scatter_vector(2, 0, FIRST)

@@ -21,7 +21,7 @@ HEADS = [272, 160]
 WIDE = 384
 SIDE = 80
 LAST_CUTS = [256, 256, 384]
-FIRST = 160
+FIRST = 224
 
 F32 = mybir.dt.float32
 BF16 = mybir.dt.bfloat16
@@ -89,10 +89,10 @@ def tile_moe_pre_lin_relu_kernel(tc, xT, w_words, w_scales, b, gate, offs, out):
             for t in range(PACK):
                 if (a, t) != (0, 0):
                     nc.sync.dma_start(out=x_rows[a][t][:], in_=x_view[a, t])
-        nc.sync.dma_start(out=bias_rows[0:N_TILES], in_=b.rearrange("(n p) e -> n p e", p=P))
         for t in range(PACK - 1):
             nc.sync.dma_start(out=x_rows[LAST][t][:], in_=x_view[LAST, t])
         nc.sync.dma_start(out=x_last[:, 0:T], in_=x_view[LAST, PACK - 1])
+        nc.sync.dma_start(out=bias_rows[0:N_TILES], in_=b.rearrange("(n p) e -> n p e", p=P))
         for e in range(E):
             load_scales(e, min(PLANES, E * PASSES - PLANES * e))
             for a in range(PASSES):

from contextlib import ExitStack

import concourse.mybir as mybir

K, T, E, C, N = 1536, 768, 2, 256, 384
S = E * C
P = 128
PACK = 4
PASSES = K // (P * PACK)
LAST = PASSES - 1
N_TILES = N // P
PER_COL = 16
GROUPS = S // P
PLANES = 4
LINE = 2
PAIR = 2
QUAD = 32

CUTS = [[256, 256, 256, 256], [384, 384, 256, 256]]
HEADS = [272, 160]
WIDE = 384
SIDE = 80
LAST_CUTS = [256, 256, 384]
FIRST = 224

F32 = mybir.dt.float32
BF16 = mybir.dt.bfloat16
I32 = mybir.dt.int32
U32 = mybir.dt.uint32
U16 = mybir.dt.uint16
U8 = mybir.dt.uint8
FP8X4 = mybir.dt.float8_e4m3fn_x4
MULT = mybir.AluOpType.mult
ADD = mybir.AluOpType.add
MAX = mybir.AluOpType.max
IS_EQUAL = mybir.AluOpType.is_equal
RELU = mybir.ActivationFunctionType.Relu
COPY = mybir.ActivationFunctionType.Copy

FLOPS = 2 * K * N * S
BYTES = 4 * K * T + E * K * N + E * (K // 32) * N + 4 * N * E + 4 * S + 2 * S + 4 * N * T


def tile_moe_pre_lin_relu_kernel(tc, xT, w_words, w_scales, b, gate, offs, out):
    nc = tc.nc
    with ExitStack() as ctx:
        sb = ctx.enter_context(tc.tile_pool(name="sb", bufs=1))
        psum = ctx.enter_context(tc.psum_pool(name="psum", bufs=1))

        offsets = sb.tile([P, S // PER_COL], U16, name="offsets")
        x_rows = [[sb.tile([P, T], F32, name="x_rows%d_%d" % (a, t), align_bytes=64) for t in range(PACK) if (a, t) != (LAST, PACK - 1)] for a in range(PASSES)]
        x_last = sb.tile([P, T + S - WIDE], F32, name="x_last", align_bytes=64)
        weights = [[sb.tile([P, N], U32, name="weights%d_%d" % (e, a), align_bytes=64) for a in range(PASSES)] for e in range(E)]
        w_planes = sb.tile([P, 2, N], U8, name="w_planes", align_bytes=64)
        gate_cols = sb.tile([P, GROUPS], F32, name="gate_cols")
        identity = sb.tile([P, P], F32, name="identity")
        bias_rows = sb.tile([P, P, E], F32, name="bias_rows")
        result = [sb.tile([P, T], F32, name="result%d" % n) for n in range(N_TILES)]
        ones = sb.tile([P, QUAD], F32, name="ones", align_bytes=64)
        column_no = sb.tile([P, QUAD], F32, name="column_no", align_bytes=64)
        row_no = sb.tile([P, QUAD], F32, name="row_no", align_bytes=64)
        nc.vector.memset(ones[:], 1.0)
        nc.vector.memset(identity[:], 0.0)
        nc.vector.tensor_tensor_scan(column_no[:], ones[:], ones[:], 0.0, MULT, ADD)
        nc.vector.transpose(row_no[:], column_no[:])
        for q in range(P // QUAD):
            quad = slice(QUAD * q, QUAD * (q + 1))
            nc.vector.tensor_tensor(identity[quad, quad], column_no[quad, :], row_no[quad, :], IS_EQUAL)

        nc.vector.memset(w_planes[:].rearrange("p g n -> p (g n)").bitcast(I32), 0)
        nc.vector.memset(bias_rows[:], 0.0)
        for n in range(N_TILES - 1):
            nc.vector.memset(result[n][:], 0.0)
        nc.scalar.activation(result[N_TILES - 1][:], result[0][:], COPY)

        x_view = xT.rearrange("(a p t) j -> a t p j", p=P, t=PACK)
        scale_view = w_scales.rearrange("e a (q r) n -> q (e a) r n", r=4)
        w_view = w_words.rearrange("e a p n t -> e p a (n t)")

        def load_scales(g, count):
            for q in range(4):
                source = scale_view[q, PLANES * g : PLANES * g + count]
                nc.sync.dma_start(out=w_planes[32 * q : 32 * q + 4 * count, g, :].bitcast(I32), in_=source.bitcast(I32))

        nc.sync.dma_start(out=x_rows[0][0][:], in_=x_view[0, 0])
        nc.sync.dma_start(offsets[:], offs)
        nc.sync.dma_start(out=gate_cols[:], in_=gate[0, :].rearrange("(p g) -> p g", g=GROUPS))
        for a in range(LAST):
            for t in range(PACK):
                if (a, t) != (0, 0):
                    nc.sync.dma_start(out=x_rows[a][t][:], in_=x_view[a, t])
        for t in range(PACK - 1):
            nc.sync.dma_start(out=x_rows[LAST][t][:], in_=x_view[LAST, t])
        nc.sync.dma_start(out=x_last[:, 0:T], in_=x_view[LAST, PACK - 1])
        nc.sync.dma_start(out=bias_rows[0:N_TILES], in_=b.rearrange("(n p) e -> n p e", p=P))
        for e in range(E):
            load_scales(e, min(PLANES, E * PASSES - PLANES * e))
            for a in range(PASSES):
                nc.sync.dma_start(out=weights[e][a][:].bitcast(I32), in_=w_view[e, :, a, :].bitcast(I32))

        def entries(lo, hi):
            return offsets[:, lo // PER_COL : hi // PER_COL]

        def gather_scalar(rows, window, lo, hi):
            nc.scalar.activation(rows, window.indirect(entries(lo, hi)), COPY)

        def gather_vector(rows, window, lo, hi):
            nc.vector.tensor_copy(rows, window.indirect(entries(lo, hi)))

        def gate_and_weave(engine, woven, rows, weights):
            slots, planes = woven.shape[1], woven.shape[2]
            engine.tensor_tensor(
                woven.rearrange("k (c i) t -> k c t i", i=LINE),
                rows.rearrange("k t (c i) -> k c t i", i=LINE),
                weights.rearrange("k (c i) -> k c i", i=LINE).unsqueeze(2).to_broadcast([P, slots // LINE, planes, LINE]),
                MULT,
            )

        def gate_and_weave_gpsimd(woven, rows, weights):
            slots, planes = woven.shape[1], woven.shape[2]
            nc.gpsimd.tensor_tensor(woven, rows.rearrange("k t j -> k j t"), weights.unsqueeze(2).to_broadcast([P, slots, planes]), MULT)

        quantised = {}

        def quantise(a, experts, woven, tag=None):
            name = "%d%d" % (a, experts[0])
            codes = sb.tile([P, len(experts) * C], U32, name="codes" + name, tag=tag or "codes" + name, align_bytes=64)
            plane = sb.tile([P, len(experts) * C], U8, name="plane" + name, align_bytes=64)
            nc.vector.quantize_mx(out=codes[:].bitcast(FP8X4), scales=plane[:], in_=woven.rearrange("k j t -> k (j t)"))
            for i, e in enumerate(experts):
                quantised[(a, e)] = (codes[:, i * C : (i + 1) * C], plane[:, i * C : (i + 1) * C])

        acc = {}

        def multiply(e):
            for n in range(N_TILES):
                acc[(e, n)] = psum.tile([P, C], F32, name="acc%d_%d" % (e, n))
            for a in range(PASSES):
                for n in range(N_TILES):
                    one_pass(e, n, a, a == 0, a == LAST)

        def one_pass(e, n, a, start, stop):
            codes, plane = quantised[(a, e)]
            g, i = divmod(e * PASSES + a, PLANES)
            nc.tensor.matmul_mx(
                out=acc[(e, n)][:],
                lhsT=weights[e][a][:, n * P : (n + 1) * P].bitcast(FP8X4),
                lhsT_scale=w_planes[4 * i :, g, n * P : (n + 1) * P],
                rhs=codes.bitcast(FP8X4),
                rhs_scale=plane,
                start=start,
                stop=stop,
            )

        ys = [sb.tile([P, S], F32, name="y%d" % n) for n in range(N_TILES)]

        def bias_of(e, n):
            return bias_first[:] if (e, n) == (0, 0) else bias[:, N_TILES * e + n - 1 : N_TILES * e + n]

        def relu_scalar(e, n):
            nc.scalar.activation(ys[n][:, e * C : (e + 1) * C], acc[(e, n)][:], RELU, bias=bias_of(e, n))

        def relu_vector(e, n):
            nc.vector.tensor_scalar(ys[n][:, e * C : (e + 1) * C], acc[(e, n)][:], bias_of(e, n), 0.0, ADD, MAX)

        def scatter_scalar(n, lo, hi):
            nc.scalar.activation(result[n][:].indirect(entries(lo, hi)), ys[n][:, lo:hi], COPY)

        def scatter_vector(n, lo, hi):
            nc.vector.tensor_copy(result[n][:].indirect(entries(lo, hi)), ys[n][:, lo:hi])

        def store(n):
            nc.sync.dma_start(out=out[n * P : (n + 1) * P, :], in_=result[n][:])

        spread = psum.tile([P, P, GROUPS], F32, name="spread")
        for g in range(GROUPS):
            nc.tensor.transpose(spread[:, :, g], gate_cols[:, g : g + 1].to_broadcast([P, P]), identity[:])
        gates = spread[:].rearrange("k c i -> k (c i)")


        gate_copy = sb.tile([P, HEADS[0]], F32, name="gate_copy")
        nc.vector.tensor_copy(gate_copy[:], gates[:, 0 : HEADS[0]])

        woven = [sb.tile([P, S, PACK], BF16, name="woven%d" % a, align_bytes=64) for a in range(LAST)]
        for a in range(LAST):
            rows = sb.tile([P, PACK, S], F32, name="rows%d" % a, align_bytes=64)
            head = HEADS[a]
            for t in range(PACK):
                cut = CUTS[a][t]
                gather_scalar(rows[:, t, 0:cut], x_rows[a][t][:], 0, cut)
                gather_vector(rows[:, t, cut:S], x_rows[a][t][:], cut, S)
            gate_and_weave_gpsimd(woven[a][:, 0:head], rows[:, :, 0:head], gate_copy[:, 0:head])
            gate_and_weave(nc.vector, woven[a][:, head:S], rows[:, :, head:S], gates[:, head:S])

        bias_turned = psum.tile([P, E * N_TILES + P], F32, name="bias_turned")
        for e in range(E):
            nc.tensor.transpose(bias_turned[:, N_TILES * e : N_TILES * e + P], bias_rows[:, :, e], identity[:])
        bias_first = sb.tile([P, 1], F32, name="bias_first", align_bytes=64)
        bias = sb.tile([P, E * N_TILES - 1], F32, name="bias")
        nc.scalar.copy(bias_first[:], bias_turned[:, 0:1])
        nc.scalar.copy(bias[:], bias_turned[:, 1 : E * N_TILES])

        rows2 = sb.tile([P, PACK, WIDE], F32, name="rows2", align_bytes=64)
        late_rows = x_last[:, T - (PACK - 1) * (S - WIDE) :].rearrange("k (t j) -> k t j", t=PACK)
        woven2 = sb.tile([P, WIDE, PACK], BF16, name="woven2", tag="woven0", align_bytes=64)
        woven20 = woven2[:, WIDE - C :]
        woven21 = woven2[:, 0:C]
        for t in range(PAIR):
            gather_scalar(rows2[:, t, 0 : LAST_CUTS[t]], x_rows[LAST][t][:], 0, LAST_CUTS[t])
            gather_vector(rows2[:, t, LAST_CUTS[t] : WIDE], x_rows[LAST][t][:], LAST_CUTS[t], WIDE)
        quantise(0, [0, 1], woven[0][:], "rows1")
        quantise(1, [0], woven[1][:, 0:C])
        gather_scalar(rows2[:, 2, 0 : LAST_CUTS[2]], x_rows[LAST][2][:], 0, LAST_CUTS[2])
        gather_scalar(rows2[:, 3, 0:C], x_last[:, 0:T], 0, C)
        gather_scalar(rows2[:, 3, C:WIDE], x_last[:, 0:T], C, WIDE)
        gate_and_weave_gpsimd(woven20[:, 0:SIDE], rows2[:, :, 0:SIDE], gate_copy[:, 0:SIDE])
        gate_and_weave(nc.vector, woven20[:, SIDE:], rows2[:, :, SIDE:C], gates[:, SIDE:C])
        gate_and_weave(nc.vector, woven21[:, 0 : WIDE - C], rows2[:, :, C:WIDE], gates[:, C:WIDE])
        quantise(LAST, [0], woven20)
        multiply(0)
        quantise(1, [1], woven[1][:, C:S], "rows2")
        gather_scalar(late_rows[:, PACK - 1, :], x_last[:, 0:T], WIDE, S)
        for t in range(PACK - 1):
            gather_scalar(late_rows[:, t, :], x_rows[LAST][t][:], WIDE, S)
        gate_and_weave(nc.vector, woven21[:, WIDE - C :], late_rows, gates[:, WIDE:S])

        relu_scalar(0, 0)
        relu_scalar(0, 1)
        relu_vector(0, 2)
        quantise(LAST, [1], woven21, "bias_first")
        multiply(1)
        scatter_scalar(0, 0, C)
        scatter_scalar(1, 0, C)
        scatter_vector(2, 0, FIRST)
        for n in range(N_TILES):
            relu_vector(1, n)
        scatter_vector(0, C, S)
        store(0)
        scatter_scalar(2, FIRST, S)
        store(2)
        scatter_vector(1, C, S)
        store(1)
